import numpy as np, ml_dtypes
CORES = [40,41,42,43,44,45,46,47]
N = 8
import mx_ref
BF = ml_dtypes.bfloat16
def gcols(t, e):
    v = np.concatenate([t.reshape(8, 16, -1, 4), np.zeros((8, 16, 1, 4), BF)], axis=2)
    return np.ascontiguousarray(np.stack([v[g][:, e[g]] for g in range(8)])).reshape(128, -1)
def tile(rs):
    return np.stack(rs, axis=2).reshape(128, -1).astype(BF)
def cut(t, i, w=512):
    return t[:, w * i:w * i + w]
def pick(q, e):
    c = np.concatenate([q[0].reshape(128, -1, 4), np.zeros((128, 1, 4), np.uint8)], axis=1); s = np.concatenate([q[1], np.ones((16, 1), np.uint8)], axis=1)
    return (np.ascontiguousarray(c[:, e].reshape(128, -1)), np.ascontiguousarray(s[:, e]))
def join(*qs):
    return (np.concatenate([q[0] for q in qs], axis=1), np.concatenate([q[1] for q in qs], axis=1))
def put(q, e, v):
    c, s = q[0].reshape(128, -1, 4).copy(), q[1].copy(); c[:, e] = v[0].reshape(128, -1, 4); s[:, e] = v[1]
    return (c.reshape(128, -1), s)
def pk(c, s):
    return (np.ascontiguousarray(c), mx_ref.live(s))
def emit(q):
    return q[0], q[1]
def packed(v, rng):
    q = [mx_ref.quantize(np.ascontiguousarray(v[r])) for r in range(N)]
    return np.stack([a for a, b in q]), np.stack([mx_ref.plane(b, rng) for a, b in q])
def values_of_codes():
    e, c = np.zeros((128, 128, 4), np.float32), np.zeros((128, 2, 4), np.uint8)
    e[np.arange(128), np.arange(128), 0] = 1
    c[:127, :, 0] = np.arange(256).reshape(2, 128).T[:127]
    return mx_ref.matmul(mx_ref.quantize(e.reshape(128, 512).astype(BF)), (c.reshape(128, 8), np.full((16, 2), 127, np.uint8))).T.reshape(-1).astype(np.float64)
CODE_VALUE, SCALE_VALUE = values_of_codes(), 2.0 ** (np.arange(256) - 127.0)
def decode(q):
    return (CODE_VALUE[q[0]].reshape(16, 8, -1, 4) * SCALE_VALUE[q[1]][:, None, :, None] + 0.0).reshape(128, -1).astype(np.float32)
def f(rng, *shape):
    return mx_ref.flush((rng.standard_normal(shape, dtype=np.float32) * np.exp2(rng.integers(-2, 3, shape[:-1] + (1,)))).astype(BF))
def wide(rng, *shape, cols=0):
    v = rng.standard_normal(shape, dtype=np.float32) * np.exp2(rng.integers(-12, 13, shape)).astype(np.float32)
    if cols: v *= np.repeat(np.exp2(rng.integers(-cols, cols + 1, shape[:-2] + (1, shape[-1] // 4))) * (rng.random(shape[:-2] + (1, shape[-1] // 4)) > 0.0625), 4, axis=-1).astype(np.float32)
    return mx_ref.flush(v.astype(BF))
C, S, R = 448, 128, 2
STEP = [1, 2]
def partner(r, t):
    return r ^ STEP[t]
def order(p):
    return np.argsort(-(p[::16] + np.float32(0.0)), axis=1, kind="stable")
def walk(pi):
    g, p = np.arange(8), np.zeros(8, int)
    e, taken = np.zeros((8, C), int), np.zeros((8, C), bool)
    for k in range(C):
        e[:, k] = p
        taken[g, p] = True
        p = pi[g, p]
        p = np.where(taken[g, p], np.argmin(taken, axis=1), p)
    return e
def common(w, rng):
    c, p = packed(np.stack([w] * N), rng)
    return {"wc": c, "ws": p}
def weights(rng, keep=()):
    w = np.array(f(rng, 128, 2048)).reshape(128, 4, 8, 16, 4)
    for p in keep: w[:, :, :, p] = 0
    if len(keep): w[::16] = 0
    return common(w.reshape(128, 2048), rng)
def numbers_of(rng):
    return {"x": np.array(f(rng, N, 128, 4 * C)), "u": np.stack([f(rng, 128, 512)] * N), "v": np.array(f(rng, N, 128, 512))}
def planted(rng, s, sign, kind):
    d = numbers_of(rng)
    x = d["x"].astype(np.float32).reshape(N, 8, 16, C, 4)
    digit = ((s[:, :, :, None] >> np.arange(12)) & 1) * np.exp2(np.arange(12) - 23.0)
    x[:, :, 0] = 0
    x[:, :, 0, :, 0] = sign[:, :, None]
    for a in range(3): x[:, :, 8 + a] = digit[:, :, :, 4 * a:4 * a + 4]
    x[:, :, 11:] = rng.integers(4, 8, (N, 8, 5, C, 4)) * rng.choice([-1.0, 1.0], (N, 8, 5, C, 4)) * 2.0 ** -20
    u = d["u"].reshape(N, 128, 128, 4)
    u[:, :, ::16] = 0
    for g in range(8):
        k = 1.0 if kind[g] < 2 else 2.0 ** -30
        u[:, 16 * g, 16 * g, 0] = k
        u[:, 16 * g + 8:16 * g + 11, 16 * g] = k
        if kind[g] == 1: x[:, g, 0, int(rng.integers(C)), 0] *= 2.0 ** 30
        if kind[g] == 3:
            x[:, g, 0] = 0
            x[:, g, 8:] *= 2.0 ** -7
            x[:, g, 8:11] *= sign[:, g][:, None, None, None]
            x[:, g, 11] = 0
            u[:, 16 * g + 11, 16 * g, 0] = 1.125 * k
            u[:, 16 * g + 11, 16 * g, 1] = k
            for r in range(N):
                if r & STEP[0]:
                    j = int(np.flatnonzero(s[r, g] == 0)[-1])
                    x[r, g, 11, j, 0] = 1.125 * 2.0 ** -30
                    x[r, g, 11, j, 1] = -1.25 * 2.0 ** -30
    return {"x": x.reshape(N, 128, 4 * C).astype(BF), "u": u.reshape(N, 128, 512), "v": d["v"], **weights(rng, [0] + [*range(8, 16)])}
def setup_inputs(rng):
    return {**numbers_of(rng), **weights(rng)}
def setup_inputs_ties(rng):
    d = numbers_of(rng)
    e = rng.permutation(N)
    x = d["x"].reshape(N, 8, 16, C, 4)
    for r in range(N):
        for g in range(8):
            k = np.zeros(C, int) if r == e[0] else rng.permutation(C) % 3
            a = x[r, g, :8, :3].copy()
            a[:, 2] = 0
            x[r, g, :8] = a[:, k]
    x[e[1]] = 0
    u = d["u"].reshape(N, 8, 16, 128, 4)
    for g in range(8):
        own = u[:, g, :8, 16 * g].copy()
        u[:, :, :, 16 * g] = 0
        u[:, g, :8, 16 * g] = own
    return {"x": x.reshape(N, 128, 4 * C), "u": u.reshape(N, 128, 512), "v": d["v"], **weights(rng, [*range(8)])}
def setup_inputs_near(rng):
    s = np.stack([np.stack([rng.permutation(C) // 2 for g in range(8)]) for r in range(N)])
    sign = np.stack([rng.permutation(8) % 2 * 2.0 - 1.0 for r in range(N)])
    return planted(rng, s, sign, rng.permutation(8) % 4)
def setup_inputs_cycles(rng):
    size = [[C], [257] + [1] * (C - 257), [2] * (C // 2), [3] * (C // 3) + [1] * (C % 3)]
    s = np.zeros((N, 8, C), int)
    h = rng.permutation(8)
    for q in range(N):
        if q & (STEP[0] | STEP[1]): continue
        for g in range(8):
            i, m, pi, at = rng.permutation(C), rng.permutation(C), np.zeros(C, int), 0
            if h[g] // 2 == 0:
                m = np.roll(m, -int(np.argmin(m)))
                m[1:3] = np.sort(m[1:3])
                m[-2:] = np.sort(m[-2:])[::-1]
            for n in size[h[g] // 2]:
                pi[m[at:at + n]] = np.roll(m[at:at + n], -1)
                at += n
            other = i.copy()
            if h[g] == 4:
                k = pi[np.flatnonzero(pi > np.arange(C))[-2:]]
                other[k] = i[k[::-1]]
            for r in (q, q ^ STEP[0], q ^ STEP[1], q ^ STEP[0] ^ STEP[1]):
                c = other if r & STEP[1] else i
                s[r, g] = C - 1 - (c[pi] if r & STEP[h[g] % 2] else c)
    sign = np.tile(rng.permutation(8) % 2 * 2.0 - 1.0, (N, 1))
    return planted(rng, s, sign, rng.permutation(8) % 2 * 2)
def setup_inputs_huge(rng):
    d = numbers_of(rng)
    x = 2.0 ** 30 * (0.9 + 0.1 * rng.random((N, 128, C, 4)))
    x[:, ::8, :, 0] = 2.0 ** 30
    c = np.stack([rng.permutation(C) % 2 * 2.0 - 1.0 for r in range(N)])
    c[rng.permutation(N) < N // 2] = 1
    x *= c[:, None, :, None]
    u = d["u"].reshape(N, 128, 128, 4)
    a = 2.0 ** 30 * (1 - 0.1 * rng.random((128, 8, 4))) * (rng.permutation(8) % 2 * 2.0 - 1.0)[None, :, None]
    u[:, :, ::16] = a.astype(np.float32).astype(BF)
    w = np.zeros((128, 4, 128, 4), np.float32)
    i = np.arange(128)
    for b in range(4): w[i, b, i, b] = -8
    return {"x": x.astype(np.float32).reshape(N, 128, 4 * C).astype(BF), "u": u.reshape(N, 128, 512), "v": d["v"], **common(w.reshape(128, 2048).astype(BF), rng)}
def setup_inputs_spread(rng):
    d = setup_inputs(rng)
    d["x"] = wide(rng, N, 128, 4 * C, cols=6)
    return d
def check_inputs(d):
    b = []
    for k in ("x", "u", "v"):
        a = np.abs(d[k].astype(np.float32))
        if not (np.isfinite(a).all() and ((a == 0) | (a >= 2.0 ** -30) & (a <= 2.0 ** 30)).all()): b.append("a value of " + k)
    if (d["u"].astype(np.float32) != d["u"][:1].astype(np.float32)).any(): b.append("u differs between ranks")
    if (d["wc"] % 128 == 127).any(): b.append("a code of wc is no number")
    if (d["wc"] != d["wc"][:1]).any(): b.append("wc differs between ranks")
    s = [mx_ref.live(p) for p in d["ws"]]
    if any((p != s[0]).any() for p in s): b.append("ws differs between ranks")
    return b
def reference(x, u, v, wc, ws):
    w, qu = pk(wc[0], ws[0]), mx_ref.quantize(u[0])
    now = [x[r] for r in range(N)]
    for t in range(R):
        o = [order(mx_ref.matmul(qu, mx_ref.quantize(now[r]))) for r in range(N)]
        i = [np.argsort(o[r], axis=1) for r in range(N)]
        e = [walk(np.take_along_axis(o[r], i[partner(r, t)], axis=1)) for r in range(N)]
        laid = [gcols(now[r], e[r]) for r in range(N)]
        came = decode(join(*[mx_ref.quantize(np.ascontiguousarray(laid[r][:, :4 * S])) for r in range(N)])).astype(BF)
        for r in range(N):
            z = np.ascontiguousarray(np.concatenate([cut(came, partner(r, t), 4 * S), laid[r][:, 4 * S:]], axis=1))
            q = mx_ref.quantize(z)
            now[r] = tile([z[:, b::4].astype(np.float32) + mx_ref.matmul(pick(w, np.arange(128 * b, 128 * b + 128)), q) * np.float32(0.015625) for b in range(4)])
    y, el = np.zeros((N, 128, C), np.float32), np.zeros((N, 8, C), np.float32)
    oc, osc = np.zeros((N, 128, 4 * C), np.uint8), np.zeros((N, 16, C), np.uint8)
    for r in range(N):
        q = mx_ref.quantize(now[r])
        y[r] = mx_ref.matmul(mx_ref.quantize(v[r]), q)
        el[r] = e[r]
        oc[r], osc[r] = emit(q)
    return {"y": y, "el": el, "oc": oc, "osc": osc}

@@ -1,0 +1,514 @@
+from concourse.mybir import dt, AluOpType as A, ActivationFunctionType as F
+
+C, S, R = 448, 128, 2
+STEP = [1, 2]
+KB = C // 16
+NQ = KB // 4
+WIDE = [max(128, 64 * (i + 1)) for i in range(NQ)]
+AT = [sum(WIDE[:i]) for i in range(NQ + 1)]
+BY_S = [27, 26, 25, 24, 7, 22, 21, 11, 10, 9, 8]
+FIRST = 24
+HIGH = 12
+PLAN = [*range(20, 12, -1), 6, 12, "q6", "q3", 23, 5, "q4", "early", 4, 3, 2, "q5", 1, 0, "q1", "tallyh", "c", "q2", "high", "q0",
+        "tallyl", "c"]
+BY_V = sorted(k for k in PLAN if k in range(KB))
+ENGINES = 8
+H2, H1 = (0, S), (S, C)
+HALVES = {1: (S, S + 160), 3: (S + 160, C)}
+HALF = C // 2
+LIFT = 480
+DEEP = 1024
+CUT = (320, 384)
+LOW = 96
+ENDS = 224
+MAGIC = 12582912
+
+SCRATCH = {}
+
+
+def _buf(dtype, n, *names):
+    for name in names:
+        SCRATCH[name] = ("psum" if name[:2] in ("pp", "pr") and name[2:].isdigit() else "sbuf", [128, n], dtype)
+
+
+_buf("bfloat16", 512, "ub", "vb", "neg", "c64", "go", "gs", "bt0", "bt1")
+_buf("bfloat16", 4 * 512, "eb")
+_buf("bfloat16", C, "mask", "gate", "ctl", "ctlp", "fh", "orow", "crow", "prow", "erow", "j0", "j1",
+     "eqr", "eqs", "rel0", "rel1", "rel2", "rel3")
+_buf("float16", C, "hrow")
+_buf("bfloat16", 224 * KB, "zs")
+_buf("bfloat16", 4 * C, "z64", "x0", "x1", "x2", "zt0", "zt1")
+_buf("float8_e4m3fn_x4", 128, "qu", "qur", "qv", "qg", "qb0", "qb1", "qc0", "qc1")
+_buf("uint8", 128, "su", "sur", "sv", "sg", "sb0", "sb1", "sc0", "sc1")
+_buf("float8_e4m3fn_x4", 512, "qw", "qe")
+_buf("uint8", 512, "sw", "se")
+_buf("float8_e4m3fn_x4", C, "qx0", "qx1", "qx2", "qz0", "qz1")
+_buf("uint8", C, "sx0", "sx1", "sx2", "sz0", "sz1")
+_buf("bfloat16", 4 * AT[NQ], "fl")
+_buf("float8_e4m3fn_x4", AT[NQ], "qf")
+_buf("uint8", AT[NQ], "sf")
+_buf("int32", C, "ci", "d15")
+_buf("int32", 8, "ku")
+_buf("uint16", 8, "offu")
+_buf("uint16", KB, "offm", "offp", "off0", "off1", "own0", "own1", "land0", "land1", "offe0", "offe1", "offe2", "offe3")
+_buf("float32", C, "thr", "mrow", "arow", "srow", "ctlb", "hkey", "hcol", "wrow", "elf", "ysb",
+     "a0", "a1", "b0", "b1", "r0", "r1", "r2", "r3")
+_buf("float32", KB, "k0", "k1", "cnt", "tie", "la", "lb", "lc", "mw", "kw", "pw")
+_buf("float32", 32, "aw")
+_buf("float32", 512, "pp0", "pp1", "pp2", "pp3", "pr0", "pr1", "pr2", "pr3")
+
+LOADS = ["ldu", "ldx1", "ldx2", "ldw", "ldv"]
+SEMAPHORES = ["cv", "cs", "ct", "cg", "stored", "sent", "rxh0", "rxh1", "rxl0", "rxl1", "rxb0", "rxb1"] + LOADS
+
+
+def rank_program(g, core, T, topo):
+    rank = T.rank_of(core)
+    if rank is None:
+        return
+    queue = {"v": g.vector, "s": g.scalar, "t": g.tensor, "g": g, "y": g.sync}
+    count = {}
+    know = {q: {} for q in queue}
+    writer, reader = {}, {}
+
+    def wait(q, tok):
+        _, sem, val, seen = tok
+        if know[q].get(sem, 0) >= val:
+            return
+        queue[q].wait_ge(T.sem[sem], val)
+        for s, n in list(seen.items()) + [(sem, val)]:
+            know[q][s] = max(know[q].get(s, 0), n)
+
+    def before(q, reads, writes):
+        for k in reads:
+            for tok in writer.get(k, []):
+                wait(q, tok)
+            if k[:2] in ("pp", "pr"):
+                for tok in reader.get(k, []):
+                    if tok[0] != q:
+                        wait(q, tok)
+        for k in writes:
+            for tok in writer.get(k, []) + reader.get(k, []):
+                wait(q, tok)
+
+    def after(q, sem, inc, reads, writes):
+        count[sem] = count.get(sem, 0) + inc
+        tok = (q, sem, count[sem], dict(know[q]))
+        for k in reads:
+            reader.setdefault(k, []).append(tok)
+        for k in writes:
+            writer[k], reader[k] = [tok], []
+
+    def do(q, reads, writes, make):
+        before(q, reads, writes)
+        make(queue[q]).then_inc(T.sem["c" + q], 1)
+        after(q, "c" + q, 1, reads, writes)
+
+    def load(q, sem, total, key, out, in_):
+        queue[q].dma_start(out, in_).then_inc(T.sem[sem], 16)
+        count[sem] = count.get(sem, 0) + 16
+        writer.setdefault(key, []).append((q, sem, total, {}))
+
+    def store(q, reads, out, in_):
+        before(q, reads, [])
+        queue[q].dma_start(out, in_).then_inc(T.sem["stored"], 16)
+        after(q, "stored", 16, reads, [])
+
+    def send(t, pairs, sem):
+        dst = T.cores[rank ^ STEP[t]]
+        rid, pid, _ = topo.addr(dst)
+        eng = topo.engines(core, dst)[:ENGINES]
+        mask = sum(1 << e for e in eng)
+        total = count.get(sem, 0) + len(pairs) * len(eng)
+        for land, there, here, view, key in pairs:
+            before("g", [key], [])
+            g.remote_dma(view(there), view(here), T.sem[sem], T.sem["sent"], pid, rid, mask)
+            count["sent"] = count.get("sent", 0) + len(eng)
+            writer[land] = [("far", sem, total, {})]
+        count[sem] = total
+
+    def ts(out, in0, s1, op0, s2=None, op1=None):
+        if op1 is None:
+            return lambda e: e.tensor_scalar(out, in0, s1, None, op0)
+        return lambda e: e.tensor_scalar(out, in0, s1, s2, op0, op1)
+
+    def tt(out, in0, in1, op):
+        return lambda e: e.tensor_tensor(out, in0, in1, op)
+
+    def act(out, in_, func=F.Copy, **kw):
+        return lambda e: e.activation(out, in_, func, **kw)
+
+    def cp(out, in_):
+        return lambda e: e.tensor_copy(out, in_)
+
+    def fill(out, x):
+        return lambda e: e.memset(out, x)
+
+    def quant(q, s, x):
+        return lambda e: e.quantize_mx(q, s, x)
+
+    def scan(out, d0, d1, init, op0, op1):
+        return lambda e: e.tensor_tensor_scan(out, d0, d1, init, op0, op1)
+
+    def back(a, b):
+        return slice(b - 1, a - 1 if a else None, -1)
+
+    def iota(name, pattern, base, cm, cols=slice(None), key=None):
+        kw = {} if SCRATCH[name][2] == "int32" else {"allow_small_or_imprecise_dtypes": True}
+        do("g", [], [key or name], lambda e: e.iota(T[name][:, cols], pattern, base, cm, **kw))
+
+    load("s", "ldu", 16, "ub", T.ub[:], T.u[:])
+    load("y", "ldx1", 16, "x0:1", T.x0[:, 4 * S:4 * C], T.x[:, 4 * S:4 * C])
+    load("y", "ldx2", 16, "x0:2", T.x0[:, 0:4 * S], T.x[:, 0:4 * S])
+    before("y", ["x0:1", "x0:2"], [])
+    load("y", "ldw", 32, "w", T.qw[:].bitcast(dt.uint8), T.wc[:])
+    load("y", "ldw", 32, "w", T.sw[:], T.ws[:])
+    load("y", "ldv", 16, "vb", T.vb[:], T.v[:])
+
+    iota("ci", [[-1, C]], C - 1, 1)
+    iota("ku", [[16, 8]], 0, 0)
+    do("v", [], ["neg"], fill(T.neg[:], -1.0))
+    do("g", ["neg"], ["go"], lambda e: e.affine_select(T.go[:], T.neg[:], [[-16, 8], [0, 64]], A.is_ge, 0.0, 0, 1))
+    do("g", ["go"], ["gs"], lambda e: e.affine_select(T.gs[:], T.go[:], [[16, 8], [0, 64]], A.is_ge, 0.0, 15, -1))
+    left, k0_keys = [], []
+    for k in range(KB):
+        n = C - 16 * k - 16 * sum(i >= k for i in BY_S) - 1 - DEEP
+        left.append(n + (16 * k if k in BY_S else HALF if k else 0))
+    k = 0
+    while k < KB:
+        step, n = (left[k + 1] - left[k] if 0 < k < KB - 1 else 0), 1
+        while 0 < k and k + n < KB and left[k + n] - left[k + n - 1] == step:
+            n += 1
+        k0_keys.append("k0:%d" % k)
+        iota("k0", [[step, n]], left[k], 0, slice(k, k + n), k0_keys[-1])
+        k += n
+    do("v", [], ["c64"], fill(T.c64[:], 64.0))
+    do("v", [], ["cnt0"], fill(T.cnt[:, 0:1], 0.0))
+    do("v", ["ci"], ["d15"], ts(T.d15[:], T.ci[:], 15, A.bitwise_and))
+    do("v", ["d15"], ["ctl"], ts(T.ctl[:], T.d15[:], 64.0, A.mult, -float(LIFT), A.add))
+    own_q = T.d15[:, 15:C:16]
+    do("v", ["d15"], ["la"], ts(T.la[:], own_q, -1.0, A.mult, 15.0, A.add))
+    do("v", ["d15"], ["lb"], ts(T.lb[:], own_q, -32.0, A.mult, -32.0, A.add))
+    do("v", ["ctl"], ["mask"], ts(T.mask[:], T.ctl[:], float(LIFT), A.is_equal))
+    do("v", ["la", "lb"], ["lc"], tt(T.lc[:], T.la[:], T.lb[:], A.mult))
+    do("v", ["ctl"], ["gate"], ts(T.gate[:], T.ctl[:], float(LIFT), A.not_equal))
+    do("v", ["lc"], ["ctl"], ts(T.ctl[:, 15:C:16], T.lc[:], -float(LIFT), A.add))
+    do("v", ["ku"], ["offu"], cp(T.offu[:], T.ku[:]))
+    do("v", ["ub"], ["qu"], quant(T.qu[:], T.su[:], T.ub[:]))
+    do("v", ["qu", "offu"], ["qur"], cp(T.qur[:, 0:128].bitcast(dt.uint32), T.qu[:, 0:128].bitcast(dt.uint32).indirect(T.offu[:, 0:8])))
+    do("v", ["qu", "offu"], ["sur"], cp(T.sur[:, 0:128], T.su[:, 0:128].indirect(T.offu[:, 0:8])))
+    for i in range(NQ):
+        for j in range(64 * i, WIDE[i], 64):
+            z = 4 * (AT[i] + j)
+            do("s", ["neg"], ["fl%d" % k for k in range(4 * i, 4 * i + 4)] if j == 64 * i else ["flz%d" % i],
+               act(T.fl[:, z:z + 256], T.neg[:, 0:256], scale=0.0))
+    do("s", ["ctl"], ["ctlb"], act(T.ctlb[:], T.ctl[:]))
+    iota("fh", [[1, C]], -HALF, 0)
+    for b in range(4):
+        do("g", ["c64"], ["eb%d" % b], lambda e: e.affine_select(
+            T.eb[:, 512 * b:512 * b + 512], T.c64[:], [[-1, 512]], A.is_equal, 0.0, b, 4))
+
+    def quant_const(b):
+        do("v", ["eb%d" % b], ["qe%d" % b], quant(T.qe[:, S * b:S * b + S], T.se[:, S * b:S * b + S], T.eb[:, 512 * b:512 * b + 512]))
+
+    later = [lambda b=b: quant_const(b) for b in range(4)] + [lambda: do("v", ["vb"], ["qv"], quant(T.qv[:], T.sv[:], T.vb[:]))]
+
+    def matmul(out, key, lhs, ls, lkey, rhs, rs, rkey, start=True, stop=True):
+        do("t", lkey + rkey, [key], lambda e: e.matmul_mx(out, lhs, ls, rhs, rs, start, stop))
+
+    def state_keys(t, h):
+        if t == 0:
+            return ["x0:%d" % h]
+        return ["x%d:%d:%d" % (t, c, i) for c in ((1, 3) if h == 1 else (2,)) for i in range(4)]
+
+    def quant_state(t, h, part):
+        a, b = part
+        do("v", state_keys(t, h), ["qx%d:%d" % (t, h)], quant(T["qx%d" % t][:, a:b], T["sx%d" % t][:, a:b], T["x%d" % t][:, 4 * a:4 * b]))
+
+    def score(t, h, part):
+        a, b = part
+        qx, sx = T["qx%d" % t], T["sx%d" % t]
+        for p in ("pp0", "pp1") if h == 1 else ("pp2", "pp3"):
+            matmul(T[p][:, 0:b - a], p, T.qur[:], T.sur[:], ["qur", "sur"], qx[:, a:b], sx[:, a:b], ["qx%d:%d" % (t, h)])
+
+    def take_scores(t, h, part):
+        a, b = part
+        p0, p1 = ("pp0", "pp1") if h == 1 else ("pp2", "pp3")
+        do("v", [p0, "mask"], ["mrow:%d" % h], tt(T.mrow[:, a:b], T[p0][:, 0:b - a], T.mask[:, a:b], A.mult))
+        do("s", [p1], ["srow:%d" % h], act(T.srow[:, a:b], T[p1][:, 0:b - a]))
+        do("v", ["mrow:%d" % h, "gate"], ["arow:%d" % h], scan(T.arow[:, back(a, b)], T.gate[:, back(a, b)], T.mrow[:, back(a, b)], 0.0, A.mult, A.add))
+
+    def add_base(a, b):
+        keys = ["cnt%d" % k if k in BY_S else "cntv%d" % (k >= HIGH) if k else "cnt0" for k in range(a, b)]
+        do("v", keys + ["tie", "ctlb"], ["ctlb:%d" % a], tt(T.ctlb[:, 16 * a + 15:16 * b:16], T.cnt[:, a:b], T.tie[:, a:b], A.add))
+
+    def settle(t, bank, a, b):
+        do("v", [bank, "ctlb:%d" % a], ["hcol:%d" % a], scan(T.hcol[:, 16 * a:16 * b], T[bank][:, 16 * a:16 * b], T.ctlb[:, 16 * a:16 * b], -float(DEEP), A.max, A.add))
+        key = "own%d:%d" % (t, a)
+        do("v", ["hcol:%d" % a], [key], ts(T["own%d" % t][:, a:b], T.hcol[:, 16 * a + 15:16 * b:16], float(DEEP), A.add))
+        h = "h" if a >= HIGH else "l"
+        send(t, [("land%d:%s" % (t, h), "land%d" % t, "own%d" % t, lambda n: T[n][:, a:b], key)], "rx%s%d" % (h, t))
+
+    def places(t):
+        row = ["srow:1", "srow:2"]
+        do("v", ["arow:1", "arow:2"], ["aw"], cp(T.aw[:, 0:KB], T.arow[:, 0:C:16]))
+        pend, done = [], []
+
+        def flags(k, a, b):
+            z = 4 * AT[k // 4]
+            return T.fl[:, z + 4 * a + k % 4:z + 4 * b:4]
+
+        def sign(k):
+            rel = "rel%d" % (k % 4)
+            do("s", [rel], ["fl%d" % k, "cnt%d" % k], act(flags(k, 0, 16 * k), T[rel][:, 0:16 * k], F.Sign, scale=-1.0, accum_out=T.cnt[:, k:k + 1]))
+            do("s", [rel], ["fld%d" % k], act(flags(k, 16 * k, 16 * k + 16), T[rel][:, 16 * k:16 * k + 16], F.Sign, scale=-1.0))
+
+        for k in BY_S:
+            rel = "rel%d" % (k % 4)
+            do("s", row + ["aw"], [rel], act(T[rel][:, 0:16 * k + 16], T.srow[:, 0:16 * k + 16], F.Relu, bias=T.aw[:, k:k + 1], scale=-1.0))
+            pend.append(k)
+            if len(pend) > 1:
+                sign(pend.pop(0))
+        sign(pend.pop(0))
+
+        def add_up(k):
+            z = 224 * k + 224
+            do("v", ["fl%d" % k], ["zs:%d" % k], scan(T.zs[:, z - 8 * k:z], flags(k, 0, 8 * k), flags(k, 8 * k, 16 * k), -float(HALF), A.add, A.add))
+
+        def tally(a, b, n):
+            ks = [k for k in BY_V if a <= k < b]
+            at, runs = 0, []
+            while at < len(ks):
+                end = at
+                while end + 1 < len(ks) and ks[end + 1] == ks[end] + 1:
+                    end += 1
+                runs.append((ks[at], ks[end] + 1))
+                at = end + 1
+            for i, (c, d) in enumerate(runs):
+                key = "cntv%d" % n
+                do("v", ["zs:%d" % k for k in range(c, d)], [key] if i == len(runs) - 1 else [key + "'"],
+                   cp(T.cnt[:, c:d], T.zs[:, 224 * c + 223:224 * d:224]))
+
+        def sum_up(i):
+            a, b = AT[i], AT[i + 1]
+            keys = [n % k for k in range(4 * i, 4 * i + 4) for n in ("fl%d", "fld%d")] + ["flz%d" % i]
+            do("v", keys, ["qf%d" % i], quant(T.qf[:, a:b], T.sf[:, a:b], T.fl[:, 4 * a:4 * b]))
+
+            def add(bank, n, start, stop):
+                matmul(T[bank][:, 0:n], bank, T.qg[:], T.sg[:], ["qg"], T.qf[:, a:a + n], T.sf[:, a:a + n], ["qf%d" % i], start, stop)
+            last = len([j for j in done if j >= HIGH // 4]) == NQ - HIGH // 4 - 1
+            if i >= HIGH // 4:
+                if t == 0 and i == NQ - 1:
+                    add("pp3", C, True, True)
+                add("pp1", b - a, not any(j >= HIGH // 4 for j in done), last)
+            add("pp2", min(16 * HIGH, b - a), not done, len(done) == NQ - 1)
+            done.append(i)
+
+        prev, n = None, 0
+        for step in PLAN:
+            if step == "c":
+                for _ in range(2 if t == 0 else 0):
+                    later.pop(0)()
+            elif step == "early":
+                if t == 0:
+                    add_base(FIRST, KB)
+                    settle(t, "pp3", FIRST, KB)
+            elif step == "tallyh":
+                tally(HIGH, KB, 1)
+                add_base(HIGH, FIRST if t == 0 else KB)
+            elif step == "high":
+                settle(t, "pp1", HIGH, FIRST if t == 0 else KB)
+            elif step == "tallyl":
+                tally(1, HIGH, 0)
+                add_base(0, HIGH)
+            elif step in ["q%d" % i for i in range(NQ)]:
+                sum_up(int(step[1]))
+            else:
+                k = step
+                do("v", row + ["aw"], ["fl%d" % k], ts(flags(k, 0, 16 * k + 16), T.srow[:, 0:16 * k + 16], T.aw[:, k:k + 1], A.is_ge))
+                if prev:
+                    add_up(prev)
+                prev = k
+                n += 1
+                if n == 1:
+                    for h, p, (a, b) in ((1, "pp0", H1), (2, "pp2", H2)):
+                        do("v", ["arow:%d" % h, p], ["eqr:%d" % h], tt(T.eqr[:, a:b], T.arow[:, a:b], T[p][:, 0:b - a], A.is_equal))
+                if n == 2:
+                    do("v", ["eqr:1", "eqr:2", "gate"], ["eqs"], scan(T.eqs[:, back(0, C)], T.gate[:, back(0, C)], T.eqr[:, back(0, C)], 0.0, A.mult, A.add))
+                    if t == 0:
+                        do("v", ["lc"] + k0_keys, ["k1"], tt(T.k1[:], T.lc[:], T.k0[:], A.add))
+                if n == 3:
+                    do("v", ["eqs", "k1"], ["tie"], tt(T.tie[:], T.eqs[:, 0:C:16], T.k1[:], A.add))
+        settle(t, "pp2", 0, HIGH)
+
+    def wrap(row, keys, part=(0, C), ctl="ctl", to=("hrow:l", "hrow:h")):
+        a, b = part
+        do("v", keys + [ctl], list(to), scan(T.hrow[:, a:b], row[:, a:b], T[ctl][:, a:b], -1024.0, A.max, A.add))
+        return T.hrow[:, a + 15:b:16]
+
+    def three(name):
+        return [name + ":s", name + ":v", name + ":h"]
+
+    def both(name):
+        return [name + ":l", name + ":h"]
+
+    def shift(q, an, keys, bn, d, a, b):
+        do(q, keys, [bn + ":%d" % a], act(T[bn][:, a:b], T[an][:, a:b], F.Identity, bias=-d) if q == "s"
+           else ts(T[bn][:, a:b], T[an][:, a:b], -d, A.add))
+        return bn + ":%d" % a
+
+    def cycles(t):
+        own, land = "own%d" % t, "land%d" % t
+        parts = [own + ":0", own + ":%d" % HIGH] + ([own + ":%d" % FIRST] if t == 0 else [])
+        do("v", parts + ["fh"], ["orow"], cp(T.orow[:, 0:C].indirect(T[own][:, 0:KB]), T.fh[:]))
+        if t == 0:
+            do("s", ["fh"], ["thr"], act(T.thr[:], T.fh[:], F.Identity, bias=-0.5))
+            do("s", ["ctl"], ["ctlp"], act(T.ctlp[:], T.ctl[:], scale=1.0 / 1024))
+        m, e, d = 16 * HIGH, LOW // 16, 1.0 / 1024
+        do("s", ["orow", land + ":h"], ["j0:h"], act(T.j0[:, m:C], T.orow[:, 0:C].indirect(T[land][:, HIGH:KB])))
+        bkeys = [shift("s", "j0", ["j0:h"], "b0", d, m, C)]
+        while later:
+            later.pop(0)()
+        h = wrap(T.j0, ["j0:h"], (m, C), to=["hrow:h"])
+        do("v", ["hrow:h"], ["off0:h"], ts(T.off0[:, HIGH:KB], h, float(LIFT + HALF), A.add))
+        do("s", ["orow", land + ":l"], ["j0:s"], act(T.j0[:, 0:LOW], T.orow[:, 0:C].indirect(T[land][:, 0:e])))
+        do("v", ["orow", land + ":l"], ["j0:v"], cp(T.j0[:, LOW:m], T.orow[:, 0:C].indirect(T[land][:, e:HIGH])))
+        h = wrap(T.j0, ["j0:s", "j0:v"], (0, m), to=["hrow:l"])
+        bkeys.append(shift("v", "j0", ["j0:v"], "b0", d, LOW, m))
+        do("v", ["hrow:l"], ["off0:l"], ts(T.off0[:, 0:HIGH], h, float(LIFT + HALF), A.add))
+        bkeys.append(shift("v", "j0", ["j0:s"], "b0", d, 0, LOW))
+        win, wkeys = T.j0, three("j0")
+        for k in range(9):
+            off, j, jn = "off%d" % (k % 2), "j%d" % (k % 2), "j%d" % ((k + 1) % 2)
+            an, bk, bn = "a%d" % (k % 2), "b%d" % (k % 2), "b%d" % ((k + 1) % 2)
+            if k < 8:
+                do("s", three(j) + both(off), three(jn), act(T[jn][:], T[j][:, 0:C].indirect(T[off][:, 0:KB])))
+            do("v", wkeys + both(off) + bkeys, [an], tt(T[an][:], win[:, 0:C].indirect(T[off][:, 0:KB]), T[bk][:], A.min))
+            for key in bkeys:
+                reader.setdefault(bk + "*", []).extend(reader.get(key, []))
+            win, wkeys = T[an], [an]
+            if k < 8:
+                d = (2.0 ** (k + 1)) / 1024
+                for q in "sv":
+                    before(q, [], [bn + "*"])
+                reader[bn + "*"] = []
+                bkeys = [shift("s", an, [an], bn, d, 0, CUT[0])]
+                h = wrap(T[jn], three(jn))
+                bkeys.append(shift("v", an, [an], bn, d, CUT[0], CUT[1]))
+                o = "off%d" % ((k + 1) % 2)
+                do("v", both("hrow"), both(o), ts(T[o][:], h, float(LIFT + HALF), A.add))
+                bkeys.append(shift("v", an, [an], bn, d, CUT[1], C))
+        wkey = wkeys[0]
+        do("v", [wkey, "thr"], ["wrow"], scan(T.wrow[:], win[:], T.thr[:], -1024.0, A.max, A.max))
+        do("v", [wkey, "ctl"], ["hkey"], scan(T.hkey[:], win[:], T.ctl[:], -1024.0, A.max, A.add))
+        do("v", ["wrow", "thr"], ["crow"], scan(T.crow[:], T.wrow[:], T.thr[:], -HALF / 1024, A.add, A.subtract))
+        own_key, up = T.hkey[:, 15:C:16], float(MAGIC + LIFT + HALF)
+        do("v", ["hkey"], ["offm"], ts(T.offm[:], own_key, up, A.add, float(MAGIC), A.subtract))
+        do("v", ["hkey"], ["mw"], ts(T.mw[:], own_key, up, A.add, float(MAGIC), A.subtract))
+        for q, a, b in (("s", 0, ENDS), ("v", ENDS, C)):
+            src = T.crow[:, 0:C].indirect(T.offm[:, a // 16:b // 16])
+            do(q, ["crow", "offm"], ["prow:" + q], act(T.prow[:, a:b], src) if q == "s" else cp(T.prow[:, a:b], src))
+        do("v", ["hkey", "mw"], ["kw"], tt(T.kw[:], own_key, T.mw[:], A.subtract))
+        h = wrap(T.prow, ["prow:s", "prow:v"], ctl="ctlp")
+        do("v", both("hrow") + ["kw"], ["pw"], tt(T.pw[:], h, T.kw[:], A.subtract))
+        do("v", ["pw"], ["offp"], ts(T.offp[:], T.pw[:], (LIFT + HALF) / 1024 - LIFT - HALF - 0.5, A.add, 1024.0, A.mult))
+        do("v", ["offp", "fh"], ["erow"], cp(T.erow[:, 0:C].indirect(T.offp[:, 0:KB]), T.fh[:]))
+        h = wrap(T.erow, ["erow"])
+        for i in (2, 0, 3, 1):
+            do("v", both("hrow"), ["offe%d" % i], ts(T["offe%d" % i][:], h, LIFT + HALF + 0.25 * i, A.add, 4.0, A.mult))
+
+    def lay_out(t, tile, key, part):
+        a, b = part
+        for i in (2, 0, 3, 1):
+            out = tile[:, 4 * a + i:4 * b:4]
+            src = T["x%d" % t][:, 0:4 * C].indirect(T["offe%d" % i][:, a // 16:b // 16])
+            do("v" if i < 2 else "s", state_keys(t, 1) + state_keys(t, 2) + ["offe%d" % i], [key + str(i)], cp(out, src) if i < 2 else act(out, src))
+
+    def layer(t, i, qz, sz, a, b, key, bank, start=True):
+        matmul(T[bank][:, 0:b - a], bank, T.qw[:, S * i:S * i + S], T.sw[:, S * i:S * i + S], ["w"], qz[:, a:b], sz[:, a:b], [key], start, True)
+
+    def stay(t):
+        zt, qz, sz, xn = T["zt%d" % t], T["qz%d" % t], T["sz%d" % t], T["x%d" % (t + 1)]
+        for h, (a, b) in HALVES.items():
+            zk = "z%d:%d:" % (t, h)
+            lay_out(t, zt, zk, (a, b))
+            do("v", [zk + str(i) for i in range(4)], ["qz%d:%d" % (t, h)], quant(qz[:, a:b], sz[:, a:b], zt[:, 4 * a:4 * b]))
+            for i in range(4):
+                layer(t, i, qz, sz, a, b, "qz%d:%d" % (t, h), ("pr%d" if h == 1 else "pp%d") % i)
+        a, b = H1
+        for i in range(4):
+            out, src = T.z64[:, 4 * a + i:4 * b:4], zt[:, 4 * a + i:4 * b:4]
+            reads = ["z%d:%d:%d" % (t, h, i) for h in HALVES]
+            do("v" if i % 2 else "s", reads, ["z64:%d" % i], ts(out, src, 64.0, A.mult) if i % 2 else act(out, src, scale=64.0))
+        for h, (a, b) in HALVES.items():
+            for i in range(4):
+                bank = ("pr%d" if h == 1 else "pp%d") % i
+                do("v", [bank, "z64:%d" % i], ["r%d:%d" % (i, h)],
+                   tt(T["r%d" % i][:, a:b], T[bank][:, 0:b - a], T.z64[:, 4 * a + i:4 * b:4], A.add))
+        for h, (a, b) in HALVES.items():
+            for i in range(4):
+                do("s", ["r%d:%d" % (i, h)], ["x%d:%d:%d" % (t + 1, h, i)], act(xn[:, 4 * a + i:4 * b:4], T["r%d" % i][:, a:b], scale=0.015625))
+
+    def unpack(t, i, start, stop):
+        qc, sc = "qc%d" % t, "sc%d" % t
+        matmul(T["pr%d" % i][:, 0:S], "pr%d" % i, T.qe[:, S * i:S * i + S], T.se[:, S * i:S * i + S], ["qe%d" % i], T[qc][:], T[sc][:], [qc, sc], start, stop)
+
+    def arrive(t):
+        zt, qz, sz = T["zt%d" % t], T["qz%d" % t], T["sz%d" % t]
+        for i in range(4):
+            unpack(t, i, True, True)
+            do("v", ["pr%d" % i], ["z%d:2:%d" % (t, i)], ts(zt[:, i:4 * S:4], T["pr%d" % i][:, 0:S], 0.015625, A.mult))
+        do("v", ["z%d:2:%d" % (t, i) for i in range(4)], ["qz%d:2" % t], quant(qz[:, 0:S], sz[:, 0:S], zt[:, 0:4 * S]))
+        for i in range(4):
+            unpack(t, i, True, False)
+        for i in range(4):
+            layer(t, i, qz, sz, 0, S, "qz%d:2" % t, "pr%d" % i, False)
+
+    def arrived(t):
+        for i in range(4):
+            out, src = T["x%d" % (t + 1)][:, i:4 * S:4], T["pr%d" % i][:, 0:S]
+            do("s" if i < 2 else "v", ["pr%d" % i], ["x%d:2:%d" % (t + 1, i)],
+               act(out, src, scale=0.015625) if i < 2 else ts(out, src, 0.015625, A.mult))
+
+    def finish(t, h, part):
+        a, b = part
+        q, s, key, p = T["qx%d" % t], T["sx%d" % t], "qx%d:%d" % (t, h), "pp0" if h == 1 else "pp2"
+        store("y", [key], T.oc[:, 4 * a:4 * b], q[:, a:b].bitcast(dt.uint8))
+        matmul(T[p][:, 0:b - a], p, T.qv[:], T.sv[:], ["qv"], q[:, a:b], s[:, a:b], [key])
+
+    def store_rest(t, h, part):
+        a, b = part
+        s, key, p = T["sx%d" % t], "qx%d:%d" % (t, h), "pp0" if h == 1 else "pp2"
+        do("s", [p], ["ysb:%d" % h], act(T.ysb[:, a:b], T[p][:, 0:b - a]))
+        store("s", ["ysb:%d" % h], T.y[:, a:b], T.ysb[:, a:b])
+        for k in range(4):
+            store("y", [key], T.osc[4 * k:4 * k + 4, a:b], s[32 * k:32 * k + 4, a:b])
+
+    quant_state(0, 1, H1)
+    score(0, 1, H1)
+    quant_state(0, 2, H2)
+    score(0, 2, H2)
+    do("v", ["gs"], ["qg"], quant(T.qg[:], T.sg[:], T.gs[:]))
+    take_scores(0, 1, H1)
+    take_scores(0, 2, H2)
+    for t in range(R):
+        places(t)
+        cycles(t)
+        bt, qb, sb, qc, sc = ["%s%d" % (n, t) for n in ("bt", "qb", "sb", "qc", "sc")]
+        lay_out(t, T[bt], bt + ":", H2)
+        do("v", [bt + ":%d" % i for i in range(4)], [qb, sb], quant(T[qb][:], T[sb][:], T[bt][:]))
+        send(t, [(qc, qc, qb, lambda n: T[n][:].bitcast(dt.uint8), qb), (sc, sc, sb, lambda n: T[n][:], sb)], "rxb%d" % t)
+        stay(t)
+        if t == R - 1:
+            do("s", ["erow"], ["elf"], act(T.elf[:], T.erow[:], F.Identity, bias=float(HALF)))
+            store("y", ["elf"], T.el[:], T.elf[0:128:16, :])
+        arrive(t)
+        quant_state(t + 1, 1, H1)
+        arrived(t)
+        last, then = (score, take_scores) if t < R - 1 else (finish, store_rest)
+        last(t + 1, 1, H1)
+        quant_state(t + 1, 2, H2)
+        last(t + 1, 2, H2)
+        then(t + 1, 1, H1)
+        then(t + 1, 2, H2)
+    for sem in sorted(count):
+        g.wait_ge(T.sem[sem], count[sem])

@@ -4,24 +4,29 @@ C, S, R = 448, 128, 2
 STEP = [1, 2]
 KB = C // 16
 NQ = KB // 4
-WIDE = [max(128, 64 * (i + 1)) for i in range(NQ)]
+WIDE = [max(128, C - 64 * i) for i in range(NQ)]
 AT = [sum(WIDE[:i]) for i in range(NQ + 1)]
-BY_S = [27, 26, 25, 24, 7, 22, 21, 11, 10, 9, 8]
-FIRST = 24
-HIGH = 12
-PLAN = [*range(20, 12, -1), 6, 12, "q6", "q3", 23, 5, "q4", "early", 4, 3, 2, "q5", 1, 0, "q1", "tallyh", "c", "q2", "high", "q0",
-        "tallyl", "c"]
-BY_V = sorted(k for k in PLAN if k in range(KB))
+FIRST = 26
+HIGH = 14
+NH = 4
+BY_S = [27, 26, 25, 24, 23, *range(13, 0, -1)]
+PLAN = [22, "flag", 21, "tie", 20, "tie2", 19, 18, 17, 16, "q0", "early", 15, "early2", 14, "early3", "q2", "sum", "q1",
+        "baseh", "q3", "c", "c", "high", "c", "offh", "c", "c", "puth", "q4", "q5", "q6", "basel", "low", "offl", "putl"]
 ENGINES = 8
 H2, H1 = (0, S), (S, C)
 HALVES = {1: (S, S + 160), 3: (S + 160, C)}
 HALF = C // 2
-LIFT = 480
+LIFT = 512
 DEEP = 1024
-CUT = (320, 384)
-LOW = 96
-ENDS = 224
+BIG = 2.0 ** 80
 MAGIC = 12582912
+LA, LB = (0, HALF), (HALF, C)
+START = [("G", "s", HALF, 352), ("G", "v", 352, C), ("G", "s", 0, 128), ("G", "v", 128, HALF),
+         ("W", "v") + LB, ("W", "v") + LA, ("O", "v") + LB, ("O", "v") + LA]
+K1, K2, K3 = (0, 128), (128, 320), (320, C)
+LEVEL = [("G", "s") + LA, ("S", "s") + K1 + (0,), ("S", "s") + K2 + (0,), ("G", "s") + LB, ("S", "s") + K3 + (0,),
+         ("W", "v") + LA, ("K", "v") + K1, ("O", "v") + LA, ("K", "v") + K2, ("W", "v") + LB, ("K", "v") + K3, ("O", "v") + LB]
+ENDS = 224
 
 SCRATCH = {}
 
@@ -33,11 +38,11 @@ def _buf(dtype, n, *names):
 
 _buf("bfloat16", 512, "ub", "vb", "neg", "c64", "go", "gs", "bt0", "bt1")
 _buf("bfloat16", 4 * 512, "eb")
-_buf("bfloat16", C, "mask", "gate", "ctl", "ctlp", "fh", "orow", "crow", "prow", "erow", "j0", "j1",
-     "eqr", "eqs", "rel0", "rel1", "rel2", "rel3")
-_buf("float16", C, "hrow")
+_buf("bfloat16", C, "rr", "side", "drop", "gate", "sg3", "sq", "ctl", "fh", "orow", "crow", "prow", "erow", "jp", "j0", "j1",
+     "eqs", "rel0", "rel1", "rel2", "rel3")
+_buf("float16", C, "hrow", "ctlp")
 _buf("bfloat16", 224 * KB, "zs")
-_buf("bfloat16", 4 * C, "z64", "x0", "x1", "x2", "zt0", "zt1")
+_buf("bfloat16", 4 * C, "z64", "x0", "x1", "x2", "zt0", "zt1", "xp")
 _buf("float8_e4m3fn_x4", 128, "qu", "qur", "qv", "qg", "qb0", "qb1", "qc0", "qc1")
 _buf("uint8", 128, "su", "sur", "sv", "sg", "sb0", "sb1", "sc0", "sc1")
 _buf("float8_e4m3fn_x4", 512, "qw", "qe")
@@ -47,14 +52,14 @@ _buf("uint8", C, "sx0", "sx1", "sx2", "sz0", "sz1")
 _buf("bfloat16", 4 * AT[NQ], "fl")
 _buf("float8_e4m3fn_x4", AT[NQ], "qf")
 _buf("uint8", AT[NQ], "sf")
-_buf("int32", C, "ci", "d15")
-_buf("int32", 8, "ku")
+_buf("int32", 8, "ku", "pc")
 _buf("uint16", 8, "offu")
-_buf("uint16", KB, "offm", "offp", "off0", "off1", "own0", "own1", "land0", "land1", "offe0", "offe1", "offe2", "offe3")
+_buf("uint16", KB, "offm", "offp", "offe", "own0", "own1", "land0", "land1")
+_buf("uint16", 9 * KB, "off")
 _buf("float32", C, "thr", "mrow", "arow", "srow", "ctlb", "hkey", "hcol", "wrow", "elf", "ysb",
      "a0", "a1", "b0", "b1", "r0", "r1", "r2", "r3")
-_buf("float32", KB, "k0", "k1", "cnt", "tie", "la", "lb", "lc", "mw", "kw", "pw")
-_buf("float32", 32, "aw")
+_buf("float32", KB, "k0", "k1", "cnt", "tie", "mw")
+_buf("float32", 8, "col")
 _buf("float32", 512, "pp0", "pp1", "pp2", "pp3", "pr0", "pr1", "pr2", "pr3")
 
 LOADS = ["ldu", "ldx1", "ldx2", "ldw", "ldv"]
@@ -70,25 +75,19 @@ def rank_program(g, core, T, topo):
     know = {q: {} for q in queue}
     writer, reader = {}, {}
 
-    def wait(q, tok):
-        _, sem, val, seen = tok
-        if know[q].get(sem, 0) >= val:
-            return
-        queue[q].wait_ge(T.sem[sem], val)
-        for s, n in list(seen.items()) + [(sem, val)]:
-            know[q][s] = max(know[q].get(s, 0), n)
-
     def before(q, reads, writes):
+        need = []
         for k in reads:
-            for tok in writer.get(k, []):
-                wait(q, tok)
+            need += writer.get(k, [])
             if k[:2] in ("pp", "pr"):
-                for tok in reader.get(k, []):
-                    if tok[0] != q:
-                        wait(q, tok)
+                need += [tok for tok in reader.get(k, []) if tok[0] != q]
         for k in writes:
-            for tok in writer.get(k, []) + reader.get(k, []):
-                wait(q, tok)
+            need += writer.get(k, []) + reader.get(k, [])
+        for _, sem, val, seen in sorted(need, key=lambda tok: -tok[2]):
+            if know[q].get(sem, 0) < val:
+                queue[q].wait_ge(T.sem[sem], val)
+                for s, n in list(seen.items()) + [(sem, val)]:
+                    know[q][s] = max(know[q].get(s, 0), n)
 
     def after(q, sem, inc, reads, writes):
         count[sem] = count.get(sem, 0) + inc
@@ -119,11 +118,12 @@ def rank_program(g, core, T, topo):
         eng = topo.engines(core, dst)[:ENGINES]
         mask = sum(1 << e for e in eng)
         total = count.get(sem, 0) + len(pairs) * len(eng)
-        for land, there, here, view, key in pairs:
-            before("g", [key], [])
+        for land, there, here, view, keys in pairs:
+            before("g", keys, [])
             g.remote_dma(view(there), view(here), T.sem[sem], T.sem["sent"], pid, rid, mask)
             count["sent"] = count.get("sent", 0) + len(eng)
-            writer[land] = [("far", sem, total, {})]
+            for k in land:
+                writer[k] = [("far", sem, total, {})]
         count[sem] = total
 
     def ts(out, in0, s1, op0, s2=None, op1=None):
@@ -140,6 +140,9 @@ def rank_program(g, core, T, topo):
     def cp(out, in_):
         return lambda e: e.tensor_copy(out, in_)
 
+    def move(q, out, in_):
+        return act(out, in_) if q == "s" else cp(out, in_)
+
     def fill(out, x):
         return lambda e: e.memset(out, x)
 
@@ -152,9 +155,16 @@ def rank_program(g, core, T, topo):
     def back(a, b):
         return slice(b - 1, a - 1 if a else None, -1)
 
+    def span(name, a=0, b=C):
+        return ["%s:%d" % (name, i) for i in range(a // 32, (b + 31) // 32)]
+
     def iota(name, pattern, base, cm, cols=slice(None), key=None):
         kw = {} if SCRATCH[name][2] == "int32" else {"allow_small_or_imprecise_dtypes": True}
         do("g", [], [key or name], lambda e: e.iota(T[name][:, cols], pattern, base, cm, **kw))
+
+    def flags(k, a, b):
+        z = 4 * AT[(KB - k) // 4] + (KB - k) % 4
+        return T.fl[:, z + 4 * a:z + 4 * b - 3:4]
 
     load("s", "ldu", 16, "ub", T.ub[:], T.u[:])
     load("y", "ldx1", 16, "x0:1", T.x0[:, 4 * S:4 * C], T.x[:, 4 * S:4 * C])
@@ -164,44 +174,45 @@ def rank_program(g, core, T, topo):
     load("y", "ldw", 32, "w", T.sw[:], T.ws[:])
     load("y", "ldv", 16, "vb", T.vb[:], T.v[:])
 
-    iota("ci", [[-1, C]], C - 1, 1)
     iota("ku", [[16, 8]], 0, 0)
+    iota("pc", [[0, 1]], 0, 1, slice(0, 1))
+    iota("rr", [[0, KB], [1, 16]], 0, 0)
     do("v", [], ["neg"], fill(T.neg[:], -1.0))
     do("g", ["neg"], ["go"], lambda e: e.affine_select(T.go[:], T.neg[:], [[-16, 8], [0, 64]], A.is_ge, 0.0, 0, 1))
     do("g", ["go"], ["gs"], lambda e: e.affine_select(T.gs[:], T.go[:], [[16, 8], [0, 64]], A.is_ge, 0.0, 15, -1))
     left, k0_keys = [], []
     for k in range(KB):
-        n = C - 16 * k - 16 * sum(i >= k for i in BY_S) - 1 - DEEP
+        n = C - 16 * (k + 1) - 16 * sum(i > k for i in BY_S) - LIFT - DEEP
         left.append(n + (16 * k if k in BY_S else HALF if k else 0))
     k = 0
     while k < KB:
-        step, n = (left[k + 1] - left[k] if 0 < k < KB - 1 else 0), 1
-        while 0 < k and k + n < KB and left[k + n] - left[k + n - 1] == step:
+        step, n = (left[k + 1] - left[k] if k < KB - 1 else 0), 1
+        while k + n < KB and left[k + n] - left[k + n - 1] == step:
             n += 1
         k0_keys.append("k0:%d" % k)
         iota("k0", [[step, n]], left[k], 0, slice(k, k + n), k0_keys[-1])
         k += n
-    do("v", [], ["c64"], fill(T.c64[:], 64.0))
-    do("v", [], ["cnt0"], fill(T.cnt[:, 0:1], 0.0))
-    do("v", ["ci"], ["d15"], ts(T.d15[:], T.ci[:], 15, A.bitwise_and))
-    do("v", ["d15"], ["ctl"], ts(T.ctl[:], T.d15[:], 64.0, A.mult, -float(LIFT), A.add))
-    own_q = T.d15[:, 15:C:16]
-    do("v", ["d15"], ["la"], ts(T.la[:], own_q, -1.0, A.mult, 15.0, A.add))
-    do("v", ["d15"], ["lb"], ts(T.lb[:], own_q, -32.0, A.mult, -32.0, A.add))
-    do("v", ["ctl"], ["mask"], ts(T.mask[:], T.ctl[:], float(LIFT), A.is_equal))
-    do("v", ["la", "lb"], ["lc"], tt(T.lc[:], T.la[:], T.lb[:], A.mult))
-    do("v", ["ctl"], ["gate"], ts(T.gate[:], T.ctl[:], float(LIFT), A.not_equal))
-    do("v", ["lc"], ["ctl"], ts(T.ctl[:, 15:C:16], T.lc[:], -float(LIFT), A.add))
     do("v", ["ku"], ["offu"], cp(T.offu[:], T.ku[:]))
+    do("v", ["pc"], ["pq"], ts(T.pc[:, 1:2], T.pc[:, 0:1], 15, A.bitwise_and))
+    do("v", [], ["cnt0"], fill(T.cnt[:, 0:1], 0.0))
+    do("v", [], ["c64"], fill(T.c64[:], 64.0))
+    own_q = T.col[:, 0:1]
+    do("v", ["pq"], ["q"], cp(own_q, T.pc[:, 1:2]))
+    do("v", ["rr", "q"], ["side"], ts(T.side[:], T.rr[:], own_q, A.subtract, BIG, A.mult))
     do("v", ["ub"], ["qu"], quant(T.qu[:], T.su[:], T.ub[:]))
+    do("v", ["rr", "q"], ["drop"], ts(T.drop[:], T.rr[:], own_q, A.is_equal, -1024 * BIG, A.mult))
     do("v", ["qu", "offu"], ["qur"], cp(T.qur[:, 0:128].bitcast(dt.uint32), T.qu[:, 0:128].bitcast(dt.uint32).indirect(T.offu[:, 0:8])))
     do("v", ["qu", "offu"], ["sur"], cp(T.sur[:, 0:128], T.su[:, 0:128].indirect(T.offu[:, 0:8])))
+    do("v", ["rr", "q"], ["gate"], ts(T.gate[:], T.rr[:], own_q, A.not_equal))
     for i in range(NQ):
-        for j in range(64 * i, WIDE[i], 64):
-            z = 4 * (AT[i] + j)
-            do("s", ["neg"], ["fl%d" % k for k in range(4 * i, 4 * i + 4)] if j == 64 * i else ["flz%d" % i],
-               act(T.fl[:, z:z + 256], T.neg[:, 0:256], scale=0.0))
-    do("s", ["ctl"], ["ctlb"], act(T.ctlb[:], T.ctl[:]))
+        n = WIDE[i] - (C - 64 * i - 48)
+        do("s", ["neg"], ["fl%d" % k for k in range(KB - 4 * i - 3, KB - 4 * i + 1)] + (["fld"] if i == 0 else []),
+           act(T.fl[:, 4 * (AT[i + 1] - n):4 * AT[i + 1]], T.neg[:, 0:4 * n], scale=0.0))
+    do("s", ["side"], ["sg3"], act(T.sg3[:], T.side[:], F.Sign))
+    do("s", ["sg3"], ["sq"], act(T.sq[:], T.sg3[:], F.Square, bias=-0.25))
+    do("s", ["side"], ["col1"], act(T.col[:, 1:2], T.side[:, 15:16], F.Identity, scale=1 / BIG, bias=576.0))
+    do("s", ["sq"], ["ctlb"], act(T.ctlb[:], T.sq[:], F.Identity, scale=-1024.0, bias=576.0))
+    do("s", ["sq", "col1"], ["col2"], act(T.col[:, 2:3], T.sq[:, 15:16], F.Identity, scale=-1024.0, bias=T.col[:, 1:2]))
     iota("fh", [[1, C]], -HALF, 0)
     for b in range(4):
         do("g", ["c64"], ["eb%d" % b], lambda e: e.affine_select(
@@ -210,7 +221,14 @@ def rank_program(g, core, T, topo):
     def quant_const(b):
         do("v", ["eb%d" % b], ["qe%d" % b], quant(T.qe[:, S * b:S * b + S], T.se[:, S * b:S * b + S], T.eb[:, 512 * b:512 * b + 512]))
 
-    later = [lambda b=b: quant_const(b) for b in range(4)] + [lambda: do("v", ["vb"], ["qv"], quant(T.qv[:], T.sv[:], T.vb[:]))]
+    later = [lambda: do("v", ["sq"], ["ctl"], ts(T.ctl[:], T.sq[:], -1024.0, A.mult, 576.0, A.add)),
+             lambda: do("v", ["sq"], ["ctlp"], ts(T.ctlp[:], T.sq[:], -2.0, A.mult, 1.125, A.add)),
+             lambda: do("v", ["sq", "ctl"], ["ctl"], ts(T.ctl[:, 15:C:16], T.sq[:, 15:C:16], -1024.0, A.mult, 576.0 - 2 * LIFT, A.add))]
+    later += [lambda b=b: quant_const(b) for b in range(4)] + [lambda: do("v", ["vb"], ["qv"], quant(T.qv[:], T.sv[:], T.vb[:]))]
+
+    def spare():
+        if later:
+            later.pop(0)()
 
     def matmul(out, key, lhs, ls, lkey, rhs, rs, rkey, start=True, stop=True):
         do("t", lkey + rkey, [key], lambda e: e.matmul_mx(out, lhs, ls, rhs, rs, start, stop))
@@ -220,51 +238,73 @@ def rank_program(g, core, T, topo):
             return ["x0:%d" % h]
         return ["x%d:%d:%d" % (t, c, i) for c in ((1, 3) if h == 1 else (2,)) for i in range(4)]
 
-    def quant_state(t, h, part):
-        a, b = part
+    def quant_state(t, h):
+        a, b = H1 if h == 1 else H2
         do("v", state_keys(t, h), ["qx%d:%d" % (t, h)], quant(T["qx%d" % t][:, a:b], T["sx%d" % t][:, a:b], T["x%d" % t][:, 4 * a:4 * b]))
 
-    def score(t, h, part):
-        a, b = part
+    def score(t, h):
+        a, b = H1 if h == 1 else H2
         qx, sx = T["qx%d" % t], T["sx%d" % t]
         for p in ("pp0", "pp1") if h == 1 else ("pp2", "pp3"):
             matmul(T[p][:, 0:b - a], p, T.qur[:], T.sur[:], ["qur", "sur"], qx[:, a:b], sx[:, a:b], ["qx%d:%d" % (t, h)])
 
-    def take_scores(t, h, part):
-        a, b = part
+    def take(step, h):
+        a, b = H1 if h == 1 else H2
         p0, p1 = ("pp0", "pp1") if h == 1 else ("pp2", "pp3")
-        do("v", [p0, "mask"], ["mrow:%d" % h], tt(T.mrow[:, a:b], T[p0][:, 0:b - a], T.mask[:, a:b], A.mult))
-        do("s", [p1], ["srow:%d" % h], act(T.srow[:, a:b], T[p1][:, 0:b - a]))
-        do("v", ["mrow:%d" % h, "gate"], ["arow:%d" % h], scan(T.arow[:, back(a, b)], T.gate[:, back(a, b)], T.mrow[:, back(a, b)], 0.0, A.mult, A.add))
+        if step == "row":
+            do("s", [p1], ["srow:%d" % h], act(T.srow[:, a:b], T[p1][:, 0:b - a]))
+        elif step == "mask":
+            do("v", [p0, "side"], ["mrow:%d" % h], tt(T.mrow[:, a:b], T[p0][:, 0:b - a], T.side[:, a:b], A.add))
+        elif step == "own":
+            do("v", ["mrow:%d" % h, "drop"], ["arow:%d" % h], scan(T.arow[:, back(a, b)], T.drop[:, back(a, b)], T.mrow[:, back(a, b)], 0.0, A.add, A.max))
+        elif step == "flag":
+            do("v", ["arow:%d" % h, p0, "fld"], ["fld:%d" % h], tt(flags(KB, a, b), T[p0][:, 0:b - a], T.arow[:, a:b], A.is_ge))
+        else:
+            z = 4 * b - 4
+            d = T.fl[:, slice(z, 4 * a - 1 if a else None, -4)]
+            do("v", ["fld:%d" % h, "gate"], ["eqs:%d" % h], scan(T.eqs[:, back(a, b)], T.gate[:, back(a, b)], d, 0.0, A.mult, A.add))
 
     def add_base(a, b):
-        keys = ["cnt%d" % k if k in BY_S else "cntv%d" % (k >= HIGH) if k else "cnt0" for k in range(a, b)]
-        do("v", keys + ["tie", "ctlb"], ["ctlb:%d" % a], tt(T.ctlb[:, 16 * a + 15:16 * b:16], T.cnt[:, a:b], T.tie[:, a:b], A.add))
+        while a < b:
+            c = a + 1
+            while c < b and (c in BY_S) == (a in BY_S or a == 0):
+                c += 1
+            if a in BY_S or a == 0:
+                keys, src = ["cnt%d" % k for k in range(a, c)], T.cnt[:, a:c]
+            else:
+                keys, src = ["zs:%d" % k for k in range(a, c)], T.zs[:, 224 * a + 223:224 * c:224]
+            do("v", keys + ["tie", "ctlb"], ["ctlb:%d" % k for k in range(a, c)], tt(T.ctlb[:, 16 * a + 15:16 * c:16], src, T.tie[:, a:c], A.add))
+            a = c
 
-    def settle(t, bank, a, b):
-        do("v", [bank, "ctlb:%d" % a], ["hcol:%d" % a], scan(T.hcol[:, 16 * a:16 * b], T[bank][:, 16 * a:16 * b], T.ctlb[:, 16 * a:16 * b], -float(DEEP), A.max, A.add))
+    def settle(bank, a, b):
+        do("v", [bank] + ["ctlb:%d" % k for k in range(a, b)], ["hcol:%d" % a],
+           scan(T.hcol[:, 16 * a:16 * b], T[bank][:, 16 * a:16 * b], T.ctlb[:, 16 * a:16 * b], -float(DEEP), A.max, A.add))
+
+    def hand(t, a, b):
         key = "own%d:%d" % (t, a)
         do("v", ["hcol:%d" % a], [key], ts(T["own%d" % t][:, a:b], T.hcol[:, 16 * a + 15:16 * b:16], float(DEEP), A.add))
         h = "h" if a >= HIGH else "l"
-        send(t, [("land%d:%s" % (t, h), "land%d" % t, "own%d" % t, lambda n: T[n][:, a:b], key)], "rx%s%d" % (h, t))
+        land = span("land%d" % t, *((16 * HIGH, C) if a >= HIGH else (0, 16 * HIGH)))
+        send(t, [(land, "land%d" % t, "own%d" % t, lambda n: T[n][:, a:b], [key])], "rx%s%d" % (h, t))
+
+    def put(t, a, b, keys):
+        do("v", keys + ["fh"], ["orow"], cp(T.orow[:, 0:C].indirect(T["own%d" % t][:, a:b]), T.fh[:, 16 * a:16 * b]))
 
     def places(t):
         row = ["srow:1", "srow:2"]
-        do("v", ["arow:1", "arow:2"], ["aw"], cp(T.aw[:, 0:KB], T.arow[:, 0:C:16]))
         pend, done = [], []
+        top = FIRST if t == 0 else KB
 
-        def flags(k, a, b):
-            z = 4 * AT[k // 4]
-            return T.fl[:, z + 4 * a + k % 4:z + 4 * b:4]
+        def own(k):
+            return T.arow[:, 16 * k:16 * k + 1], "arow:%d" % (1 if 16 * k >= S else 2)
 
         def sign(k):
-            rel = "rel%d" % (k % 4)
+            rel = "rel%d" % (BY_S.index(k) % 4)
             do("s", [rel], ["fl%d" % k, "cnt%d" % k], act(flags(k, 0, 16 * k), T[rel][:, 0:16 * k], F.Sign, scale=-1.0, accum_out=T.cnt[:, k:k + 1]))
-            do("s", [rel], ["fld%d" % k], act(flags(k, 16 * k, 16 * k + 16), T[rel][:, 16 * k:16 * k + 16], F.Sign, scale=-1.0))
 
         for k in BY_S:
-            rel = "rel%d" % (k % 4)
-            do("s", row + ["aw"], [rel], act(T[rel][:, 0:16 * k + 16], T.srow[:, 0:16 * k + 16], F.Relu, bias=T.aw[:, k:k + 1], scale=-1.0))
+            rel = "rel%d" % (BY_S.index(k) % 4)
+            do("s", row + [own(k)[1]], [rel], act(T[rel][:, 0:16 * k], T.srow[:, 0:16 * k], F.Relu, bias=own(k)[0], scale=-1.0))
             pend.append(k)
             if len(pend) > 1:
                 sign(pend.pop(0))
@@ -274,171 +314,194 @@ def rank_program(g, core, T, topo):
             z = 224 * k + 224
             do("v", ["fl%d" % k], ["zs:%d" % k], scan(T.zs[:, z - 8 * k:z], flags(k, 0, 8 * k), flags(k, 8 * k, 16 * k), -float(HALF), A.add, A.add))
 
-        def tally(a, b, n):
-            ks = [k for k in BY_V if a <= k < b]
-            at, runs = 0, []
-            while at < len(ks):
-                end = at
-                while end + 1 < len(ks) and ks[end + 1] == ks[end] + 1:
-                    end += 1
-                runs.append((ks[at], ks[end] + 1))
-                at = end + 1
-            for i, (c, d) in enumerate(runs):
-                key = "cntv%d" % n
-                do("v", ["zs:%d" % k for k in range(c, d)], [key] if i == len(runs) - 1 else [key + "'"],
-                   cp(T.cnt[:, c:d], T.zs[:, 224 * c + 223:224 * d:224]))
-
         def sum_up(i):
             a, b = AT[i], AT[i + 1]
-            keys = [n % k for k in range(4 * i, 4 * i + 4) for n in ("fl%d", "fld%d")] + ["flz%d" % i]
+            keys = ["fl%d" % k for k in range(KB - 4 * i - 3, KB - 4 * i + 1)] + (["fld:1", "fld:2"] if i == 0 else [])
             do("v", keys, ["qf%d" % i], quant(T.qf[:, a:b], T.sf[:, a:b], T.fl[:, 4 * a:4 * b]))
 
             def add(bank, n, start, stop):
                 matmul(T[bank][:, 0:n], bank, T.qg[:], T.sg[:], ["qg"], T.qf[:, a:a + n], T.sf[:, a:a + n], ["qf%d" % i], start, stop)
-            last = len([j for j in done if j >= HIGH // 4]) == NQ - HIGH // 4 - 1
-            if i >= HIGH // 4:
-                if t == 0 and i == NQ - 1:
+            high = [j for j in done if j < NH]
+            if i < NH:
+                if t == 0 and i == 0:
                     add("pp3", C, True, True)
-                add("pp1", b - a, not any(j >= HIGH // 4 for j in done), last)
+                add("pp1", b - a, not high, len(high) == NH - 1)
             add("pp2", min(16 * HIGH, b - a), not done, len(done) == NQ - 1)
             done.append(i)
 
-        prev, n = None, 0
+        prev = None
         for step in PLAN:
             if step == "c":
-                for _ in range(2 if t == 0 else 0):
-                    later.pop(0)()
+                spare()
+            elif step == "tie":
+                if t == 0:
+                    do("v", ["col2"] + k0_keys, ["k1"], ts(T.k1[:], T.k0[:], T.col[:, 2:3], A.add))
+                take("sum", 2)
+            elif step == "tie2":
+                do("v", ["eqs:1", "eqs:2", "k1"], ["tie"], tt(T.tie[:], T.eqs[:, 0:C:16], T.k1[:], A.add))
             elif step == "early":
                 if t == 0:
                     add_base(FIRST, KB)
-                    settle(t, "pp3", FIRST, KB)
-            elif step == "tallyh":
-                tally(HIGH, KB, 1)
-                add_base(HIGH, FIRST if t == 0 else KB)
+            elif step == "early2":
+                if t == 0:
+                    settle("pp3", FIRST, KB)
+            elif step == "early3":
+                if t == 0:
+                    hand(t, FIRST, KB)
+            elif step == "baseh":
+                add_base(HIGH, top)
             elif step == "high":
-                settle(t, "pp1", HIGH, FIRST if t == 0 else KB)
-            elif step == "tallyl":
-                tally(1, HIGH, 0)
+                settle("pp1", HIGH, top)
+            elif step == "offh":
+                hand(t, HIGH, top)
+            elif step == "puth":
+                put(t, HIGH, KB, ["own%d:%d" % (t, k) for k in {HIGH, top} if k < KB])
+            elif step == "basel":
                 add_base(0, HIGH)
+            elif step == "low":
+                settle("pp2", 0, HIGH)
+            elif step == "offl":
+                hand(t, 0, HIGH)
+            elif step == "putl":
+                put(t, 0, HIGH, ["own%d:0" % t])
+            elif step == "flag":
+                take("flag", 2)
+            elif step == "sum":
+                add_up(prev)
+                prev = None
             elif step in ["q%d" % i for i in range(NQ)]:
                 sum_up(int(step[1]))
             else:
                 k = step
-                do("v", row + ["aw"], ["fl%d" % k], ts(flags(k, 0, 16 * k + 16), T.srow[:, 0:16 * k + 16], T.aw[:, k:k + 1], A.is_ge))
+                do("v", row + [own(k)[1]], ["fl%d" % k], ts(flags(k, 0, 16 * k), T.srow[:, 0:16 * k], own(k)[0], A.is_ge))
                 if prev:
                     add_up(prev)
                 prev = k
-                n += 1
-                if n == 1:
-                    for h, p, (a, b) in ((1, "pp0", H1), (2, "pp2", H2)):
-                        do("v", ["arow:%d" % h, p], ["eqr:%d" % h], tt(T.eqr[:, a:b], T.arow[:, a:b], T[p][:, 0:b - a], A.is_equal))
-                if n == 2:
-                    do("v", ["eqr:1", "eqr:2", "gate"], ["eqs"], scan(T.eqs[:, back(0, C)], T.gate[:, back(0, C)], T.eqr[:, back(0, C)], 0.0, A.mult, A.add))
-                    if t == 0:
-                        do("v", ["lc"] + k0_keys, ["k1"], tt(T.k1[:], T.lc[:], T.k0[:], A.add))
-                if n == 3:
-                    do("v", ["eqs", "k1"], ["tie"], tt(T.tie[:], T.eqs[:, 0:C:16], T.k1[:], A.add))
-        settle(t, "pp2", 0, HIGH)
 
-    def wrap(row, keys, part=(0, C), ctl="ctl", to=("hrow:l", "hrow:h")):
-        a, b = part
-        do("v", keys + [ctl], list(to), scan(T.hrow[:, a:b], row[:, a:b], T[ctl][:, a:b], -1024.0, A.max, A.add))
-        return T.hrow[:, a + 15:b:16]
+    def wrap(row, keys, a, b, ctl="ctl"):
+        do("v", keys + [ctl], span("hrow", a, b), scan(T.hrow[:, a:b], row[:, a:b], T[ctl][:, a:b], -1024.0, A.max, A.add))
 
-    def three(name):
-        return [name + ":s", name + ":v", name + ":h"]
+    def offsets(name, at, key, a, b, add, times=None):
+        out, h = T[name][:, at + a // 16:at + b // 16], T.hrow[:, a + 15:b:16]
+        do("v", span("hrow", a, b), span(key, a, b), ts(out, h, add, A.add) if times is None else ts(out, h, add, A.add, times, A.mult))
 
-    def both(name):
-        return [name + ":l", name + ":h"]
-
-    def shift(q, an, keys, bn, d, a, b):
-        do(q, keys, [bn + ":%d" % a], act(T[bn][:, a:b], T[an][:, a:b], F.Identity, bias=-d) if q == "s"
-           else ts(T[bn][:, a:b], T[an][:, a:b], -d, A.add))
-        return bn + ":%d" % a
+    def planes(t, i):
+        do("s", state_keys(t, 1) + state_keys(t, 2), ["xp%d" % i], act(T.xp[:, C * i:C * i + C], T["x%d" % t][:, i:4 * C:4]))
 
     def cycles(t):
-        own, land = "own%d" % t, "land%d" % t
-        parts = [own + ":0", own + ":%d" % HIGH] + ([own + ":%d" % FIRST] if t == 0 else [])
-        do("v", parts + ["fh"], ["orow"], cp(T.orow[:, 0:C].indirect(T[own][:, 0:KB]), T.fh[:]))
+        land = "land%d" % t
         if t == 0:
             do("s", ["fh"], ["thr"], act(T.thr[:], T.fh[:], F.Identity, bias=-0.5))
-            do("s", ["ctl"], ["ctlp"], act(T.ctlp[:], T.ctl[:], scale=1.0 / 1024))
-        m, e, d = 16 * HIGH, LOW // 16, 1.0 / 1024
-        do("s", ["orow", land + ":h"], ["j0:h"], act(T.j0[:, m:C], T.orow[:, 0:C].indirect(T[land][:, HIGH:KB])))
-        bkeys = [shift("s", "j0", ["j0:h"], "b0", d, m, C)]
-        while later:
-            later.pop(0)()
-        h = wrap(T.j0, ["j0:h"], (m, C), to=["hrow:h"])
-        do("v", ["hrow:h"], ["off0:h"], ts(T.off0[:, HIGH:KB], h, float(LIFT + HALF), A.add))
-        do("s", ["orow", land + ":l"], ["j0:s"], act(T.j0[:, 0:LOW], T.orow[:, 0:C].indirect(T[land][:, 0:e])))
-        do("v", ["orow", land + ":l"], ["j0:v"], cp(T.j0[:, LOW:m], T.orow[:, 0:C].indirect(T[land][:, e:HIGH])))
-        h = wrap(T.j0, ["j0:s", "j0:v"], (0, m), to=["hrow:l"])
-        bkeys.append(shift("v", "j0", ["j0:v"], "b0", d, LOW, m))
-        do("v", ["hrow:l"], ["off0:l"], ts(T.off0[:, 0:HIGH], h, float(LIFT + HALF), A.add))
-        bkeys.append(shift("v", "j0", ["j0:s"], "b0", d, 0, LOW))
-        win, wkeys = T.j0, three("j0")
-        for k in range(9):
-            off, j, jn = "off%d" % (k % 2), "j%d" % (k % 2), "j%d" % ((k + 1) % 2)
-            an, bk, bn = "a%d" % (k % 2), "b%d" % (k % 2), "b%d" % ((k + 1) % 2)
-            if k < 8:
-                do("s", three(j) + both(off), three(jn), act(T[jn][:], T[j][:, 0:C].indirect(T[off][:, 0:KB])))
-            do("v", wkeys + both(off) + bkeys, [an], tt(T[an][:], win[:, 0:C].indirect(T[off][:, 0:KB]), T[bk][:], A.min))
-            for key in bkeys:
-                reader.setdefault(bk + "*", []).extend(reader.get(key, []))
-            win, wkeys = T[an], [an]
-            if k < 8:
-                d = (2.0 ** (k + 1)) / 1024
-                for q in "sv":
-                    before(q, [], [bn + "*"])
-                reader[bn + "*"] = []
-                bkeys = [shift("s", an, [an], bn, d, 0, CUT[0])]
-                h = wrap(T[jn], three(jn))
-                bkeys.append(shift("v", an, [an], bn, d, CUT[0], CUT[1]))
-                o = "off%d" % ((k + 1) % 2)
-                do("v", both("hrow"), both(o), ts(T[o][:], h, float(LIFT + HALF), A.add))
-                bkeys.append(shift("v", an, [an], bn, d, CUT[1], C))
-        wkey = wkeys[0]
-        do("v", [wkey, "thr"], ["wrow"], scan(T.wrow[:], win[:], T.thr[:], -1024.0, A.max, A.max))
-        do("v", [wkey, "ctl"], ["hkey"], scan(T.hkey[:], win[:], T.ctl[:], -1024.0, A.max, A.add))
-        do("v", ["wrow", "thr"], ["crow"], scan(T.crow[:], T.wrow[:], T.thr[:], -HALF / 1024, A.add, A.subtract))
-        own_key, up = T.hkey[:, 15:C:16], float(MAGIC + LIFT + HALF)
-        do("v", ["hkey"], ["offm"], ts(T.offm[:], own_key, up, A.add, float(MAGIC), A.subtract))
-        do("v", ["hkey"], ["mw"], ts(T.mw[:], own_key, up, A.add, float(MAGIC), A.subtract))
-        for q, a, b in (("s", 0, ENDS), ("v", ENDS, C)):
-            src = T.crow[:, 0:C].indirect(T.offm[:, a // 16:b // 16])
-            do(q, ["crow", "offm"], ["prow:" + q], act(T.prow[:, a:b], src) if q == "s" else cp(T.prow[:, a:b], src))
-        do("v", ["hkey", "mw"], ["kw"], tt(T.kw[:], own_key, T.mw[:], A.subtract))
-        h = wrap(T.prow, ["prow:s", "prow:v"], ctl="ctlp")
-        do("v", both("hrow") + ["kw"], ["pw"], tt(T.pw[:], h, T.kw[:], A.subtract))
-        do("v", ["pw"], ["offp"], ts(T.offp[:], T.pw[:], (LIFT + HALF) / 1024 - LIFT - HALF - 0.5, A.add, 1024.0, A.mult))
-        do("v", ["offp", "fh"], ["erow"], cp(T.erow[:, 0:C].indirect(T.offp[:, 0:KB]), T.fh[:]))
-        h = wrap(T.erow, ["erow"])
-        for i in (2, 0, 3, 1):
-            do("v", both("hrow"), ["offe%d" % i], ts(T["offe%d" % i][:], h, LIFT + HALF + 0.25 * i, A.add, 4.0, A.mult))
+            do("s", ["sq"], ["col3"], act(T.col[:, 3:4], T.sq[:, 15:16], F.Identity, scale=2.0, bias=float(MAGIC + LIFT + HALF + 1)))
 
-    def lay_out(t, tile, key, part):
+        def jrow(k):
+            return "jp" if k == 0 else "j%d" % (k % 2)
+
+        def arow(k):
+            return "jp" if k == 0 else "a%d" % (k % 2)
+
+        def step(k, op):
+            what = op[0]
+            if what == "c":
+                return spare()
+            q, a, b = op[1:4]
+            lists = (T[land], 0, land) if k < 0 else (T.off, KB * k, "off%d" % k)
+            off = lists[0][:, lists[1] + a // 16:lists[1] + b // 16]
+            if what == "G" and k < 8:
+                j, jn = "orow" if k < 0 else jrow(k), jrow(k + 1)
+                do(q, (["orow"] if k < 0 else span(j)) + span(lists[2], a, b), span(jn, a, b), move(q, T[jn][:, a:b], T[j][:, 0:C].indirect(off)))
+            elif what == "W" and k < 8:
+                wrap(T[jrow(k + 1)], span(jrow(k + 1), a, b), a, b)
+            elif what == "O" and k < 8:
+                offsets("off", KB * (k + 1), "off%d" % (k + 1), a, b, float(LIFT + HALF))
+            elif what == "S" and k + op[4] < 9:
+                n = k + op[4]
+                src, out, d = arow(n), "b%d" % (n % 2), 2.0 ** n / 1024
+                do(q, span(src, a, b), span(out, a, b), act(T[out][:, a:b], T[src][:, a:b], F.Identity, bias=-d) if q == "s"
+                   else ts(T[out][:, a:b], T[src][:, a:b], -d, A.add))
+            elif what == "K":
+                win, out, bk = arow(k), arow(k + 1), "b%d" % (k % 2)
+                do("v", span(win) + span(lists[2], a, b) + span(bk, a, b), span(out, a, b),
+                   tt(T[out][:, a:b], T[win][:, 0:C].indirect(off), T[bk][:, a:b], A.min))
+
+        for op in START:
+            step(-1, op)
+        while later:
+            spare()
+        for k in range(9):
+            for op in LEVEL:
+                step(k, op)
+        planes(t, 0)
+        planes(t, 1)
+        key = arow(9)
+        win = T[key]
+        for a, b in (LA, LB):
+            do("v", span(key, a, b) + ["thr"], span("wrow", a, b), scan(T.wrow[:, a:b], win[:, a:b], T.thr[:, a:b], -1024.0, A.max, A.max))
+            do("v", span(key, a, b) + ["ctl"], span("hkey", a, b), scan(T.hkey[:, a:b], win[:, a:b], T.ctl[:, a:b], -1024.0, A.max, A.add))
+        own_key, up = T.hkey[:, 15:C:16], float(MAGIC + LIFT + HALF)
+        a, b = LA
+        do("v", span("wrow", a, b) + ["thr"], span("crow", a, b), scan(T.crow[:, a:b], T.wrow[:, a:b], T.thr[:, a:b], -HALF / 1024, A.add, A.subtract))
+        do("v", span("hkey"), ["offm"], ts(T.offm[:], own_key, up, A.add, float(MAGIC), A.subtract))
+        do("v", span("hkey") + ["col3"], ["mw"], ts(T.mw[:], own_key, up, A.add, T.col[:, 3:4], A.subtract))
+        a, b = LB
+        do("v", span("wrow", a, b) + span("crow", a - 32, a) + ["thr"], span("crow", a, b),
+           scan(T.crow[:, a:b], T.wrow[:, a:b], T.thr[:, a:b], T.crow[:, a - 1:a], A.add, A.subtract))
+        do("v", span("hkey") + ["mw"], ["ctlp"], tt(T.ctlp[:, 15:C:16], T.mw[:], own_key, A.subtract))
+        for q, a, b in (("s", 0, ENDS), ("v", ENDS, C)):
+            do(q, span("crow") + ["offm"], span("prow", a, b), move(q, T.prow[:, a:b], T.crow[:, 0:C].indirect(T.offm[:, a // 16:b // 16])))
+        planes(t, 2)
+        planes(t, 3)
+        wrap(T.prow, span("prow"), 0, C, "ctlp")
+        offsets("offp", 0, "offp", 0, C, (LIFT + HALF) / 1024, 1024.0)
+        do("v", span("offp") + ["fh"], ["erow"], cp(T.erow[:, 0:C].indirect(T.offp[:, 0:KB]), T.fh[:]))
+        for a, b in (H2, H1):
+            wrap(T.erow, ["erow"], a, b)
+        for a, b in (H2, H1):
+            offsets("offe", 0, "offe", a, b, float(LIFT + HALF))
+
+    def lay(t, tile, key, part, i):
         a, b = part
-        for i in (2, 0, 3, 1):
-            out = tile[:, 4 * a + i:4 * b:4]
-            src = T["x%d" % t][:, 0:4 * C].indirect(T["offe%d" % i][:, a // 16:b // 16])
-            do("v" if i < 2 else "s", state_keys(t, 1) + state_keys(t, 2) + ["offe%d" % i], [key + str(i)], cp(out, src) if i < 2 else act(out, src))
+        q = "v" if i < 2 else "s"
+        src = T.xp[:, C * i:C * i + C].indirect(T.offe[:, a // 16:b // 16])
+        do(q, ["xp%d" % i] + span("offe", a, b), [key + str(i)], move(q, tile[:, 4 * a + i:4 * b:4], src))
 
     def layer(t, i, qz, sz, a, b, key, bank, start=True):
         matmul(T[bank][:, 0:b - a], bank, T.qw[:, S * i:S * i + S], T.sw[:, S * i:S * i + S], ["w"], qz[:, a:b], sz[:, a:b], [key], start, True)
 
-    def stay(t):
+    def lay_out(t):
         zt, qz, sz, xn = T["zt%d" % t], T["qz%d" % t], T["sz%d" % t], T["x%d" % (t + 1)]
-        for h, (a, b) in HALVES.items():
-            zk = "z%d:%d:" % (t, h)
-            lay_out(t, zt, zk, (a, b))
-            do("v", [zk + str(i) for i in range(4)], ["qz%d:%d" % (t, h)], quant(qz[:, a:b], sz[:, a:b], zt[:, 4 * a:4 * b]))
+        bt, qb, sb, qc, sc = ["%s%d" % (n, t) for n in ("bt", "qb", "sb", "qc", "sc")]
+
+        def gather(h, i):
+            lay(t, zt, "z%d:%d:" % (t, h), HALVES[h], i)
+
+        def through(h):
+            a, b = HALVES[h]
+            do("v", ["z%d:%d:%d" % (t, h, i) for i in range(4)], ["qz%d:%d" % (t, h)], quant(qz[:, a:b], sz[:, a:b], zt[:, 4 * a:4 * b]))
             for i in range(4):
                 layer(t, i, qz, sz, a, b, "qz%d:%d" % (t, h), ("pr%d" if h == 1 else "pp%d") % i)
-        a, b = H1
-        for i in range(4):
+
+        def times64(i):
+            a, b = H1
             out, src = T.z64[:, 4 * a + i:4 * b:4], zt[:, 4 * a + i:4 * b:4]
-            reads = ["z%d:%d:%d" % (t, h, i) for h in HALVES]
-            do("v" if i % 2 else "s", reads, ["z64:%d" % i], ts(out, src, 64.0, A.mult) if i % 2 else act(out, src, scale=64.0))
+            do("v" if i < 2 else "s", ["z%d:%d:%d" % (t, h, i) for h in HALVES], ["z64:%d" % i],
+               ts(out, src, 64.0, A.mult) if i < 2 else act(out, src, scale=64.0))
+
+        for i in (2, 0, 3, 1):
+            lay(t, T[bt], bt + ":", H2, i)
+        for h, i in ((1, 2), (1, 3), (3, 2), (3, 3), (1, 0)):
+            gather(h, i)
+        do("v", [bt + ":%d" % i for i in range(4)], [qb, sb], quant(T[qb][:], T[sb][:], T[bt][:]))
+        send(t, [([qc], qc, qb, lambda n: T[n][:].bitcast(dt.uint8), [qb]), ([sc], sc, sb, lambda n: T[n][:], [sb])], "rxb%d" % t)
+        gather(1, 1)
+        gather(3, 0)
+        through(1)
+        gather(3, 1)
+        times64(2)
+        times64(3)
+        times64(0)
+        through(3)
+        times64(1)
         for h, (a, b) in HALVES.items():
             for i in range(4):
                 bank = ("pr%d" if h == 1 else "pp%d") % i
@@ -453,13 +516,16 @@ def rank_program(g, core, T, topo):
         matmul(T["pr%d" % i][:, 0:S], "pr%d" % i, T.qe[:, S * i:S * i + S], T.se[:, S * i:S * i + S], ["qe%d" % i], T[qc][:], T[sc][:], [qc, sc], start, stop)
 
     def arrive(t):
-        zt, qz, sz = T["zt%d" % t], T["qz%d" % t], T["sz%d" % t]
+        zt = T["zt%d" % t]
         for i in range(4):
             unpack(t, i, True, True)
             do("v", ["pr%d" % i], ["z%d:2:%d" % (t, i)], ts(zt[:, i:4 * S:4], T["pr%d" % i][:, 0:S], 0.015625, A.mult))
-        do("v", ["z%d:2:%d" % (t, i) for i in range(4)], ["qz%d:2" % t], quant(qz[:, 0:S], sz[:, 0:S], zt[:, 0:4 * S]))
         for i in range(4):
             unpack(t, i, True, False)
+
+    def arrive_layer(t):
+        zt, qz, sz = T["zt%d" % t], T["qz%d" % t], T["sz%d" % t]
+        do("v", ["z%d:2:%d" % (t, i) for i in range(4)], ["qz%d:2" % t], quant(qz[:, 0:S], sz[:, 0:S], zt[:, 0:4 * S]))
         for i in range(4):
             layer(t, i, qz, sz, 0, S, "qz%d:2" % t, "pr%d" % i, False)
 
@@ -469,46 +535,63 @@ def rank_program(g, core, T, topo):
             do("s" if i < 2 else "v", ["pr%d" % i], ["x%d:2:%d" % (t + 1, i)],
                act(out, src, scale=0.015625) if i < 2 else ts(out, src, 0.015625, A.mult))
 
-    def finish(t, h, part):
-        a, b = part
+    def finish(t, h):
+        a, b = H1 if h == 1 else H2
         q, s, key, p = T["qx%d" % t], T["sx%d" % t], "qx%d:%d" % (t, h), "pp0" if h == 1 else "pp2"
-        store("y", [key], T.oc[:, 4 * a:4 * b], q[:, a:b].bitcast(dt.uint8))
         matmul(T[p][:, 0:b - a], p, T.qv[:], T.sv[:], ["qv"], q[:, a:b], s[:, a:b], [key])
-
-    def store_rest(t, h, part):
-        a, b = part
-        s, key, p = T["sx%d" % t], "qx%d:%d" % (t, h), "pp0" if h == 1 else "pp2"
-        do("s", [p], ["ysb:%d" % h], act(T.ysb[:, a:b], T[p][:, 0:b - a]))
-        store("s", ["ysb:%d" % h], T.y[:, a:b], T.ysb[:, a:b])
+        store("y", [key], T.oc[:, 4 * a:4 * b], q[:, a:b].bitcast(dt.uint8))
         for k in range(4):
             store("y", [key], T.osc[4 * k:4 * k + 4, a:b], s[32 * k:32 * k + 4, a:b])
 
-    quant_state(0, 1, H1)
-    score(0, 1, H1)
-    quant_state(0, 2, H2)
-    score(0, 2, H2)
+    def store_y(h):
+        a, b = H1 if h == 1 else H2
+        p = "pp0" if h == 1 else "pp2"
+        do("s", [p], ["ysb:%d" % h], act(T.ysb[:, a:b], T[p][:, 0:b - a]))
+        store("s", ["ysb:%d" % h], T.y[:, a:b], T.ysb[:, a:b])
+
+    quant_state(0, 1)
+    score(0, 1)
+    quant_state(0, 2)
+    score(0, 2)
+    take("row", 1)
+    take("row", 2)
+    take("mask", 1)
+    take("mask", 2)
+    take("own", 1)
+    take("own", 2)
+    take("flag", 1)
     do("v", ["gs"], ["qg"], quant(T.qg[:], T.sg[:], T.gs[:]))
-    take_scores(0, 1, H1)
-    take_scores(0, 2, H2)
+    take("sum", 1)
     for t in range(R):
         places(t)
         cycles(t)
-        bt, qb, sb, qc, sc = ["%s%d" % (n, t) for n in ("bt", "qb", "sb", "qc", "sc")]
-        lay_out(t, T[bt], bt + ":", H2)
-        do("v", [bt + ":%d" % i for i in range(4)], [qb, sb], quant(T[qb][:], T[sb][:], T[bt][:]))
-        send(t, [(qc, qc, qb, lambda n: T[n][:].bitcast(dt.uint8), qb), (sc, sc, sb, lambda n: T[n][:], sb)], "rxb%d" % t)
-        stay(t)
+        lay_out(t)
         if t == R - 1:
             do("s", ["erow"], ["elf"], act(T.elf[:], T.erow[:], F.Identity, bias=float(HALF)))
             store("y", ["elf"], T.el[:], T.elf[0:128:16, :])
         arrive(t)
-        quant_state(t + 1, 1, H1)
-        arrived(t)
-        last, then = (score, take_scores) if t < R - 1 else (finish, store_rest)
-        last(t + 1, 1, H1)
-        quant_state(t + 1, 2, H2)
-        last(t + 1, 2, H2)
-        then(t + 1, 1, H1)
-        then(t + 1, 2, H2)
+        quant_state(t + 1, 1)
+        if t < R - 1:
+            score(t + 1, 1)
+            arrive_layer(t)
+            take("row", 1)
+            take("mask", 1)
+            arrived(t)
+            take("own", 1)
+            quant_state(t + 1, 2)
+            score(t + 1, 2)
+            take("row", 2)
+            take("flag", 1)
+            take("mask", 2)
+            take("sum", 1)
+            take("own", 2)
+        else:
+            arrive_layer(t)
+            finish(t + 1, 1)
+            arrived(t)
+            store_y(1)
+            quant_state(t + 1, 2)
+            finish(t + 1, 2)
+            store_y(2)
     for sem in sorted(count):
         g.wait_ge(T.sem[sem], count[sem])

@@ -9,24 +9,65 @@ AT = [sum(WIDE[:i]) for i in range(NQ + 1)]
 FIRST = 26
 HIGH = 14
 NH = 4
-BY_S = [27, 26, 25, 24, 23, *range(13, 0, -1)]
-PLAN = [22, "flag", 21, "tie", 20, "tie2", 19, 18, 17, 16, "q0", "early", 15, "early2", 14, "early3", "q2", "sum", "q1",
-        "baseh", "q3", "c", "c", "high", "c", "offh", "c", "c", "puth", "q4", "q5", "q6", "basel", "low", "offl", "putl"]
 ENGINES = 8
-H2, H1 = (0, S), (S, C)
-HALVES = {1: (S, S + 160), 3: (S + 160, C)}
+PART = {1: (S, S + 160), 3: (S + 160, C), 2: (0, S)}
+BANKS = {1: ("pp0", "pp1"), 3: ("pp2", "pp3"), 2: ("pr0", "pr1")}
 HALF = C // 2
 LIFT = 512
 DEEP = 1024
 BIG = 2.0 ** 80
 MAGIC = 12582912
-LA, LB = (0, HALF), (HALF, C)
-START = [("G", "s", HALF, 352), ("G", "v", 352, C), ("G", "s", 0, 128), ("G", "v", 128, HALF),
-         ("W", "v") + LB, ("W", "v") + LA, ("O", "v") + LB, ("O", "v") + LA]
-K1, K2, K3 = (0, 128), (128, 320), (320, C)
-LEVEL = [("G", "s") + LA, ("S", "s") + K1 + (0,), ("S", "s") + K2 + (0,), ("G", "s") + LB, ("S", "s") + K3 + (0,),
-         ("W", "v") + LA, ("K", "v") + K1, ("O", "v") + LA, ("K", "v") + K2, ("W", "v") + LB, ("K", "v") + K3, ("O", "v") + LB]
-ENDS = 224
+RELS = 6
+
+SCORE = {"v": "qx1 qx2 mask1 mask2 own1 own2 flag1 qg sum1", "s": "row1 row2", "t": "sc1 sc2"}
+ORDER = {"v": "g22 flag2 g21 u22 k1 sum2 g20 u21 tie g19 u20 g18 u19 g17 u18 g16 u17 q0 base26 g15 u16 set26 g14 u15 off26 q2 u14 q1 "
+              "base14 base23 q3 g12 ctl u12 set14 g11 off14 u11 ctlp ctl15 q4 put:224:352 q5 q6 base0 base11 base13 put:352:384 set0 put:384:448 off0 "
+              "qe0 qe1 put:0:224",
+         "s": "r27 r26 s27 r25 s26 r24 s25 r23 s24 r13 s23 r10 s13 r9 s10 r8 s9 r7 s8 r6 s7 r5 s6 r4 s5 r3 s4 r2 s3 r1 s2 s1 thr col3",
+         "t": "e0 h0 l0 h2 l2 h1 l1 h3 l3 l4 l5 l6"}
+START = {"v": "G:352:448@-1 G:128:224@-1 W:224:448@-1 W:0:224@-1 O:224:448@-1 O:0:224@-1 qe2 qe3 qv "
+              "W:0:224@0 K:0:128@0 O:0:224@0 K:128:320@0 W:224:448@0 K:320:448@0 O:224:448@0",
+         "s": "G:224:352@-1 G:0:128@-1 G:0:224@0 S:0:128@0 S:128:320@0 G:224:448@0 S:320:448@0"}
+LEVEL = {"v": "W:0:224@0 K:0:128@0 O:0:224@0 K:128:320@0 W:224:448@0 K:320:448@0 O:224:448@0",
+         "s": "G:0:224@0 S:0:128@0 S:128:320@0 G:224:448@0 S:320:448@0"}
+ENDS = {"v": "K:0:128@8 K:128:320@8 K:320:448@8 U:0:224 H:0:224 U:224:448 H:224:448 C:0:224 offm mw C:224:448 ctlm P:224:448 W:0:448 O:0:448 "
+             "pute W:0:128e W:128:448e O:0:128e O:128:448e",
+        "s": "S:0:128@8 S:128:320@8 S:320:448@8 p0 p1 P:0:224 p2 p3"}
+NEXT = {"v": "b0 b1 z10 qb z11 z30 qz1 z31 m30 m32 m33 qz3 a10 a11 a12 a13 m31 a30 a31 a32 a33 c2 c3 "
+             "qz2 qx1 mask1 y2 y3 own1 qx2 flag1 mask2 sum1 own2",
+        "s": "b2 b3 z12 z13 z32 z33 m10 m11 m12 m13 x10 x11 x12 x13 c0 c1 x30 x31 x32 x33 row1 y0 y1 row2",
+        "t": "w10 w11 w12 w13 w30 w31 w32 w33 d0 d1 d2 d3 f0 f1 f2 f3 w20 w21 w22 w23 sc1 sc2"}
+LAST = {"v": "b0 b1 z10 qb z11 z30 qz1 z31 m30 m32 m33 qz3 a10 a11 a12 a13 m31 a30 a31 a32 a33 c2 c3 qz2 qx1 y2 y3 qx2",
+        "s": "b2 b3 z12 z13 z32 z33 m10 m11 m12 m13 x10 x11 x12 x13 c0 c1 x30 x31 x32 x33 elf y0 y1 ysb1 sty1 ysb2 sty2",
+        "t": "w10 w11 w12 w13 w30 w31 w32 w33 d0 d1 d2 d3 f0 f1 f2 f3 w20 w21 w22 w23 fin1 fin2"}
+SCORE = {'v': 'qx3 qx1 mask3 qx2 mask1 own3 qg own1 mask2 flag3 flag1 own2 g22:128:352 sum3 sum1', 's': 'row3 row1 r27:128:432 r26:128:416 row2 r25:128:400', 't': 'sc3 sc1 sc2'}
+ORDER = {'v': 'g22:0:128 flag2 g21 u22 sum2 g20 u21 tie g19 u20 g18 u19 g17 u18 q0 base26 g16 u17 g15 set26 u16 q2 off26 g14 u15 q1 u14 q3 g12 base23 base14 g11 u12 set14 u11 q4 off14 q5 q6 put:224:352 base0 base11 base13 put:352:384 set0 put:384:448 off0 ctlp put:0:224', 's': 'k1 r27:0:128 r26:0:128 r25:0:128 s27 s26 s25 r24 r23 r13 s24 s23 r10 s13 r9 r8 s10 r7 s9 r6 s8 r5 s7 r4 s6 r3 s5 r2 s4 r1 s3 s2 s1 ctl thr ctl15 col3', 't': 'e0 h0 l0 h2 h1 h3 l1 l2 l3 l4 l5 l6'}
+START = {'v': 'G:320:448@-1 G:0:128@-1 W:224:448@-1 W:0:224@-1 O:224:448@-1 O:0:224@-1 K:320:448@0 W:224:448@0 K:224:320@0 O:224:448@0 W:0:224@0 K:96:224@0 O:0:224@0', 's': 'G:224:320@-1 G:128:224@-1 S:320:448@0 S:96:320@0 S:0:96@0 G:224:448@0 G:0:224@0'}
+LEVEL = {'v': 'W:224:448@0 K:0:96@-1 O:224:448@0 W:0:224@0 K:320:448@0 O:0:224@0 K:96:320@0', 's': 'G:224:448@0 G:0:224@0 S:320:448@0 S:96:320@0 S:0:96@0'}
+ENDS = {'v': 'W:224:448@7 K:0:96@6 O:224:448@7 K:320:448@7 K:96:320@7 K:0:96@7 W:0:224@7 K:320:448@8 O:0:224@7 K:224:320@8 K:0:224@8 U:224:448 U:0:224 H:224:448 H:0:224 C:0:448 offm mw qe0 P:224:448 ctlm qe1 W:0:448 qe2 O:0:448 qe3 pute qv W:0:128e W:128:448e O:0:128e O:128:448e', 's': 'G:224:448@7 S:320:448@7 S:96:320@7 S:0:96@7 G:0:224@7 S:320:448@8 S:96:320@8 S:0:96@8 p0 p1 P:0:224 p2 p3'}
+NEXT = {'v': 'b0 b1 z10 qb z11 z31 qz1 z30 m13 m32 qz3 a11 a10 a13 a12 a31 a32 a30 a33 c3 c2 qz2 x10 qx3 qx1 y2 mask3 qx2 mask1 own3 own1 mask2 flag3 flag1 own2 g22:128:352 sum1 sum3', 's': 'b3 b2 z13 z12 z33 z32 m11 m10 m30 m12 m31 m33 x13 x11 x31 c1 c0 x30 x32 x33 x12 y0 y3 y1 row3 row1 r26:128:416 r25:128:400 row2 r27:128:432', 't': 'w11 w10 w13 w12 w31 w32 w30 w33 d3 d1 d2 d0 f1 f2 f3 f0 w20 w23 w22 w21 sc3 sc1 sc2'}
+LAST = {'v': 'b1 b0 z10 qb z11 z31 qz1 z30 m32 m13 qz3 a13 a12 a10 a11 a33 a32 m30 c3 c2 a31 a30 qz2 x31 qx1 qx3 y2 y3 qx2', 's': 'elf b3 b2 z12 z13 z32 m12 z33 m10 m31 m11 m33 x12 x13 x11 x10 c0 c1 x33 x32 x30 y1 y0 ysb1 ysb2 sty1 sty2', 't': 'w13 w12 w11 w10 w33 w32 w31 d3 d0 d2 d1 w30 f0 f3 f2 f1 w22 w21 w23 w20 fin1 fin2'}
+OF_NEXT = ("qx", "sc", "fin", "mask", "own", "flag", "sum", "row", "r", "g")
+
+
+def orders():
+    seq = {q: [] for q in "vst"}
+
+    def add(lists, t, k=0, ahead=()):
+        for q, names in lists.items():
+            for n in names.split():
+                n, _, at = n.partition("@")
+                seq[q].append((n, t + (n.split(":")[0].rstrip("0123456789") in ahead)) + ((k + int(at),) if at else ()))
+    add(SCORE, 0)
+    for t in range(R):
+        add(ORDER, t)
+        add(START, t)
+        for k in range(1, 7):
+            add(LEVEL, t, k)
+        add(ENDS, t)
+        add(NEXT if t < R - 1 else LAST, t, 0, OF_NEXT)
+    return seq
+
 
 SCRATCH = {}
 
@@ -38,8 +79,8 @@ def _buf(dtype, n, *names):
 
 _buf("bfloat16", 512, "ub", "vb", "neg", "c64", "go", "gs", "bt0", "bt1")
 _buf("bfloat16", 4 * 512, "eb")
-_buf("bfloat16", C, "rr", "side", "drop", "gate", "sg3", "sq", "ctl", "fh", "orow", "crow", "prow", "erow", "jp", "j0", "j1",
-     "eqs", "rel0", "rel1", "rel2", "rel3")
+_buf("bfloat16", C, "rr", "side", "drop", "gate", "sg3", "sq", "ctl", "fh", "orow", "crow", "prow", "erow", "jp", "j0", "j1", "eqs")
+_buf("bfloat16", RELS * C, "rel")
 _buf("float16", C, "hrow", "ctlp")
 _buf("bfloat16", 224 * KB, "zs")
 _buf("bfloat16", 4 * C, "z64", "x0", "x1", "x2", "zt0", "zt1", "xp")
@@ -62,69 +103,65 @@ _buf("float32", KB, "k0", "k1", "cnt", "tie", "mw")
 _buf("float32", 8, "col")
 _buf("float32", 512, "pp0", "pp1", "pp2", "pp3", "pr0", "pr1", "pr2", "pr3")
 
-LOADS = ["ldu", "ldx1", "ldx2", "ldw", "ldv"]
+LOADS = ["ldu", "ldx1", "ldx2", "ldx3", "ldw", "ldv"]
+FETCH = [3, 1, 2]
 SEMAPHORES = ["cv", "cs", "ct", "cg", "stored", "sent", "rxh0", "rxh1", "rxl0", "rxl1", "rxb0", "rxb1"] + LOADS
+HOOK = []
 
 
 def rank_program(g, core, T, topo):
     rank = T.rank_of(core)
     if rank is None:
         return
-    queue = {"v": g.vector, "s": g.scalar, "t": g.tensor, "g": g, "y": g.sync}
-    count = {}
-    know = {q: {} for q in queue}
+    seq = orders()
+    who = {n: q for q in seq for n in seq[q]}
+    calls = []
     writer, reader = {}, {}
+    fixed = {}
 
-    def before(q, reads, writes):
-        need = []
+    def note(q, name, reads, writes, issue, sem, inc, joins=False):
+        need, ahead = set(), set()
         for k in reads:
-            need += writer.get(k, [])
+            need.update(writer.get(k, []))
             if k[:2] in ("pp", "pr"):
-                need += [tok for tok in reader.get(k, []) if tok[0] != q]
+                need.update(i for i in reader.get(k, []) if calls[i][0] != q)
         for k in writes:
-            need += writer.get(k, []) + reader.get(k, [])
-        for _, sem, val, seen in sorted(need, key=lambda tok: -tok[2]):
-            if know[q].get(sem, 0) < val:
-                queue[q].wait_ge(T.sem[sem], val)
-                for s, n in list(seen.items()) + [(sem, val)]:
-                    know[q][s] = max(know[q].get(s, 0), n)
-
-    def after(q, sem, inc, reads, writes):
-        count[sem] = count.get(sem, 0) + inc
-        tok = (q, sem, count[sem], dict(know[q]))
+            (ahead if joins else need).update(writer.get(k, []))
+            need.update(reader.get(k, []))
+        calls.append((q, name, need, ahead, issue, sem, inc))
         for k in reads:
-            reader.setdefault(k, []).append(tok)
+            reader.setdefault(k, []).append(len(calls) - 1)
         for k in writes:
-            writer[k], reader[k] = [tok], []
+            writer[k], reader[k] = [len(calls) - 1], []
+        return len(calls) - 1
 
-    def do(q, reads, writes, make):
-        before(q, reads, writes)
-        make(queue[q]).then_inc(T.sem["c" + q], 1)
-        after(q, "c" + q, 1, reads, writes)
+    def do(q, name, reads, writes, make, joins=False):
+        note(q, name, reads, writes, lambda e: make(e).then_inc(T.sem["c" + q], 1), "c" + q, 1, joins)
 
-    def load(q, sem, total, key, out, in_):
-        queue[q].dma_start(out, in_).then_inc(T.sem[sem], 16)
-        count[sem] = count.get(sem, 0) + 16
-        writer.setdefault(key, []).append((q, sem, total, {}))
+    def load(q, sem, total, key, out, in_, after=()):
+        held = writer.get(key, [])
+        i = note(q, None, list(after), [], lambda e: e.dma_start(out, in_).then_inc(T.sem[sem], 16), sem, 16)
+        writer[key], fixed[i] = held + [i], (sem, total)
 
-    def store(q, reads, out, in_):
-        before(q, reads, [])
-        queue[q].dma_start(out, in_).then_inc(T.sem["stored"], 16)
-        after(q, "stored", 16, reads, [])
+    def store(q, name, reads, out, in_):
+        note(q, name, reads, [], lambda e: e.dma_start(out, in_).then_inc(T.sem["stored"], 16), "stored", 16)
+
+    landed = {}
 
     def send(t, pairs, sem):
         dst = T.cores[rank ^ STEP[t]]
         rid, pid, _ = topo.addr(dst)
         eng = topo.engines(core, dst)[:ENGINES]
         mask = sum(1 << e for e in eng)
-        total = count.get(sem, 0) + len(pairs) * len(eng)
+        landed[sem] = landed.get(sem, 0) + len(pairs) * len(eng)
         for land, there, here, view, keys in pairs:
-            before("g", keys, [])
-            g.remote_dma(view(there), view(here), T.sem[sem], T.sem["sent"], pid, rid, mask)
-            count["sent"] = count.get("sent", 0) + len(eng)
+            i = note("g", None, keys, [], lambda e, a=view(there), b=view(here): e.remote_dma(a, b, T.sem[sem], T.sem["sent"], pid, rid, mask),
+                     "sent", len(eng))
+            fixed[i] = (sem, landed[sem])
             for k in land:
-                writer[k] = [("far", sem, total, {})]
-        count[sem] = total
+                writer[k] = [i]
+            for k in keys:
+                reader[k].remove(i)
 
     def ts(out, in0, s1, op0, s2=None, op1=None):
         if op1 is None:
@@ -143,6 +180,9 @@ def rank_program(g, core, T, topo):
     def move(q, out, in_):
         return act(out, in_) if q == "s" else cp(out, in_)
 
+    def times(q, out, in_, x):
+        return act(out, in_, scale=x) if q == "s" else ts(out, in_, x, A.mult)
+
     def fill(out, x):
         return lambda e: e.memset(out, x)
 
@@ -152,38 +192,58 @@ def rank_program(g, core, T, topo):
     def scan(out, d0, d1, init, op0, op1):
         return lambda e: e.tensor_tensor_scan(out, d0, d1, init, op0, op1)
 
+    def matmul(name, out, key, lhs, ls, lkey, rhs, rs, rkey, start=True, stop=True):
+        do("t", name, lkey + rkey, [key], lambda e: e.matmul_mx(out, lhs, ls, rhs, rs, start, stop), not start)
+
     def back(a, b):
         return slice(b - 1, a - 1 if a else None, -1)
 
     def span(name, a=0, b=C):
         return ["%s:%d" % (name, i) for i in range(a // 32, (b + 31) // 32)]
 
+    def pieces(what, t, k=None, tail=""):
+        out = []
+        for q in "vs":
+            for n in seq[q]:
+                w = n[0].split(":")
+                if len(w) == 3 and w[0] == what and n[1:] == ((t,) if k is None else (t, k)) and w[2].lstrip("0123456789") == tail:
+                    out.append((n, q, int(w[1]), int(w[2].rstrip(tail))))
+        return out
+
     def iota(name, pattern, base, cm, cols=slice(None), key=None):
         kw = {} if SCRATCH[name][2] == "int32" else {"allow_small_or_imprecise_dtypes": True}
-        do("g", [], [key or name], lambda e: e.iota(T[name][:, cols], pattern, base, cm, **kw))
+        do("g", None, [], [key or name], lambda e: e.iota(T[name][:, cols], pattern, base, cm, **kw))
 
     def flags(k, a, b):
         z = 4 * AT[(KB - k) // 4] + (KB - k) % 4
         return T.fl[:, z + 4 * a:z + 4 * b - 3:4]
 
+    def parts(name):
+        return ["%s:%d" % (name, h) for h in PART]
+
+    def rows(i):
+        return [n for k in range(KB - 4 * i - 3, KB - 4 * i + 1) for n in parts("fl%d" % k)]
+
+    by_s = [k for k in range(KB) if ("s%d" % k, 0) in who]
+
     load("s", "ldu", 16, "ub", T.ub[:], T.u[:])
-    load("y", "ldx1", 16, "x0:1", T.x0[:, 4 * S:4 * C], T.x[:, 4 * S:4 * C])
-    load("y", "ldx2", 16, "x0:2", T.x0[:, 0:4 * S], T.x[:, 0:4 * S])
-    before("y", ["x0:1", "x0:2"], [])
-    load("y", "ldw", 32, "w", T.qw[:].bitcast(dt.uint8), T.wc[:])
+    for h in FETCH:
+        a, b = PART[h]
+        load("y", "ldx%d" % h, 16, "x0:%d" % h, T.x0[:, 4 * a:4 * b], T.x[:, 4 * a:4 * b])
+    load("y", "ldw", 32, "w", T.qw[:].bitcast(dt.uint8), T.wc[:], parts("x0"))
     load("y", "ldw", 32, "w", T.sw[:], T.ws[:])
     load("y", "ldv", 16, "vb", T.vb[:], T.v[:])
 
     iota("ku", [[16, 8]], 0, 0)
     iota("pc", [[0, 1]], 0, 1, slice(0, 1))
     iota("rr", [[0, KB], [1, 16]], 0, 0)
-    do("v", [], ["neg"], fill(T.neg[:], -1.0))
-    do("g", ["neg"], ["go"], lambda e: e.affine_select(T.go[:], T.neg[:], [[-16, 8], [0, 64]], A.is_ge, 0.0, 0, 1))
-    do("g", ["go"], ["gs"], lambda e: e.affine_select(T.gs[:], T.go[:], [[16, 8], [0, 64]], A.is_ge, 0.0, 15, -1))
+    do("v", None, [], ["neg"], fill(T.neg[:], -1.0))
+    do("g", None, ["neg"], ["go"], lambda e: e.affine_select(T.go[:], T.neg[:], [[-16, 8], [0, 64]], A.is_ge, 0.0, 0, 1))
+    do("g", None, ["go"], ["gs"], lambda e: e.affine_select(T.gs[:], T.go[:], [[16, 8], [0, 64]], A.is_ge, 0.0, 15, -1))
     left, k0_keys = [], []
     for k in range(KB):
-        n = C - 16 * (k + 1) - 16 * sum(i > k for i in BY_S) - LIFT - DEEP
-        left.append(n + (16 * k if k in BY_S else HALF if k else 0))
+        n = C - 16 * (k + 1) - 16 * sum(i > k for i in by_s) - LIFT - DEEP
+        left.append(n + (16 * k if k in by_s else HALF if k else 0))
     k = 0
     while k < KB:
         step, n = (left[k + 1] - left[k] if k < KB - 1 else 0), 1
@@ -192,406 +252,272 @@ def rank_program(g, core, T, topo):
         k0_keys.append("k0:%d" % k)
         iota("k0", [[step, n]], left[k], 0, slice(k, k + n), k0_keys[-1])
         k += n
-    do("v", ["ku"], ["offu"], cp(T.offu[:], T.ku[:]))
-    do("v", ["pc"], ["pq"], ts(T.pc[:, 1:2], T.pc[:, 0:1], 15, A.bitwise_and))
-    do("v", [], ["cnt0"], fill(T.cnt[:, 0:1], 0.0))
-    do("v", [], ["c64"], fill(T.c64[:], 64.0))
+    do("v", None, ["ku"], ["offu"], cp(T.offu[:], T.ku[:]))
+    do("v", None, ["pc"], ["pq"], ts(T.pc[:, 1:2], T.pc[:, 0:1], 15, A.bitwise_and))
+    do("v", None, [], ["cnt0"], fill(T.cnt[:, 0:1], 0.0))
+    do("v", None, [], ["c64"], fill(T.c64[:], 64.0))
     own_q = T.col[:, 0:1]
-    do("v", ["pq"], ["q"], cp(own_q, T.pc[:, 1:2]))
-    do("v", ["rr", "q"], ["side"], ts(T.side[:], T.rr[:], own_q, A.subtract, BIG, A.mult))
-    do("v", ["ub"], ["qu"], quant(T.qu[:], T.su[:], T.ub[:]))
-    do("v", ["rr", "q"], ["drop"], ts(T.drop[:], T.rr[:], own_q, A.is_equal, -1024 * BIG, A.mult))
-    do("v", ["qu", "offu"], ["qur"], cp(T.qur[:, 0:128].bitcast(dt.uint32), T.qu[:, 0:128].bitcast(dt.uint32).indirect(T.offu[:, 0:8])))
-    do("v", ["qu", "offu"], ["sur"], cp(T.sur[:, 0:128], T.su[:, 0:128].indirect(T.offu[:, 0:8])))
-    do("v", ["rr", "q"], ["gate"], ts(T.gate[:], T.rr[:], own_q, A.not_equal))
+    do("v", None, ["pq"], ["q"], cp(own_q, T.pc[:, 1:2]))
+    do("v", None, ["rr", "q"], ["side"], ts(T.side[:], T.rr[:], own_q, A.subtract, BIG, A.mult))
+    do("v", None, ["ub"], ["qu"], quant(T.qu[:], T.su[:], T.ub[:]))
+    do("v", None, ["rr", "q"], ["drop"], ts(T.drop[:], T.rr[:], own_q, A.is_equal, -1024 * BIG, A.mult))
+    do("v", None, ["qu", "offu"], ["qur"], cp(T.qur[:, 0:128].bitcast(dt.uint32), T.qu[:, 0:128].bitcast(dt.uint32).indirect(T.offu[:, 0:8])))
+    do("v", None, ["qu", "offu"], ["sur"], cp(T.sur[:, 0:128], T.su[:, 0:128].indirect(T.offu[:, 0:8])))
+    do("v", None, ["rr", "q"], ["gate"], ts(T.gate[:], T.rr[:], own_q, A.not_equal))
     for i in range(NQ):
         n = WIDE[i] - (C - 64 * i - 48)
-        do("s", ["neg"], ["fl%d" % k for k in range(KB - 4 * i - 3, KB - 4 * i + 1)] + (["fld"] if i == 0 else []),
-           act(T.fl[:, 4 * (AT[i + 1] - n):4 * AT[i + 1]], T.neg[:, 0:4 * n], scale=0.0))
-    do("s", ["side"], ["sg3"], act(T.sg3[:], T.side[:], F.Sign))
-    do("s", ["sg3"], ["sq"], act(T.sq[:], T.sg3[:], F.Square, bias=-0.25))
-    do("s", ["side"], ["col1"], act(T.col[:, 1:2], T.side[:, 15:16], F.Identity, scale=1 / BIG, bias=576.0))
-    do("s", ["sq"], ["ctlb"], act(T.ctlb[:], T.sq[:], F.Identity, scale=-1024.0, bias=576.0))
-    do("s", ["sq", "col1"], ["col2"], act(T.col[:, 2:3], T.sq[:, 15:16], F.Identity, scale=-1024.0, bias=T.col[:, 1:2]))
+        do("s", None, ["neg"], rows(i), act(T.fl[:, 4 * (AT[i + 1] - n):4 * AT[i + 1]], T.neg[:, 0:4 * n], scale=0.0))
+    do("s", None, ["side"], ["sg3"], act(T.sg3[:], T.side[:], F.Sign))
+    do("s", None, ["side"], ["col1"], act(T.col[:, 1:2], T.side[:, 15:16], F.Identity, scale=1 / BIG, bias=576.0))
+    do("s", None, ["sg3"], ["sq"], act(T.sq[:], T.sg3[:], F.Square, bias=-0.25))
+    do("s", None, ["sq"], ["ctlb"], act(T.ctlb[:], T.sq[:], F.Identity, scale=-1024.0, bias=576.0))
+    do("s", None, ["sq", "col1"], ["col2"], act(T.col[:, 2:3], T.sq[:, 15:16], F.Identity, scale=-1024.0, bias=T.col[:, 1:2]))
     iota("fh", [[1, C]], -HALF, 0)
     for b in range(4):
-        do("g", ["c64"], ["eb%d" % b], lambda e: e.affine_select(
+        do("g", None, ["c64"], ["eb%d" % b], lambda e, b=b: e.affine_select(
             T.eb[:, 512 * b:512 * b + 512], T.c64[:], [[-1, 512]], A.is_equal, 0.0, b, 4))
-
-    def quant_const(b):
-        do("v", ["eb%d" % b], ["qe%d" % b], quant(T.qe[:, S * b:S * b + S], T.se[:, S * b:S * b + S], T.eb[:, 512 * b:512 * b + 512]))
-
-    later = [lambda: do("v", ["sq"], ["ctl"], ts(T.ctl[:], T.sq[:], -1024.0, A.mult, 576.0, A.add)),
-             lambda: do("v", ["sq"], ["ctlp"], ts(T.ctlp[:], T.sq[:], -2.0, A.mult, 1.125, A.add)),
-             lambda: do("v", ["sq", "ctl"], ["ctl"], ts(T.ctl[:, 15:C:16], T.sq[:, 15:C:16], -1024.0, A.mult, 576.0 - 2 * LIFT, A.add))]
-    later += [lambda b=b: quant_const(b) for b in range(4)] + [lambda: do("v", ["vb"], ["qv"], quant(T.qv[:], T.sv[:], T.vb[:]))]
-
-    def spare():
-        if later:
-            later.pop(0)()
-
-    def matmul(out, key, lhs, ls, lkey, rhs, rs, rkey, start=True, stop=True):
-        do("t", lkey + rkey, [key], lambda e: e.matmul_mx(out, lhs, ls, rhs, rs, start, stop))
+        do("v", ("qe%d" % b, 0), ["eb%d" % b], ["qe%d" % b], quant(T.qe[:, S * b:S * b + S], T.se[:, S * b:S * b + S], T.eb[:, 512 * b:512 * b + 512]))
+    do("v", ("qg", 0), ["gs"], ["qg"], quant(T.qg[:], T.sg[:], T.gs[:]))
+    do("v", ("qv", 0), ["vb"], ["qv"], quant(T.qv[:], T.sv[:], T.vb[:]))
+    do("s", ("k1", 0), ["col2"] + k0_keys, ["k1"], act(T.k1[:], T.k0[:], F.Identity, bias=T.col[:, 2:3]))
+    do("s", ("ctl", 0), ["sq"], ["ctl"], act(T.ctl[:], T.sq[:], F.Identity, scale=-1024.0, bias=576.0))
+    do("v", ("ctlp", 0), ["sq"], ["ctlp"], ts(T.ctlp[:], T.sq[:], -2.0, A.mult, 1.125, A.add))
+    do("s", ("ctl15", 0), ["sq"], ["ctl"], act(T.ctl[:, 15:C:16], T.sq[:, 15:C:16], F.Identity, scale=-1024.0, bias=576.0 - 2 * LIFT))
+    do("s", ("thr", 0), ["fh"], ["thr"], act(T.thr[:], T.fh[:], F.Identity, bias=-0.5))
+    do("s", ("col3", 0), ["sq"], ["col3"], act(T.col[:, 3:4], T.sq[:, 15:16], F.Identity, scale=2.0, bias=float(MAGIC + LIFT + HALF + 1)))
 
     def state_keys(t, h):
         if t == 0:
             return ["x0:%d" % h]
-        return ["x%d:%d:%d" % (t, c, i) for c in ((1, 3) if h == 1 else (2,)) for i in range(4)]
+        return ["x%d:%d:%d" % (t, h, i) for i in range(4)]
 
     def quant_state(t, h):
-        a, b = H1 if h == 1 else H2
-        do("v", state_keys(t, h), ["qx%d:%d" % (t, h)], quant(T["qx%d" % t][:, a:b], T["sx%d" % t][:, a:b], T["x%d" % t][:, 4 * a:4 * b]))
+        a, b = PART[h]
+        do("v", ("qx%d" % h, t), state_keys(t, h), ["qx%d:%d" % (t, h)], quant(T["qx%d" % t][:, a:b], T["sx%d" % t][:, a:b], T["x%d" % t][:, 4 * a:4 * b]))
 
     def score(t, h):
-        a, b = H1 if h == 1 else H2
+        a, b = PART[h]
         qx, sx = T["qx%d" % t], T["sx%d" % t]
-        for p in ("pp0", "pp1") if h == 1 else ("pp2", "pp3"):
-            matmul(T[p][:, 0:b - a], p, T.qur[:], T.sur[:], ["qur", "sur"], qx[:, a:b], sx[:, a:b], ["qx%d:%d" % (t, h)])
-
-    def take(step, h):
-        a, b = H1 if h == 1 else H2
-        p0, p1 = ("pp0", "pp1") if h == 1 else ("pp2", "pp3")
-        if step == "row":
-            do("s", [p1], ["srow:%d" % h], act(T.srow[:, a:b], T[p1][:, 0:b - a]))
-        elif step == "mask":
-            do("v", [p0, "side"], ["mrow:%d" % h], tt(T.mrow[:, a:b], T[p0][:, 0:b - a], T.side[:, a:b], A.add))
-        elif step == "own":
-            do("v", ["mrow:%d" % h, "drop"], ["arow:%d" % h], scan(T.arow[:, back(a, b)], T.drop[:, back(a, b)], T.mrow[:, back(a, b)], 0.0, A.add, A.max))
-        elif step == "flag":
-            do("v", ["arow:%d" % h, p0, "fld"], ["fld:%d" % h], tt(flags(KB, a, b), T[p0][:, 0:b - a], T.arow[:, a:b], A.is_ge))
-        else:
-            z = 4 * b - 4
-            d = T.fl[:, slice(z, 4 * a - 1 if a else None, -4)]
-            do("v", ["fld:%d" % h, "gate"], ["eqs:%d" % h], scan(T.eqs[:, back(a, b)], T.gate[:, back(a, b)], d, 0.0, A.mult, A.add))
-
-    def add_base(a, b):
-        while a < b:
-            c = a + 1
-            while c < b and (c in BY_S) == (a in BY_S or a == 0):
-                c += 1
-            if a in BY_S or a == 0:
-                keys, src = ["cnt%d" % k for k in range(a, c)], T.cnt[:, a:c]
-            else:
-                keys, src = ["zs:%d" % k for k in range(a, c)], T.zs[:, 224 * a + 223:224 * c:224]
-            do("v", keys + ["tie", "ctlb"], ["ctlb:%d" % k for k in range(a, c)], tt(T.ctlb[:, 16 * a + 15:16 * c:16], src, T.tie[:, a:c], A.add))
-            a = c
-
-    def settle(bank, a, b):
-        do("v", [bank] + ["ctlb:%d" % k for k in range(a, b)], ["hcol:%d" % a],
-           scan(T.hcol[:, 16 * a:16 * b], T[bank][:, 16 * a:16 * b], T.ctlb[:, 16 * a:16 * b], -float(DEEP), A.max, A.add))
-
-    def hand(t, a, b):
-        key = "own%d:%d" % (t, a)
-        do("v", ["hcol:%d" % a], [key], ts(T["own%d" % t][:, a:b], T.hcol[:, 16 * a + 15:16 * b:16], float(DEEP), A.add))
-        h = "h" if a >= HIGH else "l"
-        land = span("land%d" % t, *((16 * HIGH, C) if a >= HIGH else (0, 16 * HIGH)))
-        send(t, [(land, "land%d" % t, "own%d" % t, lambda n: T[n][:, a:b], [key])], "rx%s%d" % (h, t))
-
-    def put(t, a, b, keys):
-        do("v", keys + ["fh"], ["orow"], cp(T.orow[:, 0:C].indirect(T["own%d" % t][:, a:b]), T.fh[:, 16 * a:16 * b]))
+        quant_state(t, h)
+        p0, p1 = BANKS[h]
+        for p in (p0, p1):
+            matmul(("sc%d" % h, t), T[p][:, 0:b - a], p, T.qur[:], T.sur[:], ["qur", "sur"], qx[:, a:b], sx[:, a:b], ["qx%d:%d" % (t, h)])
+        do("s", ("row%d" % h, t), [p1], ["srow:%d" % h], act(T.srow[:, a:b], T[p1][:, 0:b - a]))
+        do("v", ("mask%d" % h, t), [p0, "side"], ["mrow:%d" % h], tt(T.mrow[:, a:b], T[p0][:, 0:b - a], T.side[:, a:b], A.add))
+        do("v", ("own%d" % h, t), ["mrow:%d" % h, "drop"], ["arow:%d" % h],
+           scan(T.arow[:, back(a, b)], T.drop[:, back(a, b)], T.mrow[:, back(a, b)], 0.0, A.add, A.max))
+        do("v", ("flag%d" % h, t), ["arow:%d" % h, p0], ["fl%d:%d" % (KB, h)], tt(flags(KB, a, b), T[p0][:, 0:b - a], T.arow[:, a:b], A.is_ge))
+        d = T.fl[:, slice(4 * b - 4, 4 * a - 1 if a else None, -4)]
+        do("v", ("sum%d" % h, t), ["fl%d:%d" % (KB, h), "gate"], ["eqs:%d" % h], scan(T.eqs[:, back(a, b)], T.gate[:, back(a, b)], d, 0.0, A.mult, A.add))
 
     def places(t):
-        row = ["srow:1", "srow:2"]
-        pend, done = [], []
+        own, land = "own%d" % t, "land%d" % t
         top = FIRST if t == 0 else KB
 
-        def own(k):
-            return T.arow[:, 16 * k:16 * k + 1], "arow:%d" % (1 if 16 * k >= S else 2)
+        def compare(k, what):
+            cut = [(n, a, b) for n, q, a, b in pieces(what + str(k), t)] or [((what + str(k), t), 0, 16 * k)]
+            for n, a, b in cut:
+                hs = [h for h in PART if a < PART[h][1] and PART[h][0] < b]
+                yield n, a, b, hs, ["srow:%d" % h for h in hs] + ["arow:%d" % h for h in PART if PART[h][0] <= 16 * k < PART[h][1]]
 
-        def sign(k):
-            rel = "rel%d" % (BY_S.index(k) % 4)
-            do("s", [rel], ["fl%d" % k, "cnt%d" % k], act(flags(k, 0, 16 * k), T[rel][:, 0:16 * k], F.Sign, scale=-1.0, accum_out=T.cnt[:, k:k + 1]))
-
-        for k in BY_S:
-            rel = "rel%d" % (BY_S.index(k) % 4)
-            do("s", row + [own(k)[1]], [rel], act(T[rel][:, 0:16 * k], T.srow[:, 0:16 * k], F.Relu, bias=own(k)[0], scale=-1.0))
-            pend.append(k)
-            if len(pend) > 1:
-                sign(pend.pop(0))
-        sign(pend.pop(0))
-
-        def add_up(k):
-            z = 224 * k + 224
-            do("v", ["fl%d" % k], ["zs:%d" % k], scan(T.zs[:, z - 8 * k:z], flags(k, 0, 8 * k), flags(k, 8 * k, 16 * k), -float(HALF), A.add, A.add))
-
-        def sum_up(i):
+        turn = [int(n[0][1:]) for n in seq["s"] if n[1] == t and n[0][0] == "s" and n[0][1:].isdigit()]
+        for at, k in enumerate(turn):
+            z, rel = C * (at % RELS), "rel%d:" % (at % RELS)
+            for n, a, b, hs, keys in compare(k, "r"):
+                do("s", n, keys, [rel + str(h) for h in hs], act(T.rel[:, z + a:z + b], T.srow[:, a:b], F.Relu, bias=T.arow[:, 16 * k:16 * k + 1], scale=-1.0))
+            do("s", ("s%d" % k, t), parts(rel[:-1]), parts("fl%d" % k) + ["cnt%d" % k],
+               act(flags(k, 0, 16 * k), T.rel[:, z:z + 16 * k], F.Sign, scale=-1.0, accum_out=T.cnt[:, k:k + 1]))
+        for k in range(1, KB):
+            if k not in by_s:
+                for n, a, b, hs, keys in compare(k, "g"):
+                    do("v", n, keys, ["fl%d:%d" % (k, h) for h in hs], ts(flags(k, a, b), T.srow[:, a:b], T.arow[:, 16 * k:16 * k + 1], A.is_ge))
+                z = 224 * k + 224
+                do("v", ("u%d" % k, t), parts("fl%d" % k), ["zs:%d" % k],
+                   scan(T.zs[:, z - 8 * k:z], flags(k, 0, 8 * k), flags(k, 8 * k, 16 * k), -float(HALF), A.add, A.add))
+        do("v", ("tie", t), parts("eqs") + ["k1"], ["tie"], tt(T.tie[:], T.eqs[:, 0:C:16], T.k1[:], A.add))
+        for i in range(NQ):
             a, b = AT[i], AT[i + 1]
-            keys = ["fl%d" % k for k in range(KB - 4 * i - 3, KB - 4 * i + 1)] + (["fld:1", "fld:2"] if i == 0 else [])
-            do("v", keys, ["qf%d" % i], quant(T.qf[:, a:b], T.sf[:, a:b], T.fl[:, 4 * a:4 * b]))
+            do("v", ("q%d" % i, t), rows(i), ["qf%d" % i], quant(T.qf[:, a:b], T.sf[:, a:b], T.fl[:, 4 * a:4 * b]))
+        for what, bank, width in (("e", "pp3", C), ("h", "pp1", C), ("l", "pp2", 16 * HIGH)):
+            tiles = [int(n[0][1:]) for n in seq["t"] if n[1] == t and n[0][0] == what and n[0][1:].isdigit()]
+            for i in tiles if what != "e" or t == 0 else []:
+                a, n = AT[i], min(width, WIDE[i])
+                matmul((what + str(i), t), T[bank][:, 0:n], bank, T.qg[:], T.sg[:], ["qg"], T.qf[:, a:a + n], T.sf[:, a:a + n], ["qf%d" % i],
+                       i == tiles[0], i == tiles[-1])
+        for bank, a, b in (("pp3", top, KB), ("pp1", HIGH, top), ("pp2", 0, HIGH)):
+            c = a
+            while c < b:
+                d = c + 1
+                while d < b and (d in by_s) == (c in by_s or c == 0):
+                    d += 1
+                if c in by_s or c == 0:
+                    keys, src = ["cnt%d" % k for k in range(c, d)], T.cnt[:, c:d]
+                else:
+                    keys, src = ["zs:%d" % k for k in range(c, d)], T.zs[:, 224 * c + 223:224 * d:224]
+                do("v", ("base%d" % c, t), keys + ["tie", "ctlb"], ["ctlb:%d" % k for k in range(c, d)],
+                   tt(T.ctlb[:, 16 * c + 15:16 * d:16], src, T.tie[:, c:d], A.add))
+                c = d
+            if a < b:
+                do("v", ("set%d" % a, t), [bank] + ["ctlb:%d" % k for k in range(a, b)], ["hcol:%d" % a],
+                   scan(T.hcol[:, 16 * a:16 * b], T[bank][:, 16 * a:16 * b], T.ctlb[:, 16 * a:16 * b], -float(DEEP), A.max, A.add))
+                do("v", ("off%d" % a, t), ["hcol:%d" % a], span(own, 16 * a, 16 * b), ts(T[own][:, a:b], T.hcol[:, 16 * a + 15:16 * b:16], float(DEEP), A.add))
+                there = span(land, 16 * HIGH, C) if a else span(land, 0, 16 * HIGH)
+                send(t, [(there, land, own, lambda n, a=a, b=b: T[n][:, a:b], span(own, 16 * a, 16 * b))], "rx%s%d" % ("h" if a else "l", t))
+        for n, q, a, b in pieces("put", t):
+            do("v", n, span(own, a, b) + ["fh"], ["orow"], cp(T.orow[:, 0:C].indirect(T[own][:, a // 16:b // 16]), T.fh[:, a:b]))
 
-            def add(bank, n, start, stop):
-                matmul(T[bank][:, 0:n], bank, T.qg[:], T.sg[:], ["qg"], T.qf[:, a:a + n], T.sf[:, a:a + n], ["qf%d" % i], start, stop)
-            high = [j for j in done if j < NH]
-            if i < NH:
-                if t == 0 and i == 0:
-                    add("pp3", C, True, True)
-                add("pp1", b - a, not high, len(high) == NH - 1)
-            add("pp2", min(16 * HIGH, b - a), not done, len(done) == NQ - 1)
-            done.append(i)
+    def wrap(n, row, keys, a, b, ctl="ctl"):
+        do("v", n, keys + [ctl], span("hrow", a, b), scan(T.hrow[:, a:b], row[:, a:b], T[ctl][:, a:b], -1024.0, A.max, A.add))
 
-        prev = None
-        for step in PLAN:
-            if step == "c":
-                spare()
-            elif step == "tie":
-                if t == 0:
-                    do("v", ["col2"] + k0_keys, ["k1"], ts(T.k1[:], T.k0[:], T.col[:, 2:3], A.add))
-                take("sum", 2)
-            elif step == "tie2":
-                do("v", ["eqs:1", "eqs:2", "k1"], ["tie"], tt(T.tie[:], T.eqs[:, 0:C:16], T.k1[:], A.add))
-            elif step == "early":
-                if t == 0:
-                    add_base(FIRST, KB)
-            elif step == "early2":
-                if t == 0:
-                    settle("pp3", FIRST, KB)
-            elif step == "early3":
-                if t == 0:
-                    hand(t, FIRST, KB)
-            elif step == "baseh":
-                add_base(HIGH, top)
-            elif step == "high":
-                settle("pp1", HIGH, top)
-            elif step == "offh":
-                hand(t, HIGH, top)
-            elif step == "puth":
-                put(t, HIGH, KB, ["own%d:%d" % (t, k) for k in {HIGH, top} if k < KB])
-            elif step == "basel":
-                add_base(0, HIGH)
-            elif step == "low":
-                settle("pp2", 0, HIGH)
-            elif step == "offl":
-                hand(t, 0, HIGH)
-            elif step == "putl":
-                put(t, 0, HIGH, ["own%d:0" % t])
-            elif step == "flag":
-                take("flag", 2)
-            elif step == "sum":
-                add_up(prev)
-                prev = None
-            elif step in ["q%d" % i for i in range(NQ)]:
-                sum_up(int(step[1]))
-            else:
-                k = step
-                do("v", row + [own(k)[1]], ["fl%d" % k], ts(flags(k, 0, 16 * k), T.srow[:, 0:16 * k], own(k)[0], A.is_ge))
-                if prev:
-                    add_up(prev)
-                prev = k
-
-    def wrap(row, keys, a, b, ctl="ctl"):
-        do("v", keys + [ctl], span("hrow", a, b), scan(T.hrow[:, a:b], row[:, a:b], T[ctl][:, a:b], -1024.0, A.max, A.add))
-
-    def offsets(name, at, key, a, b, add, times=None):
+    def offsets(n, name, at, key, a, b, add, by=None):
         out, h = T[name][:, at + a // 16:at + b // 16], T.hrow[:, a + 15:b:16]
-        do("v", span("hrow", a, b), span(key, a, b), ts(out, h, add, A.add) if times is None else ts(out, h, add, A.add, times, A.mult))
-
-    def planes(t, i):
-        do("s", state_keys(t, 1) + state_keys(t, 2), ["xp%d" % i], act(T.xp[:, C * i:C * i + C], T["x%d" % t][:, i:4 * C:4]))
+        do("v", n, span("hrow", a, b), span(key, a, b), ts(out, h, add, A.add) if by is None else ts(out, h, add, A.add, by, A.mult))
 
     def cycles(t):
-        land = "land%d" % t
-        if t == 0:
-            do("s", ["fh"], ["thr"], act(T.thr[:], T.fh[:], F.Identity, bias=-0.5))
-            do("s", ["sq"], ["col3"], act(T.col[:, 3:4], T.sq[:, 15:16], F.Identity, scale=2.0, bias=float(MAGIC + LIFT + HALF + 1)))
-
         def jrow(k):
-            return "jp" if k == 0 else "j%d" % (k % 2)
+            return "orow" if k < 0 else "jp" if k == 0 else "j%d" % (k % 2)
 
         def arow(k):
             return "jp" if k == 0 else "a%d" % (k % 2)
 
-        def step(k, op):
-            what = op[0]
-            if what == "c":
-                return spare()
-            q, a, b = op[1:4]
-            lists = (T[land], 0, land) if k < 0 else (T.off, KB * k, "off%d" % k)
-            off = lists[0][:, lists[1] + a // 16:lists[1] + b // 16]
-            if what == "G" and k < 8:
-                j, jn = "orow" if k < 0 else jrow(k), jrow(k + 1)
-                do(q, (["orow"] if k < 0 else span(j)) + span(lists[2], a, b), span(jn, a, b), move(q, T[jn][:, a:b], T[j][:, 0:C].indirect(off)))
-            elif what == "W" and k < 8:
-                wrap(T[jrow(k + 1)], span(jrow(k + 1), a, b), a, b)
-            elif what == "O" and k < 8:
-                offsets("off", KB * (k + 1), "off%d" % (k + 1), a, b, float(LIFT + HALF))
-            elif what == "S" and k + op[4] < 9:
-                n = k + op[4]
-                src, out, d = arow(n), "b%d" % (n % 2), 2.0 ** n / 1024
-                do(q, span(src, a, b), span(out, a, b), act(T[out][:, a:b], T[src][:, a:b], F.Identity, bias=-d) if q == "s"
-                   else ts(T[out][:, a:b], T[src][:, a:b], -d, A.add))
-            elif what == "K":
-                win, out, bk = arow(k), arow(k + 1), "b%d" % (k % 2)
-                do("v", span(win) + span(lists[2], a, b) + span(bk, a, b), span(out, a, b),
-                   tt(T[out][:, a:b], T[win][:, 0:C].indirect(off), T[bk][:, a:b], A.min))
-
-        for op in START:
-            step(-1, op)
-        while later:
-            spare()
-        for k in range(9):
-            for op in LEVEL:
-                step(k, op)
-        planes(t, 0)
-        planes(t, 1)
+        for k in range(-1, 9):
+            lists, at, key = (T["land%d" % t], 0, "land%d" % t) if k < 0 else (T.off, KB * k, "off%d" % k)
+            j, jn = jrow(k), jrow(k + 1)
+            win, out, bk, d = arow(k), arow(k + 1), "b%d" % (k % 2), 2.0 ** k / 1024
+            if k < 8:
+                for n, q, a, b in pieces("G", t, k):
+                    do(q, n, ([j] if k < 0 else span(j)) + span(key, a, b), span(jn, a, b),
+                       move(q, T[jn][:, a:b], T[j][:, 0:C].indirect(lists[:, at + a // 16:at + b // 16])))
+                for n, q, a, b in pieces("W", t, k):
+                    wrap(n, T[jn], span(jn, a, b), a, b)
+                for n, q, a, b in pieces("O", t, k):
+                    offsets(n, "off", KB * (k + 1), "off%d" % (k + 1), a, b, float(LIFT + HALF))
+            if k >= 0:
+                for n, q, a, b in pieces("S", t, k):
+                    do(q, n, span(win, a, b), span(bk, a, b), act(T[bk][:, a:b], T[win][:, a:b], F.Identity, bias=-d) if q == "s"
+                       else ts(T[bk][:, a:b], T[win][:, a:b], -d, A.add))
+                for n, q, a, b in pieces("K", t, k):
+                    do("v", n, span(win) + span(key, a, b) + span(bk, a, b), span(out, a, b),
+                       tt(T[out][:, a:b], T[win][:, 0:C].indirect(lists[:, at + a // 16:at + b // 16]), T[bk][:, a:b], A.min))
         key = arow(9)
         win = T[key]
-        for a, b in (LA, LB):
-            do("v", span(key, a, b) + ["thr"], span("wrow", a, b), scan(T.wrow[:, a:b], win[:, a:b], T.thr[:, a:b], -1024.0, A.max, A.max))
-            do("v", span(key, a, b) + ["ctl"], span("hkey", a, b), scan(T.hkey[:, a:b], win[:, a:b], T.ctl[:, a:b], -1024.0, A.max, A.add))
+        for n, q, a, b in pieces("U", t):
+            do("v", n, span(key, a, b) + ["thr"], span("wrow", a, b), scan(T.wrow[:, a:b], win[:, a:b], T.thr[:, a:b], -1024.0, A.max, A.max))
+        for n, q, a, b in pieces("H", t):
+            do("v", n, span(key, a, b) + ["ctl"], span("hkey", a, b), scan(T.hkey[:, a:b], win[:, a:b], T.ctl[:, a:b], -1024.0, A.max, A.add))
+        for n, q, a, b in sorted(pieces("C", t), key=lambda p: p[2]):
+            do("v", n, span("wrow", a, b) + span("crow", a - 32, a) + ["thr"], span("crow", a, b),
+               scan(T.crow[:, a:b], T.wrow[:, a:b], T.thr[:, a:b], T.crow[:, a - 1:a] if a else -HALF / 1024, A.add, A.subtract))
         own_key, up = T.hkey[:, 15:C:16], float(MAGIC + LIFT + HALF)
-        a, b = LA
-        do("v", span("wrow", a, b) + ["thr"], span("crow", a, b), scan(T.crow[:, a:b], T.wrow[:, a:b], T.thr[:, a:b], -HALF / 1024, A.add, A.subtract))
-        do("v", span("hkey"), ["offm"], ts(T.offm[:], own_key, up, A.add, float(MAGIC), A.subtract))
-        do("v", span("hkey") + ["col3"], ["mw"], ts(T.mw[:], own_key, up, A.add, T.col[:, 3:4], A.subtract))
-        a, b = LB
-        do("v", span("wrow", a, b) + span("crow", a - 32, a) + ["thr"], span("crow", a, b),
-           scan(T.crow[:, a:b], T.wrow[:, a:b], T.thr[:, a:b], T.crow[:, a - 1:a], A.add, A.subtract))
-        do("v", span("hkey") + ["mw"], ["ctlp"], tt(T.ctlp[:, 15:C:16], T.mw[:], own_key, A.subtract))
-        for q, a, b in (("s", 0, ENDS), ("v", ENDS, C)):
-            do(q, span("crow") + ["offm"], span("prow", a, b), move(q, T.prow[:, a:b], T.crow[:, 0:C].indirect(T.offm[:, a // 16:b // 16])))
-        planes(t, 2)
-        planes(t, 3)
-        wrap(T.prow, span("prow"), 0, C, "ctlp")
-        offsets("offp", 0, "offp", 0, C, (LIFT + HALF) / 1024, 1024.0)
-        do("v", span("offp") + ["fh"], ["erow"], cp(T.erow[:, 0:C].indirect(T.offp[:, 0:KB]), T.fh[:]))
-        for a, b in (H2, H1):
-            wrap(T.erow, ["erow"], a, b)
-        for a, b in (H2, H1):
-            offsets("offe", 0, "offe", a, b, float(LIFT + HALF))
-
-    def lay(t, tile, key, part, i):
-        a, b = part
-        q = "v" if i < 2 else "s"
-        src = T.xp[:, C * i:C * i + C].indirect(T.offe[:, a // 16:b // 16])
-        do(q, ["xp%d" % i] + span("offe", a, b), [key + str(i)], move(q, tile[:, 4 * a + i:4 * b:4], src))
-
-    def layer(t, i, qz, sz, a, b, key, bank, start=True):
-        matmul(T[bank][:, 0:b - a], bank, T.qw[:, S * i:S * i + S], T.sw[:, S * i:S * i + S], ["w"], qz[:, a:b], sz[:, a:b], [key], start, True)
+        do("v", ("offm", t), span("hkey"), ["offm"], ts(T.offm[:], own_key, up, A.add, float(MAGIC), A.subtract))
+        do("v", ("mw", t), span("hkey") + ["col3"], ["mw"], ts(T.mw[:], own_key, up, A.add, T.col[:, 3:4], A.subtract))
+        do("v", ("ctlm", t), span("hkey") + ["mw"], ["ctlp"], tt(T.ctlp[:, 15:C:16], T.mw[:], own_key, A.subtract))
+        for n, q, a, b in pieces("P", t):
+            do(q, n, span("crow") + ["offm"], span("prow", a, b), move(q, T.prow[:, a:b], T.crow[:, 0:C].indirect(T.offm[:, a // 16:b // 16])))
+        for n, q, a, b in pieces("W", t):
+            wrap(n, T.prow, span("prow", a, b), a, b, "ctlp")
+        for n, q, a, b in pieces("O", t):
+            offsets(n, "offp", 0, "offp", a, b, (LIFT + HALF) / 1024, 1024.0)
+        do("v", ("pute", t), span("offp") + ["fh"], ["erow"], cp(T.erow[:, 0:C].indirect(T.offp[:, 0:KB]), T.fh[:]))
+        for n, q, a, b in pieces("W", t, None, "e"):
+            wrap(n, T.erow, ["erow"], a, b)
+        for n, q, a, b in pieces("O", t, None, "e"):
+            offsets(n, "offe", 0, "offe", a, b, float(LIFT + HALF))
 
     def lay_out(t):
         zt, qz, sz, xn = T["zt%d" % t], T["qz%d" % t], T["sz%d" % t], T["x%d" % (t + 1)]
         bt, qb, sb, qc, sc = ["%s%d" % (n, t) for n in ("bt", "qb", "sb", "qc", "sc")]
 
-        def gather(h, i):
-            lay(t, zt, "z%d:%d:" % (t, h), HALVES[h], i)
+        def lay(name, tile, key, a, b, i):
+            q = who[name, t]
+            src = T.xp[:, C * i:C * i + C].indirect(T.offe[:, a // 16:b // 16])
+            do(q, (name, t), ["xp%d" % i] + span("offe", a, b), [key], move(q, tile[:, 4 * a + i:4 * b:4], src))
 
-        def through(h):
-            a, b = HALVES[h]
-            do("v", ["z%d:%d:%d" % (t, h, i) for i in range(4)], ["qz%d:%d" % (t, h)], quant(qz[:, a:b], sz[:, a:b], zt[:, 4 * a:4 * b]))
+        def through(h, a, b, bank, start):
+            key = "qz%d:%d" % (t, h)
+            do("v", ("qz%d" % h, t), ["z%d:%d:%d" % (t, h, i) for i in range(4)], [key], quant(qz[:, a:b], sz[:, a:b], zt[:, 4 * a:4 * b]))
             for i in range(4):
-                layer(t, i, qz, sz, a, b, "qz%d:%d" % (t, h), ("pr%d" if h == 1 else "pp%d") % i)
+                matmul(("w%d%d" % (h, i), t), T[bank % i][:, 0:b - a], bank % i, T.qw[:, S * i:S * i + S], T.sw[:, S * i:S * i + S], ["w"],
+                       qz[:, a:b], sz[:, a:b], [key], start, True)
 
-        def times64(i):
-            a, b = H1
-            out, src = T.z64[:, 4 * a + i:4 * b:4], zt[:, 4 * a + i:4 * b:4]
-            do("v" if i < 2 else "s", ["z%d:%d:%d" % (t, h, i) for h in HALVES], ["z64:%d" % i],
-               ts(out, src, 64.0, A.mult) if i < 2 else act(out, src, scale=64.0))
+        def unpack(name, i, stop):
+            matmul((name, t), T["pr%d" % i][:, 0:S], "pr%d" % i, T.qe[:, S * i:S * i + S], T.se[:, S * i:S * i + S], ["qe%d" % i],
+                   T[qc][:], T[sc][:], [qc, sc], True, stop)
 
-        for i in (2, 0, 3, 1):
-            lay(t, T[bt], bt + ":", H2, i)
-        for h, i in ((1, 2), (1, 3), (3, 2), (3, 3), (1, 0)):
-            gather(h, i)
-        do("v", [bt + ":%d" % i for i in range(4)], [qb, sb], quant(T[qb][:], T[sb][:], T[bt][:]))
+        for i in range(4):
+            do("s", ("p%d" % i, t), [k for h in PART for k in state_keys(t, h)], ["xp%d" % i], act(T.xp[:, C * i:C * i + C], T["x%d" % t][:, i:4 * C:4]))
+        for i in range(4):
+            lay("b%d" % i, T[bt], bt + ":%d" % i, 0, S, i)
+        do("v", ("qb", t), [bt + ":%d" % i for i in range(4)], [qb, sb], quant(T[qb][:], T[sb][:], T[bt][:]))
         send(t, [([qc], qc, qb, lambda n: T[n][:].bitcast(dt.uint8), [qb]), ([sc], sc, sb, lambda n: T[n][:], [sb])], "rxb%d" % t)
-        gather(1, 1)
-        gather(3, 0)
-        through(1)
-        gather(3, 1)
-        times64(2)
-        times64(3)
-        times64(0)
-        through(3)
-        times64(1)
-        for h, (a, b) in HALVES.items():
+        for h in (1, 3):
+            a, b = PART[h]
+            bank = "pr%d" if h == 1 else "pp%d"
             for i in range(4):
-                bank = ("pr%d" if h == 1 else "pp%d") % i
-                do("v", [bank, "z64:%d" % i], ["r%d:%d" % (i, h)],
-                   tt(T["r%d" % i][:, a:b], T[bank][:, 0:b - a], T.z64[:, 4 * a + i:4 * b:4], A.add))
-        for h, (a, b) in HALVES.items():
+                lay("z%d%d" % (h, i), zt, "z%d:%d:%d" % (t, h, i), a, b, i)
+            through(h, a, b, bank, True)
             for i in range(4):
-                do("s", ["r%d:%d" % (i, h)], ["x%d:%d:%d" % (t + 1, h, i)], act(xn[:, 4 * a + i:4 * b:4], T["r%d" % i][:, a:b], scale=0.015625))
-
-    def unpack(t, i, start, stop):
-        qc, sc = "qc%d" % t, "sc%d" % t
-        matmul(T["pr%d" % i][:, 0:S], "pr%d" % i, T.qe[:, S * i:S * i + S], T.se[:, S * i:S * i + S], ["qe%d" % i], T[qc][:], T[sc][:], [qc, sc], start, stop)
-
-    def arrive(t):
-        zt = T["zt%d" % t]
+                name, cols, r = "%d%d" % (h, i), slice(4 * a + i, 4 * b, 4), T["r%d" % i][:, a:b]
+                q = who["m" + name, t]
+                do(q, ("m" + name, t), ["z%d:%d:%d" % (t, h, i)], ["z64:" + name], times(q, T.z64[:, cols], zt[:, cols], 64.0))
+                do("v", ("a" + name, t), [bank % i, "z64:" + name], ["r" + name], tt(r, T[bank % i][:, 0:b - a], T.z64[:, cols], A.add))
+                q = who["x" + name, t]
+                do(q, ("x" + name, t), ["r" + name], ["x%d:%d:%d" % (t + 1, h, i)], times(q, xn[:, cols], r, 0.015625))
         for i in range(4):
-            unpack(t, i, True, True)
-            do("v", ["pr%d" % i], ["z%d:2:%d" % (t, i)], ts(zt[:, i:4 * S:4], T["pr%d" % i][:, 0:S], 0.015625, A.mult))
+            q = who["c%d" % i, t]
+            unpack("d%d" % i, i, True)
+            do(q, ("c%d" % i, t), ["pr%d" % i], ["z%d:2:%d" % (t, i)], times(q, zt[:, i:4 * S:4], T["pr%d" % i][:, 0:S], 0.015625))
+            unpack("f%d" % i, i, False)
+        through(2, 0, S, "pr%d", False)
         for i in range(4):
-            unpack(t, i, True, False)
-
-    def arrive_layer(t):
-        zt, qz, sz = T["zt%d" % t], T["qz%d" % t], T["sz%d" % t]
-        do("v", ["z%d:2:%d" % (t, i) for i in range(4)], ["qz%d:2" % t], quant(qz[:, 0:S], sz[:, 0:S], zt[:, 0:4 * S]))
-        for i in range(4):
-            layer(t, i, qz, sz, 0, S, "qz%d:2" % t, "pr%d" % i, False)
-
-    def arrived(t):
-        for i in range(4):
-            out, src = T["x%d" % (t + 1)][:, i:4 * S:4], T["pr%d" % i][:, 0:S]
-            do("s" if i < 2 else "v", ["pr%d" % i], ["x%d:2:%d" % (t + 1, i)],
-               act(out, src, scale=0.015625) if i < 2 else ts(out, src, 0.015625, A.mult))
+            q = who["y%d" % i, t]
+            do(q, ("y%d" % i, t), ["pr%d" % i], ["x%d:2:%d" % (t + 1, i)], times(q, xn[:, i:4 * S:4], T["pr%d" % i][:, 0:S], 0.015625))
 
     def finish(t, h):
-        a, b = H1 if h == 1 else H2
-        q, s, key, p = T["qx%d" % t], T["sx%d" % t], "qx%d:%d" % (t, h), "pp0" if h == 1 else "pp2"
-        matmul(T[p][:, 0:b - a], p, T.qv[:], T.sv[:], ["qv"], q[:, a:b], s[:, a:b], [key])
-        store("y", [key], T.oc[:, 4 * a:4 * b], q[:, a:b].bitcast(dt.uint8))
+        a, b = (S, C) if h == 1 else (0, S)
+        q, s, p = T["qx%d" % t], T["sx%d" % t], BANKS[h][0]
+        keys = ["qx%d:%d" % (t, i) for i in ((1, 3) if h == 1 else (2,))]
+        matmul(("fin%d" % h, t), T[p][:, 0:b - a], p, T.qv[:], T.sv[:], ["qv"], q[:, a:b], s[:, a:b], keys)
+        store("y", None, keys, T.oc[:, 4 * a:4 * b], q[:, a:b].bitcast(dt.uint8))
         for k in range(4):
-            store("y", [key], T.osc[4 * k:4 * k + 4, a:b], s[32 * k:32 * k + 4, a:b])
+            store("y", None, keys, T.osc[4 * k:4 * k + 4, a:b], s[32 * k:32 * k + 4, a:b])
+        do("s", ("ysb%d" % h, t - 1), [p], ["ysb:%d" % h], act(T.ysb[:, a:b], T[p][:, 0:b - a]))
+        store("s", ("sty%d" % h, t - 1), ["ysb:%d" % h], T.y[:, a:b], T.ysb[:, a:b])
 
-    def store_y(h):
-        a, b = H1 if h == 1 else H2
-        p = "pp0" if h == 1 else "pp2"
-        do("s", [p], ["ysb:%d" % h], act(T.ysb[:, a:b], T[p][:, 0:b - a]))
-        store("s", ["ysb:%d" % h], T.y[:, a:b], T.ysb[:, a:b])
-
-    quant_state(0, 1)
-    score(0, 1)
-    quant_state(0, 2)
-    score(0, 2)
-    take("row", 1)
-    take("row", 2)
-    take("mask", 1)
-    take("mask", 2)
-    take("own", 1)
-    take("own", 2)
-    take("flag", 1)
-    do("v", ["gs"], ["qg"], quant(T.qg[:], T.sg[:], T.gs[:]))
-    take("sum", 1)
     for t in range(R):
+        for h in PART:
+            score(t, h)
         places(t)
         cycles(t)
-        lay_out(t)
         if t == R - 1:
-            do("s", ["erow"], ["elf"], act(T.elf[:], T.erow[:], F.Identity, bias=float(HALF)))
-            store("y", ["elf"], T.el[:], T.elf[0:128:16, :])
-        arrive(t)
-        quant_state(t + 1, 1)
-        if t < R - 1:
-            score(t + 1, 1)
-            arrive_layer(t)
-            take("row", 1)
-            take("mask", 1)
-            arrived(t)
-            take("own", 1)
-            quant_state(t + 1, 2)
-            score(t + 1, 2)
-            take("row", 2)
-            take("flag", 1)
-            take("mask", 2)
-            take("sum", 1)
-            take("own", 2)
-        else:
-            arrive_layer(t)
-            finish(t + 1, 1)
-            arrived(t)
-            store_y(1)
-            quant_state(t + 1, 2)
-            finish(t + 1, 2)
-            store_y(2)
+            do("s", ("elf", t), ["erow"], ["elf"], act(T.elf[:], T.erow[:], F.Identity, bias=float(HALF)))
+            store("y", None, ["elf"], T.el[:], T.elf[0:128:16, :])
+        lay_out(t)
+    for h in PART:
+        quant_state(R, h)
+    finish(R, 1)
+    finish(R, 2)
+
+    queue = {"v": g.vector, "s": g.scalar, "t": g.tensor, "g": g, "y": g.sync}
+    place = {n: i for q in seq for i, n in enumerate(seq[q])}
+    todo = {q: sorted((i for i, c in enumerate(calls) if c[0] == q), key=lambda i: (place[calls[i][1]] if calls[i][1] else -1, i)) for q in queue}
+    for h in HOOK:
+        h(calls, fixed, todo)
+    count = dict(landed)
+    know = {q: {} for q in queue}
+    token = {}
+    while any(todo.values()):
+        ready = [q for q in queue if todo[q] and all(i in token for i in calls[todo[q][0]][2] | calls[todo[q][0]][3])]
+        q = ready[0]
+        i = todo[q].pop(0)
+        _, _, need, _, issue, sem, inc = calls[i]
+        for s, val, seen in sorted((token[j] for j in need), key=lambda tok: -tok[1]):
+            if know[q].get(s, 0) < val:
+                queue[q].wait_ge(T.sem[s], val)
+                for s2, n in list(seen.items()) + [(s, val)]:
+                    know[q][s2] = max(know[q].get(s2, 0), n)
+        issue(queue[q])
+        count[sem] = count.get(sem, 0) + inc
+        token[i] = fixed[i] + ({},) if i in fixed else (sem, count[sem], dict(know[q]))
     for sem in sorted(count):
         g.wait_ge(T.sem[sem], count[sem])

from concourse.mybir import dt, AluOpType as A, ActivationFunctionType as F

C, S, R = 448, 128, 2
STEP = [1, 2]
KB = C // 16
NQ = KB // 4
WIDE = [max(128, C - 64 * i) for i in range(NQ)]
AT = [sum(WIDE[:i]) for i in range(NQ + 1)]
FIRST = 26
HIGH = 14
NH = 4
ENGINES = 8
PART = {1: (S, S + 160), 3: (S + 160, C), 2: (0, S)}
BANKS = {1: ("pp0", "pp1"), 3: ("pp2", "pp3"), 2: ("pr0", "pr1")}
HALF = C // 2
LIFT = 512
DEEP = 1024
BIG = 2.0 ** 80
MAGIC = 12582912
RELS = 6

SCORE = {"v": "qx1 qx2 mask1 mask2 own1 own2 flag1 qg sum1", "s": "row1 row2", "t": "sc1 sc2"}
ORDER = {"v": "g22 flag2 g21 u22 k1 sum2 g20 u21 tie g19 u20 g18 u19 g17 u18 g16 u17 q0 base26 g15 u16 set26 g14 u15 off26 q2 u14 q1 "
              "base14 base23 q3 g12 ctl u12 set14 g11 off14 u11 ctlp ctl15 q4 put:224:352 q5 q6 base0 base11 base13 put:352:384 set0 put:384:448 off0 "
              "qe0 qe1 put:0:224",
         "s": "r27 r26 s27 r25 s26 r24 s25 r23 s24 r13 s23 r10 s13 r9 s10 r8 s9 r7 s8 r6 s7 r5 s6 r4 s5 r3 s4 r2 s3 r1 s2 s1 thr col3",
         "t": "e0 h0 l0 h2 l2 h1 l1 h3 l3 l4 l5 l6"}
START = {"v": "G:352:448@-1 G:128:224@-1 W:224:448@-1 W:0:224@-1 O:224:448@-1 O:0:224@-1 qe2 qe3 qv "
              "W:0:224@0 K:0:128@0 O:0:224@0 K:128:320@0 W:224:448@0 K:320:448@0 O:224:448@0",
         "s": "G:224:352@-1 G:0:128@-1 G:0:224@0 S:0:128@0 S:128:320@0 G:224:448@0 S:320:448@0"}
LEVEL = {"v": "W:0:224@0 K:0:128@0 O:0:224@0 K:128:320@0 W:224:448@0 K:320:448@0 O:224:448@0",
         "s": "G:0:224@0 S:0:128@0 S:128:320@0 G:224:448@0 S:320:448@0"}
ENDS = {"v": "K:0:128@8 K:128:320@8 K:320:448@8 U:0:224 H:0:224 U:224:448 H:224:448 C:0:224 offm mw C:224:448 ctlm P:224:448 W:0:448 O:0:448 "
             "pute W:0:128e W:128:448e O:0:128e O:128:448e",
        "s": "S:0:128@8 S:128:320@8 S:320:448@8 p0 p1 P:0:224 p2 p3"}
NEXT = {"v": "b0 b1 z10 qb z11 z30 qz1 z31 m30 m32 m33 qz3 a10 a11 a12 a13 m31 a30 a31 a32 a33 c2 c3 "
             "qz2 qx1 mask1 y2 y3 own1 qx2 flag1 mask2 sum1 own2",
        "s": "b2 b3 z12 z13 z32 z33 m10 m11 m12 m13 x10 x11 x12 x13 c0 c1 x30 x31 x32 x33 row1 y0 y1 row2",
        "t": "w10 w11 w12 w13 w30 w31 w32 w33 d0 d1 d2 d3 f0 f1 f2 f3 w20 w21 w22 w23 sc1 sc2"}
LAST = {"v": "b0 b1 z10 qb z11 z30 qz1 z31 m30 m32 m33 qz3 a10 a11 a12 a13 m31 a30 a31 a32 a33 c2 c3 qz2 qx1 y2 y3 qx2",
        "s": "b2 b3 z12 z13 z32 z33 m10 m11 m12 m13 x10 x11 x12 x13 c0 c1 x30 x31 x32 x33 elf y0 y1 ysb1 sty1 ysb2 sty2",
        "t": "w10 w11 w12 w13 w30 w31 w32 w33 d0 d1 d2 d3 f0 f1 f2 f3 w20 w21 w22 w23 fin1 fin2"}
SCORE = {'v': 'qx3 qx1 mask3 qx2 mask1 own3 qg own1 mask2 flag3 flag1 own2 g22:128:352 sum3 sum1', 's': 'row3 row1 r27:128:432 r26:128:416 row2 r25:128:400', 't': 'sc3 sc1 sc2'}
ORDER = {'v': 'g22:0:128 flag2 g21 u22 sum2 g20 u21 tie g19 u20 g18 u19 g17 u18 q0 base26 g16 u17 g15 set26 u16 q2 off26 g14 u15 q1 u14 q3 g12 base23 base14 g11 u12 set14 u11 q4 off14 q5 q6 put:224:352 base0 base11 base13 put:352:384 set0 put:384:448 off0 ctlp put:0:224', 's': 'k1 r27:0:128 r26:0:128 r25:0:128 s27 s26 s25 r24 r23 r13 s24 s23 r10 s13 r9 r8 s10 r7 s9 r6 s8 r5 s7 r4 s6 r3 s5 r2 s4 r1 s3 s2 s1 ctl thr ctl15 col3', 't': 'e0 h0 l0 h2 h1 h3 l1 l2 l3 l4 l5 l6'}
START = {'v': 'G:320:448@-1 G:0:128@-1 W:224:448@-1 W:0:224@-1 O:224:448@-1 O:0:224@-1 K:320:448@0 W:224:448@0 K:224:320@0 O:224:448@0 W:0:224@0 K:96:224@0 O:0:224@0', 's': 'G:224:320@-1 G:128:224@-1 S:320:448@0 S:96:320@0 S:0:96@0 G:224:448@0 G:0:224@0'}
LEVEL = {'v': 'W:224:448@0 K:0:96@-1 O:224:448@0 W:0:224@0 K:320:448@0 O:0:224@0 K:96:320@0', 's': 'G:224:448@0 G:0:224@0 S:320:448@0 S:96:320@0 S:0:96@0'}
ENDS = {'v': 'W:224:448@7 K:0:96@6 O:224:448@7 K:320:448@7 K:96:320@7 K:0:96@7 W:0:224@7 K:320:448@8 O:0:224@7 K:224:320@8 K:0:224@8 U:224:448 U:0:224 H:224:448 H:0:224 C:0:448 offm mw qe0 P:224:448 ctlm qe1 W:0:448 qe2 O:0:448 qe3 pute qv W:0:128e W:128:448e O:0:128e O:128:448e', 's': 'G:224:448@7 S:320:448@7 S:96:320@7 S:0:96@7 G:0:224@7 S:320:448@8 S:96:320@8 S:0:96@8 p0 p1 P:0:224 p2 p3'}
NEXT = {'v': 'b0 b1 z10 qb z11 z31 qz1 z30 m13 m32 qz3 a11 a10 a13 a12 a31 a32 a30 a33 c3 c2 qz2 x10 qx3 qx1 y2 mask3 qx2 mask1 own3 own1 mask2 flag3 flag1 own2 g22:128:352 sum1 sum3', 's': 'b3 b2 z13 z12 z33 z32 m11 m10 m30 m12 m31 m33 x13 x11 x31 c1 c0 x30 x32 x33 x12 y0 y3 y1 row3 row1 r26:128:416 r25:128:400 row2 r27:128:432', 't': 'w11 w10 w13 w12 w31 w32 w30 w33 d3 d1 d2 d0 f1 f2 f3 f0 w20 w23 w22 w21 sc3 sc1 sc2'}
LAST = {'v': 'b1 b0 z10 qb z11 z31 qz1 z30 m32 m13 qz3 a13 a12 a10 a11 a33 a32 m30 c3 c2 a31 a30 qz2 x31 qx1 qx3 y2 y3 qx2', 's': 'elf b3 b2 z12 z13 z32 m12 z33 m10 m31 m11 m33 x12 x13 x11 x10 c0 c1 x33 x32 x30 y1 y0 ysb1 ysb2 sty1 sty2', 't': 'w13 w12 w11 w10 w33 w32 w31 d3 d0 d2 d1 w30 f0 f3 f2 f1 w22 w21 w23 w20 fin1 fin2'}
OF_NEXT = ("qx", "sc", "fin", "mask", "own", "flag", "sum", "row", "r", "g")


def orders():
    seq = {q: [] for q in "vst"}

    def add(lists, t, k=0, ahead=()):
        for q, names in lists.items():
            for n in names.split():
                n, _, at = n.partition("@")
                seq[q].append((n, t + (n.split(":")[0].rstrip("0123456789") in ahead)) + ((k + int(at),) if at else ()))
    add(SCORE, 0)
    for t in range(R):
        add(ORDER, t)
        add(START, t)
        for k in range(1, 7):
            add(LEVEL, t, k)
        add(ENDS, t)
        add(NEXT if t < R - 1 else LAST, t, 0, OF_NEXT)
    return seq


SCRATCH = {}


def _buf(dtype, n, *names):
    for name in names:
        SCRATCH[name] = ("psum" if name[:2] in ("pp", "pr") and name[2:].isdigit() else "sbuf", [128, n], dtype)


_buf("bfloat16", 512, "ub", "vb", "neg", "c64", "go", "gs", "bt0", "bt1")
_buf("bfloat16", 4 * 512, "eb")
_buf("bfloat16", C, "rr", "side", "drop", "gate", "sg3", "sq", "ctl", "fh", "orow", "crow", "prow", "erow", "jp", "j0", "j1", "eqs")
_buf("bfloat16", RELS * C, "rel")
_buf("float16", C, "hrow", "ctlp")
_buf("bfloat16", 224 * KB, "zs")
_buf("bfloat16", 4 * C, "z64", "x0", "x1", "x2", "zt0", "zt1", "xp")
_buf("float8_e4m3fn_x4", 128, "qu", "qur", "qv", "qg", "qb0", "qb1", "qc0", "qc1")
_buf("uint8", 128, "su", "sur", "sv", "sg", "sb0", "sb1", "sc0", "sc1")
_buf("float8_e4m3fn_x4", 512, "qw", "qe")
_buf("uint8", 512, "sw", "se")
_buf("float8_e4m3fn_x4", C, "qx0", "qx1", "qx2", "qz0", "qz1")
_buf("uint8", C, "sx0", "sx1", "sx2", "sz0", "sz1")
_buf("bfloat16", 4 * AT[NQ], "fl")
_buf("float8_e4m3fn_x4", AT[NQ], "qf")
_buf("uint8", AT[NQ], "sf")
_buf("int32", 8, "ku", "pc")
_buf("uint16", 8, "offu")
_buf("uint16", KB, "offm", "offp", "offe", "own0", "own1", "land0", "land1")
_buf("uint16", 9 * KB, "off")
_buf("float32", C, "thr", "mrow", "arow", "srow", "ctlb", "hkey", "hcol", "wrow", "elf", "ysb",
     "a0", "a1", "b0", "b1", "r0", "r1", "r2", "r3")
_buf("float32", KB, "k0", "k1", "cnt", "tie", "mw")
_buf("float32", 8, "col")
_buf("float32", 512, "pp0", "pp1", "pp2", "pp3", "pr0", "pr1", "pr2", "pr3")

LOADS = ["ldu", "ldx1", "ldx2", "ldx3", "ldw", "ldv"]
FETCH = [3, 1, 2]
SEMAPHORES = ["cv", "cs", "ct", "cg", "stored", "sent", "rxh0", "rxh1", "rxl0", "rxl1", "rxb0", "rxb1"] + LOADS
HOOK = []


def rank_program(g, core, T, topo):
    rank = T.rank_of(core)
    if rank is None:
        return
    seq = orders()
    who = {n: q for q in seq for n in seq[q]}
    calls = []
    writer, reader = {}, {}
    fixed = {}

    def note(q, name, reads, writes, issue, sem, inc, joins=False):
        need, ahead = set(), set()
        for k in reads:
            need.update(writer.get(k, []))
            if k[:2] in ("pp", "pr"):
                need.update(i for i in reader.get(k, []) if calls[i][0] != q)
        for k in writes:
            (ahead if joins else need).update(writer.get(k, []))
            need.update(reader.get(k, []))
        calls.append((q, name, need, ahead, issue, sem, inc))
        for k in reads:
            reader.setdefault(k, []).append(len(calls) - 1)
        for k in writes:
            writer[k], reader[k] = [len(calls) - 1], []
        return len(calls) - 1

    def do(q, name, reads, writes, make, joins=False):
        note(q, name, reads, writes, lambda e: make(e).then_inc(T.sem["c" + q], 1), "c" + q, 1, joins)

    def load(q, sem, total, key, out, in_, after=()):
        held = writer.get(key, [])
        i = note(q, None, list(after), [], lambda e: e.dma_start(out, in_).then_inc(T.sem[sem], 16), sem, 16)
        writer[key], fixed[i] = held + [i], (sem, total)

    def store(q, name, reads, out, in_):
        note(q, name, reads, [], lambda e: e.dma_start(out, in_).then_inc(T.sem["stored"], 16), "stored", 16)

    landed = {}

    def send(t, pairs, sem):
        dst = T.cores[rank ^ STEP[t]]
        rid, pid, _ = topo.addr(dst)
        eng = topo.engines(core, dst)[:ENGINES]
        mask = sum(1 << e for e in eng)
        landed[sem] = landed.get(sem, 0) + len(pairs) * len(eng)
        for land, there, here, view, keys in pairs:
            i = note("g", None, keys, [], lambda e, a=view(there), b=view(here): e.remote_dma(a, b, T.sem[sem], T.sem["sent"], pid, rid, mask),
                     "sent", len(eng))
            fixed[i] = (sem, landed[sem])
            for k in land:
                writer[k] = [i]
            for k in keys:
                reader[k].remove(i)

    def ts(out, in0, s1, op0, s2=None, op1=None):
        if op1 is None:
            return lambda e: e.tensor_scalar(out, in0, s1, None, op0)
        return lambda e: e.tensor_scalar(out, in0, s1, s2, op0, op1)

    def tt(out, in0, in1, op):
        return lambda e: e.tensor_tensor(out, in0, in1, op)

    def act(out, in_, func=F.Copy, **kw):
        return lambda e: e.activation(out, in_, func, **kw)

    def cp(out, in_):
        return lambda e: e.tensor_copy(out, in_)

    def move(q, out, in_):
        return act(out, in_) if q == "s" else cp(out, in_)

    def times(q, out, in_, x):
        return act(out, in_, scale=x) if q == "s" else ts(out, in_, x, A.mult)

    def fill(out, x):
        return lambda e: e.memset(out, x)

    def quant(q, s, x):
        return lambda e: e.quantize_mx(q, s, x)

    def scan(out, d0, d1, init, op0, op1):
        return lambda e: e.tensor_tensor_scan(out, d0, d1, init, op0, op1)

    def matmul(name, out, key, lhs, ls, lkey, rhs, rs, rkey, start=True, stop=True):
        do("t", name, lkey + rkey, [key], lambda e: e.matmul_mx(out, lhs, ls, rhs, rs, start, stop), not start)

    def back(a, b):
        return slice(b - 1, a - 1 if a else None, -1)

    def span(name, a=0, b=C):
        return ["%s:%d" % (name, i) for i in range(a // 32, (b + 31) // 32)]

    def pieces(what, t, k=None, tail=""):
        out = []
        for q in "vs":
            for n in seq[q]:
                w = n[0].split(":")
                if len(w) == 3 and w[0] == what and n[1:] == ((t,) if k is None else (t, k)) and w[2].lstrip("0123456789") == tail:
                    out.append((n, q, int(w[1]), int(w[2].rstrip(tail))))
        return out

    def iota(name, pattern, base, cm, cols=slice(None), key=None):
        kw = {} if SCRATCH[name][2] == "int32" else {"allow_small_or_imprecise_dtypes": True}
        do("g", None, [], [key or name], lambda e: e.iota(T[name][:, cols], pattern, base, cm, **kw))

    def flags(k, a, b):
        z = 4 * AT[(KB - k) // 4] + (KB - k) % 4
        return T.fl[:, z + 4 * a:z + 4 * b - 3:4]

    def parts(name):
        return ["%s:%d" % (name, h) for h in PART]

    def rows(i):
        return [n for k in range(KB - 4 * i - 3, KB - 4 * i + 1) for n in parts("fl%d" % k)]

    by_s = [k for k in range(KB) if ("s%d" % k, 0) in who]

    load("s", "ldu", 16, "ub", T.ub[:], T.u[:])
    for h in FETCH:
        a, b = PART[h]
        load("y", "ldx%d" % h, 16, "x0:%d" % h, T.x0[:, 4 * a:4 * b], T.x[:, 4 * a:4 * b])
    load("y", "ldw", 32, "w", T.qw[:].bitcast(dt.uint8), T.wc[:], parts("x0"))
    load("y", "ldw", 32, "w", T.sw[:], T.ws[:])
    load("y", "ldv", 16, "vb", T.vb[:], T.v[:])

    iota("ku", [[16, 8]], 0, 0)
    iota("pc", [[0, 1]], 0, 1, slice(0, 1))
    iota("rr", [[0, KB], [1, 16]], 0, 0)
    do("v", None, [], ["neg"], fill(T.neg[:], -1.0))
    do("g", None, ["neg"], ["go"], lambda e: e.affine_select(T.go[:], T.neg[:], [[-16, 8], [0, 64]], A.is_ge, 0.0, 0, 1))
    do("g", None, ["go"], ["gs"], lambda e: e.affine_select(T.gs[:], T.go[:], [[16, 8], [0, 64]], A.is_ge, 0.0, 15, -1))
    left, k0_keys = [], []
    for k in range(KB):
        n = C - 16 * (k + 1) - 16 * sum(i > k for i in by_s) - LIFT - DEEP
        left.append(n + (16 * k if k in by_s else HALF if k else 0))
    k = 0
    while k < KB:
        step, n = (left[k + 1] - left[k] if k < KB - 1 else 0), 1
        while k + n < KB and left[k + n] - left[k + n - 1] == step:
            n += 1
        k0_keys.append("k0:%d" % k)
        iota("k0", [[step, n]], left[k], 0, slice(k, k + n), k0_keys[-1])
        k += n
    do("v", None, ["ku"], ["offu"], cp(T.offu[:], T.ku[:]))
    do("v", None, ["pc"], ["pq"], ts(T.pc[:, 1:2], T.pc[:, 0:1], 15, A.bitwise_and))
    do("v", None, [], ["cnt0"], fill(T.cnt[:, 0:1], 0.0))
    do("v", None, [], ["c64"], fill(T.c64[:], 64.0))
    own_q = T.col[:, 0:1]
    do("v", None, ["pq"], ["q"], cp(own_q, T.pc[:, 1:2]))
    do("v", None, ["rr", "q"], ["side"], ts(T.side[:], T.rr[:], own_q, A.subtract, BIG, A.mult))
    do("v", None, ["ub"], ["qu"], quant(T.qu[:], T.su[:], T.ub[:]))
    do("v", None, ["rr", "q"], ["drop"], ts(T.drop[:], T.rr[:], own_q, A.is_equal, -1024 * BIG, A.mult))
    do("v", None, ["qu", "offu"], ["qur"], cp(T.qur[:, 0:128].bitcast(dt.uint32), T.qu[:, 0:128].bitcast(dt.uint32).indirect(T.offu[:, 0:8])))
    do("v", None, ["qu", "offu"], ["sur"], cp(T.sur[:, 0:128], T.su[:, 0:128].indirect(T.offu[:, 0:8])))
    do("v", None, ["rr", "q"], ["gate"], ts(T.gate[:], T.rr[:], own_q, A.not_equal))
    for i in range(NQ):
        n = WIDE[i] - (C - 64 * i - 48)
        do("s", None, ["neg"], rows(i), act(T.fl[:, 4 * (AT[i + 1] - n):4 * AT[i + 1]], T.neg[:, 0:4 * n], scale=0.0))
    do("s", None, ["side"], ["sg3"], act(T.sg3[:], T.side[:], F.Sign))
    do("s", None, ["side"], ["col1"], act(T.col[:, 1:2], T.side[:, 15:16], F.Identity, scale=1 / BIG, bias=576.0))
    do("s", None, ["sg3"], ["sq"], act(T.sq[:], T.sg3[:], F.Square, bias=-0.25))
    do("s", None, ["sq"], ["ctlb"], act(T.ctlb[:], T.sq[:], F.Identity, scale=-1024.0, bias=576.0))
    do("s", None, ["sq", "col1"], ["col2"], act(T.col[:, 2:3], T.sq[:, 15:16], F.Identity, scale=-1024.0, bias=T.col[:, 1:2]))
    iota("fh", [[1, C]], -HALF, 0)
    for b in range(4):
        do("g", None, ["c64"], ["eb%d" % b], lambda e, b=b: e.affine_select(
            T.eb[:, 512 * b:512 * b + 512], T.c64[:], [[-1, 512]], A.is_equal, 0.0, b, 4))
        do("v", ("qe%d" % b, 0), ["eb%d" % b], ["qe%d" % b], quant(T.qe[:, S * b:S * b + S], T.se[:, S * b:S * b + S], T.eb[:, 512 * b:512 * b + 512]))
    do("v", ("qg", 0), ["gs"], ["qg"], quant(T.qg[:], T.sg[:], T.gs[:]))
    do("v", ("qv", 0), ["vb"], ["qv"], quant(T.qv[:], T.sv[:], T.vb[:]))
    do("s", ("k1", 0), ["col2"] + k0_keys, ["k1"], act(T.k1[:], T.k0[:], F.Identity, bias=T.col[:, 2:3]))
    do("s", ("ctl", 0), ["sq"], ["ctl"], act(T.ctl[:], T.sq[:], F.Identity, scale=-1024.0, bias=576.0))
    do("v", ("ctlp", 0), ["sq"], ["ctlp"], ts(T.ctlp[:], T.sq[:], -2.0, A.mult, 1.125, A.add))
    do("s", ("ctl15", 0), ["sq"], ["ctl"], act(T.ctl[:, 15:C:16], T.sq[:, 15:C:16], F.Identity, scale=-1024.0, bias=576.0 - 2 * LIFT))
    do("s", ("thr", 0), ["fh"], ["thr"], act(T.thr[:], T.fh[:], F.Identity, bias=-0.5))
    do("s", ("col3", 0), ["sq"], ["col3"], act(T.col[:, 3:4], T.sq[:, 15:16], F.Identity, scale=2.0, bias=float(MAGIC + LIFT + HALF + 1)))

    def state_keys(t, h):
        if t == 0:
            return ["x0:%d" % h]
        return ["x%d:%d:%d" % (t, h, i) for i in range(4)]

    def quant_state(t, h):
        a, b = PART[h]
        do("v", ("qx%d" % h, t), state_keys(t, h), ["qx%d:%d" % (t, h)], quant(T["qx%d" % t][:, a:b], T["sx%d" % t][:, a:b], T["x%d" % t][:, 4 * a:4 * b]))

    def score(t, h):
        a, b = PART[h]
        qx, sx = T["qx%d" % t], T["sx%d" % t]
        quant_state(t, h)
        p0, p1 = BANKS[h]
        for p in (p0, p1):
            matmul(("sc%d" % h, t), T[p][:, 0:b - a], p, T.qur[:], T.sur[:], ["qur", "sur"], qx[:, a:b], sx[:, a:b], ["qx%d:%d" % (t, h)])
        do("s", ("row%d" % h, t), [p1], ["srow:%d" % h], act(T.srow[:, a:b], T[p1][:, 0:b - a]))
        do("v", ("mask%d" % h, t), [p0, "side"], ["mrow:%d" % h], tt(T.mrow[:, a:b], T[p0][:, 0:b - a], T.side[:, a:b], A.add))
        do("v", ("own%d" % h, t), ["mrow:%d" % h, "drop"], ["arow:%d" % h],
           scan(T.arow[:, back(a, b)], T.drop[:, back(a, b)], T.mrow[:, back(a, b)], 0.0, A.add, A.max))
        do("v", ("flag%d" % h, t), ["arow:%d" % h, p0], ["fl%d:%d" % (KB, h)], tt(flags(KB, a, b), T[p0][:, 0:b - a], T.arow[:, a:b], A.is_ge))
        d = T.fl[:, slice(4 * b - 4, 4 * a - 1 if a else None, -4)]
        do("v", ("sum%d" % h, t), ["fl%d:%d" % (KB, h), "gate"], ["eqs:%d" % h], scan(T.eqs[:, back(a, b)], T.gate[:, back(a, b)], d, 0.0, A.mult, A.add))

    def places(t):
        own, land = "own%d" % t, "land%d" % t
        top = FIRST if t == 0 else KB

        def compare(k, what):
            cut = [(n, a, b) for n, q, a, b in pieces(what + str(k), t)] or [((what + str(k), t), 0, 16 * k)]
            for n, a, b in cut:
                hs = [h for h in PART if a < PART[h][1] and PART[h][0] < b]
                yield n, a, b, hs, ["srow:%d" % h for h in hs] + ["arow:%d" % h for h in PART if PART[h][0] <= 16 * k < PART[h][1]]

        turn = [int(n[0][1:]) for n in seq["s"] if n[1] == t and n[0][0] == "s" and n[0][1:].isdigit()]
        for at, k in enumerate(turn):
            z, rel = C * (at % RELS), "rel%d:" % (at % RELS)
            for n, a, b, hs, keys in compare(k, "r"):
                do("s", n, keys, [rel + str(h) for h in hs], act(T.rel[:, z + a:z + b], T.srow[:, a:b], F.Relu, bias=T.arow[:, 16 * k:16 * k + 1], scale=-1.0))
            do("s", ("s%d" % k, t), parts(rel[:-1]), parts("fl%d" % k) + ["cnt%d" % k],
               act(flags(k, 0, 16 * k), T.rel[:, z:z + 16 * k], F.Sign, scale=-1.0, accum_out=T.cnt[:, k:k + 1]))
        for k in range(1, KB):
            if k not in by_s:
                for n, a, b, hs, keys in compare(k, "g"):
                    do("v", n, keys, ["fl%d:%d" % (k, h) for h in hs], ts(flags(k, a, b), T.srow[:, a:b], T.arow[:, 16 * k:16 * k + 1], A.is_ge))
                z = 224 * k + 224
                do("v", ("u%d" % k, t), parts("fl%d" % k), ["zs:%d" % k],
                   scan(T.zs[:, z - 8 * k:z], flags(k, 0, 8 * k), flags(k, 8 * k, 16 * k), -float(HALF), A.add, A.add))
        do("v", ("tie", t), parts("eqs") + ["k1"], ["tie"], tt(T.tie[:], T.eqs[:, 0:C:16], T.k1[:], A.add))
        for i in range(NQ):
            a, b = AT[i], AT[i + 1]
            do("v", ("q%d" % i, t), rows(i), ["qf%d" % i], quant(T.qf[:, a:b], T.sf[:, a:b], T.fl[:, 4 * a:4 * b]))
        for what, bank, width in (("e", "pp3", C), ("h", "pp1", C), ("l", "pp2", 16 * HIGH)):
            tiles = [int(n[0][1:]) for n in seq["t"] if n[1] == t and n[0][0] == what and n[0][1:].isdigit()]
            for i in tiles if what != "e" or t == 0 else []:
                a, n = AT[i], min(width, WIDE[i])
                matmul((what + str(i), t), T[bank][:, 0:n], bank, T.qg[:], T.sg[:], ["qg"], T.qf[:, a:a + n], T.sf[:, a:a + n], ["qf%d" % i],
                       i == tiles[0], i == tiles[-1])
        for bank, a, b in (("pp3", top, KB), ("pp1", HIGH, top), ("pp2", 0, HIGH)):
            c = a
            while c < b:
                d = c + 1
                while d < b and (d in by_s) == (c in by_s or c == 0):
                    d += 1
                if c in by_s or c == 0:
                    keys, src = ["cnt%d" % k for k in range(c, d)], T.cnt[:, c:d]
                else:
                    keys, src = ["zs:%d" % k for k in range(c, d)], T.zs[:, 224 * c + 223:224 * d:224]
                do("v", ("base%d" % c, t), keys + ["tie", "ctlb"], ["ctlb:%d" % k for k in range(c, d)],
                   tt(T.ctlb[:, 16 * c + 15:16 * d:16], src, T.tie[:, c:d], A.add))
                c = d
            if a < b:
                do("v", ("set%d" % a, t), [bank] + ["ctlb:%d" % k for k in range(a, b)], ["hcol:%d" % a],
                   scan(T.hcol[:, 16 * a:16 * b], T[bank][:, 16 * a:16 * b], T.ctlb[:, 16 * a:16 * b], -float(DEEP), A.max, A.add))
                do("v", ("off%d" % a, t), ["hcol:%d" % a], span(own, 16 * a, 16 * b), ts(T[own][:, a:b], T.hcol[:, 16 * a + 15:16 * b:16], float(DEEP), A.add))
                there = span(land, 16 * HIGH, C) if a else span(land, 0, 16 * HIGH)
                send(t, [(there, land, own, lambda n, a=a, b=b: T[n][:, a:b], span(own, 16 * a, 16 * b))], "rx%s%d" % ("h" if a else "l", t))
        for n, q, a, b in pieces("put", t):
            do("v", n, span(own, a, b) + ["fh"], ["orow"], cp(T.orow[:, 0:C].indirect(T[own][:, a // 16:b // 16]), T.fh[:, a:b]))

    def wrap(n, row, keys, a, b, ctl="ctl"):
        do("v", n, keys + [ctl], span("hrow", a, b), scan(T.hrow[:, a:b], row[:, a:b], T[ctl][:, a:b], -1024.0, A.max, A.add))

    def offsets(n, name, at, key, a, b, add, by=None):
        out, h = T[name][:, at + a // 16:at + b // 16], T.hrow[:, a + 15:b:16]
        do("v", n, span("hrow", a, b), span(key, a, b), ts(out, h, add, A.add) if by is None else ts(out, h, add, A.add, by, A.mult))

    def cycles(t):
        def jrow(k):
            return "orow" if k < 0 else "jp" if k == 0 else "j%d" % (k % 2)

        def arow(k):
            return "jp" if k == 0 else "a%d" % (k % 2)

        for k in range(-1, 9):
            lists, at, key = (T["land%d" % t], 0, "land%d" % t) if k < 0 else (T.off, KB * k, "off%d" % k)
            j, jn = jrow(k), jrow(k + 1)
            win, out, bk, d = arow(k), arow(k + 1), "b%d" % (k % 2), 2.0 ** k / 1024
            if k < 8:
                for n, q, a, b in pieces("G", t, k):
                    do(q, n, ([j] if k < 0 else span(j)) + span(key, a, b), span(jn, a, b),
                       move(q, T[jn][:, a:b], T[j][:, 0:C].indirect(lists[:, at + a // 16:at + b // 16])))
                for n, q, a, b in pieces("W", t, k):
                    wrap(n, T[jn], span(jn, a, b), a, b)
                for n, q, a, b in pieces("O", t, k):
                    offsets(n, "off", KB * (k + 1), "off%d" % (k + 1), a, b, float(LIFT + HALF))
            if k >= 0:
                for n, q, a, b in pieces("S", t, k):
                    do(q, n, span(win, a, b), span(bk, a, b), act(T[bk][:, a:b], T[win][:, a:b], F.Identity, bias=-d) if q == "s"
                       else ts(T[bk][:, a:b], T[win][:, a:b], -d, A.add))
                for n, q, a, b in pieces("K", t, k):
                    do("v", n, span(win) + span(key, a, b) + span(bk, a, b), span(out, a, b),
                       tt(T[out][:, a:b], T[win][:, 0:C].indirect(lists[:, at + a // 16:at + b // 16]), T[bk][:, a:b], A.min))
        key = arow(9)
        win = T[key]
        for n, q, a, b in pieces("U", t):
            do("v", n, span(key, a, b) + ["thr"], span("wrow", a, b), scan(T.wrow[:, a:b], win[:, a:b], T.thr[:, a:b], -1024.0, A.max, A.max))
        for n, q, a, b in pieces("H", t):
            do("v", n, span(key, a, b) + ["ctl"], span("hkey", a, b), scan(T.hkey[:, a:b], win[:, a:b], T.ctl[:, a:b], -1024.0, A.max, A.add))
        for n, q, a, b in sorted(pieces("C", t), key=lambda p: p[2]):
            do("v", n, span("wrow", a, b) + span("crow", a - 32, a) + ["thr"], span("crow", a, b),
               scan(T.crow[:, a:b], T.wrow[:, a:b], T.thr[:, a:b], T.crow[:, a - 1:a] if a else -HALF / 1024, A.add, A.subtract))
        own_key, up = T.hkey[:, 15:C:16], float(MAGIC + LIFT + HALF)
        do("v", ("offm", t), span("hkey"), ["offm"], ts(T.offm[:], own_key, up, A.add, float(MAGIC), A.subtract))
        do("v", ("mw", t), span("hkey") + ["col3"], ["mw"], ts(T.mw[:], own_key, up, A.add, T.col[:, 3:4], A.subtract))
        do("v", ("ctlm", t), span("hkey") + ["mw"], ["ctlp"], tt(T.ctlp[:, 15:C:16], T.mw[:], own_key, A.subtract))
        for n, q, a, b in pieces("P", t):
            do(q, n, span("crow") + ["offm"], span("prow", a, b), move(q, T.prow[:, a:b], T.crow[:, 0:C].indirect(T.offm[:, a // 16:b // 16])))
        for n, q, a, b in pieces("W", t):
            wrap(n, T.prow, span("prow", a, b), a, b, "ctlp")
        for n, q, a, b in pieces("O", t):
            offsets(n, "offp", 0, "offp", a, b, (LIFT + HALF) / 1024, 1024.0)
        do("v", ("pute", t), span("offp") + ["fh"], ["erow"], cp(T.erow[:, 0:C].indirect(T.offp[:, 0:KB]), T.fh[:]))
        for n, q, a, b in pieces("W", t, None, "e"):
            wrap(n, T.erow, ["erow"], a, b)
        for n, q, a, b in pieces("O", t, None, "e"):
            offsets(n, "offe", 0, "offe", a, b, float(LIFT + HALF))

    def lay_out(t):
        zt, qz, sz, xn = T["zt%d" % t], T["qz%d" % t], T["sz%d" % t], T["x%d" % (t + 1)]
        bt, qb, sb, qc, sc = ["%s%d" % (n, t) for n in ("bt", "qb", "sb", "qc", "sc")]

        def lay(name, tile, key, a, b, i):
            q = who[name, t]
            src = T.xp[:, C * i:C * i + C].indirect(T.offe[:, a // 16:b // 16])
            do(q, (name, t), ["xp%d" % i] + span("offe", a, b), [key], move(q, tile[:, 4 * a + i:4 * b:4], src))

        def through(h, a, b, bank, start):
            key = "qz%d:%d" % (t, h)
            do("v", ("qz%d" % h, t), ["z%d:%d:%d" % (t, h, i) for i in range(4)], [key], quant(qz[:, a:b], sz[:, a:b], zt[:, 4 * a:4 * b]))
            for i in range(4):
                matmul(("w%d%d" % (h, i), t), T[bank % i][:, 0:b - a], bank % i, T.qw[:, S * i:S * i + S], T.sw[:, S * i:S * i + S], ["w"],
                       qz[:, a:b], sz[:, a:b], [key], start, True)

        def unpack(name, i, stop):
            matmul((name, t), T["pr%d" % i][:, 0:S], "pr%d" % i, T.qe[:, S * i:S * i + S], T.se[:, S * i:S * i + S], ["qe%d" % i],
                   T[qc][:], T[sc][:], [qc, sc], True, stop)

        for i in range(4):
            do("s", ("p%d" % i, t), [k for h in PART for k in state_keys(t, h)], ["xp%d" % i], act(T.xp[:, C * i:C * i + C], T["x%d" % t][:, i:4 * C:4]))
        for i in range(4):
            lay("b%d" % i, T[bt], bt + ":%d" % i, 0, S, i)
        do("v", ("qb", t), [bt + ":%d" % i for i in range(4)], [qb, sb], quant(T[qb][:], T[sb][:], T[bt][:]))
        send(t, [([qc], qc, qb, lambda n: T[n][:].bitcast(dt.uint8), [qb]), ([sc], sc, sb, lambda n: T[n][:], [sb])], "rxb%d" % t)
        for h in (1, 3):
            a, b = PART[h]
            bank = "pr%d" if h == 1 else "pp%d"
            for i in range(4):
                lay("z%d%d" % (h, i), zt, "z%d:%d:%d" % (t, h, i), a, b, i)
            through(h, a, b, bank, True)
            for i in range(4):
                name, cols, r = "%d%d" % (h, i), slice(4 * a + i, 4 * b, 4), T["r%d" % i][:, a:b]
                q = who["m" + name, t]
                do(q, ("m" + name, t), ["z%d:%d:%d" % (t, h, i)], ["z64:" + name], times(q, T.z64[:, cols], zt[:, cols], 64.0))
                do("v", ("a" + name, t), [bank % i, "z64:" + name], ["r" + name], tt(r, T[bank % i][:, 0:b - a], T.z64[:, cols], A.add))
                q = who["x" + name, t]
                do(q, ("x" + name, t), ["r" + name], ["x%d:%d:%d" % (t + 1, h, i)], times(q, xn[:, cols], r, 0.015625))
        for i in range(4):
            q = who["c%d" % i, t]
            unpack("d%d" % i, i, True)
            do(q, ("c%d" % i, t), ["pr%d" % i], ["z%d:2:%d" % (t, i)], times(q, zt[:, i:4 * S:4], T["pr%d" % i][:, 0:S], 0.015625))
            unpack("f%d" % i, i, False)
        through(2, 0, S, "pr%d", False)
        for i in range(4):
            q = who["y%d" % i, t]
            do(q, ("y%d" % i, t), ["pr%d" % i], ["x%d:2:%d" % (t + 1, i)], times(q, xn[:, i:4 * S:4], T["pr%d" % i][:, 0:S], 0.015625))

    def finish(t, h):
        a, b = (S, C) if h == 1 else (0, S)
        q, s, p = T["qx%d" % t], T["sx%d" % t], BANKS[h][0]
        keys = ["qx%d:%d" % (t, i) for i in ((1, 3) if h == 1 else (2,))]
        matmul(("fin%d" % h, t), T[p][:, 0:b - a], p, T.qv[:], T.sv[:], ["qv"], q[:, a:b], s[:, a:b], keys)
        store("y", None, keys, T.oc[:, 4 * a:4 * b], q[:, a:b].bitcast(dt.uint8))
        for k in range(4):
            store("y", None, keys, T.osc[4 * k:4 * k + 4, a:b], s[32 * k:32 * k + 4, a:b])
        do("s", ("ysb%d" % h, t - 1), [p], ["ysb:%d" % h], act(T.ysb[:, a:b], T[p][:, 0:b - a]))
        store("s", ("sty%d" % h, t - 1), ["ysb:%d" % h], T.y[:, a:b], T.ysb[:, a:b])

    for t in range(R):
        for h in PART:
            score(t, h)
        places(t)
        cycles(t)
        if t == R - 1:
            do("s", ("elf", t), ["erow"], ["elf"], act(T.elf[:], T.erow[:], F.Identity, bias=float(HALF)))
            store("y", None, ["elf"], T.el[:], T.elf[0:128:16, :])
        lay_out(t)
    for h in PART:
        quant_state(R, h)
    finish(R, 1)
    finish(R, 2)

    queue = {"v": g.vector, "s": g.scalar, "t": g.tensor, "g": g, "y": g.sync}
    place = {n: i for q in seq for i, n in enumerate(seq[q])}
    todo = {q: sorted((i for i, c in enumerate(calls) if c[0] == q), key=lambda i: (place[calls[i][1]] if calls[i][1] else -1, i)) for q in queue}
    for h in HOOK:
        h(calls, fixed, todo)
    count = dict(landed)
    know = {q: {} for q in queue}
    token = {}
    while any(todo.values()):
        ready = [q for q in queue if todo[q] and all(i in token for i in calls[todo[q][0]][2] | calls[todo[q][0]][3])]
        q = ready[0]
        i = todo[q].pop(0)
        _, _, need, _, issue, sem, inc = calls[i]
        for s, val, seen in sorted((token[j] for j in need), key=lambda tok: -tok[1]):
            if know[q].get(s, 0) < val:
                queue[q].wait_ge(T.sem[s], val)
                for s2, n in list(seen.items()) + [(s, val)]:
                    know[q][s2] = max(know[q].get(s2, 0), n)
        issue(queue[q])
        count[sem] = count.get(sem, 0) + inc
        token[i] = fixed[i] + ({},) if i in fixed else (sem, count[sem], dict(know[q]))
    for sem in sorted(count):
        g.wait_ge(T.sem[sem], count[sem])
